import numpy as np
import ml_dtypes


def mxq(x, axis, fmt="e4m3"):
    dtype, down = {"e4m3": (ml_dtypes.float8_e4m3fn, 7), "e5m2": (ml_dtypes.float8_e5m2, 14)}[fmt]
    v = np.moveaxis(np.asarray(x, np.float32).astype(ml_dtypes.bfloat16).astype(np.float64), axis, -1)
    blocks = v.reshape(v.shape[:-1] + (-1, 32))
    amax = np.abs(blocks).max(-1, keepdims=True)
    byte = np.maximum(np.where(amax > 0, np.frexp(amax)[1] - 1 + 127, 0) - down, 1)
    scale = np.exp2(byte - 127.0)
    codes = (blocks / scale).astype(np.float32).astype(dtype).astype(np.float64)
    return np.moveaxis((codes * scale).reshape(v.shape), -1, axis)


WIDE = False


def mx_kscale(k):
    if not WIDE:
        return np.ones(k)
    levels = np.array([10, -10, 5, -5, 0])
    if k % 512:
        return np.exp2(np.random.permutation(np.resize(levels, k // 32))).repeat(32)
    a = np.empty((k // 512, 16))
    for p in range(k // 512):
        a[p, :8] = np.random.permutation(np.resize(levels, 8))
        for g in range(8):
            far = levels[np.abs(levels - a[p, g]) >= 10]
            a[p, g + 8] = far[np.random.randint(len(far))]
    return np.exp2(a.ravel()).repeat(32)


def f64(x):
    return np.asarray(x).astype(np.float64)


def striped(idx):
    return np.tile(idx.reshape(-1, 16).T, (8, 1)).astype(np.uint16)


def unstriped(offs):
    return offs[:16].T.reshape(-1).astype(np.int64)


E2M1 = np.array([0.0, 0.5, 1.0, 1.5, 2.0, 3.0, 4.0, 6.0, -0.0, -0.5, -1.0, -1.5, -2.0, -3.0, -4.0, -6.0])


def pack_weight(w, fmt):
    k, n = w.shape
    w = f64(np.asarray(w, np.float32).astype(ml_dtypes.bfloat16)).reshape(k // 32, 32, n)
    amax = np.abs(w).max(1)
    if fmt == "e4m3":
        byte = np.frexp(amax)[1] - 1 + 127 - 7
    else:
        mant, ex = np.frexp(amax / 6.0)
        byte = np.where(mant > 0.5, ex, ex - 1) + 127
    byte = np.clip(np.where(amax > 0, byte, 1), 1, 254)
    scaled = (w * np.exp2(127.0 - byte)[:, None, :]).reshape(k, n).astype(np.float32)
    by_word = np.ascontiguousarray(scaled.reshape(k // 512, 128, 4, n).transpose(0, 1, 3, 2))
    if fmt == "e4m3":
        words = by_word.astype(ml_dtypes.float8_e4m3fn).view(np.uint8)
    else:
        c = by_word.astype(ml_dtypes.float4_e2m1fn).view(np.uint8) & 0xF
        words = (c[..., 0::2] | (c[..., 1::2] << 4)).reshape(k // 512, 128, 2 * n)
    return np.ascontiguousarray(words), np.ascontiguousarray(byte.astype(np.uint8).reshape(k // 512, 16, n))


def unpack_weight(words, scales, fmt):
    g, _, n = scales.shape
    words = np.ascontiguousarray(words).reshape(g, 128, n, -1)
    if fmt == "e4m3":
        vals = words.view(ml_dtypes.float8_e4m3fn).astype(np.float64)
    else:
        nib = np.empty((g, 128, n, 4), np.uint8)
        nib[..., 0::2] = words & 0xF
        nib[..., 1::2] = words >> 4
        vals = E2M1[nib]
    vals = vals * np.repeat(np.exp2(scales.astype(np.float64) - 127.0), 8, axis=1)[..., None]
    return vals.transpose(0, 1, 3, 2).reshape(g * 512, n)


def gelu(v):
    return 0.5 * v * (1.0 + np.tanh(np.sqrt(2.0 / np.pi) * (v + 0.044715 * v**3)))


K, T, S, H, N, T2 = 1024, 4096, 1024, 512, 512, 2048

def setup_inputs():
    n = np.random.standard_normal
    s = mx_kscale(K)[:, None]
    u = mx_kscale(H)[:, None]
    tab_words, tab_scales = pack_weight(n((K, T)) * s, "e4m3")
    wg_words, wg_scales = pack_weight(n((K, H)) / np.sqrt(K) / s, "e2m1")
    wr_words, wr_scales = pack_weight(n((K, N)) / np.sqrt(K) / s, "e4m3")
    return {
        "tab_words": tab_words, "tab_scales": tab_scales,
        "offs": striped(np.random.permutation(T)[:S]),
        "offs2": striped(np.random.permutation(T2)[:S]),
        "wg_words": wg_words, "wg_scales": wg_scales,
        "wr_words": wr_words, "wr_scales": wr_scales,
        "wc": (n((K, H)) / np.sqrt(K) / s).astype(np.float32),
        "wp": (n((K, H)) / np.sqrt(K) / s).astype(np.float32),
        "gain": (np.exp(0.3 * n(H)) * u[:, 0]).astype(np.float32),
        "wo": (n((H, N)) / np.sqrt(H) / u).astype(np.float32),
        "wgo": np.exp(0.3 * n((128, S))).astype(np.float32),
    }

def reference(tab_words, tab_scales, offs, offs2, wg_words, wg_scales, wr_words, wr_scales, wc, wp, gain, wo, wgo):
    v = unpack_weight(tab_words, tab_scales, "e4m3")[:, unstriped(offs)]
    wg = unpack_weight(wg_words, wg_scales, "e2m1")
    wr = unpack_weight(wr_words, wr_scales, "e4m3")
    g = 1 / (1 + np.exp(-(wg.T @ v)))
    c = np.tanh(mxq(f64(wc), 0, "e4m3").T @ v)
    p = mxq(f64(wp), 0, "e4m3").T @ v
    h = f64(gain)[:, None] * (g * (c - p))
    y = mxq(f64(wo), 0, "e4m3").T @ mxq(h, 0, "e4m3") + wr.T @ v
    out = np.zeros((N, T2))
    out[:, unstriped(offs2)] = np.tile(f64(wgo), (N // 128, 1)) * y
    return out

@@ -1,0 +1,277 @@
+from contextlib import ExitStack
+
+import concourse.mybir as mybir
+
+K, T, S, H, N, T2 = 1024, 4096, 1024, 512, 512, 2048
+FLOPS = 2 * S * (3 * K * H + K * N + H * N)
+
+F32 = mybir.dt.float32
+BF16 = mybir.dt.bfloat16
+I32 = mybir.dt.int32
+U32 = mybir.dt.uint32
+U16 = mybir.dt.uint16
+U8 = mybir.dt.uint8
+FP8X4 = mybir.dt.float8_e4m3fn_x4
+FP4X4 = mybir.dt.float4_e2m1fn_x4
+ACT = mybir.ActivationFunctionType
+ALU = mybir.AluOpType
+
+P = 128
+PACK = 4
+K_PASS = P * PACK
+PASSES = K // K_PASS
+HALF = 512
+HALVES = S // HALF
+CHUNKS = N // P
+COLS = HALF // 16
+
+
+def tile_list_gated_node_update_kernel(
+    tc, tab_words, tab_scales, offs, offs2, wg_words, wg_scales, wr_words, wr_scales, wc, wp, gain, wo, wgo, out
+):
+    nc = tc.nc
+    with ExitStack() as ctx:
+        lists = ctx.enter_context(tc.tile_pool(name="lists", bufs=1))
+        keep = ctx.enter_context(tc.tile_pool(name="keep", bufs=1))
+        ring = ctx.enter_context(tc.tile_pool(name="ring", bufs=2))
+        psum = ctx.enter_context(tc.psum_pool(name="psum", bufs=1))
+
+        def load_scale_rows(queue, plane, rows):
+            words = rows.bitcast(I32)
+            for r in range(4):
+                queue.dma_start(out=plane[r:P:32, :, :], in_=words[:, r:16:4, :].rearrange("a q w -> q a w"))
+
+        tab_plane = keep.tile([P, PASSES, T // 4], I32, name="tab_plane", tag="slot_a", align_bytes=64)
+        wg_plane_raw = keep.tile([P, PASSES, H // 4], I32, name="wg_plane_raw", tag="slot_b", align_bytes=64)
+        wr_plane = keep.tile([P, PASSES, N // 4], I32, name="wr_plane", align_bytes=64)
+        for plane in (tab_plane, wg_plane_raw, wr_plane):
+            nc.vector.memset(plane[:], 0)
+        load_scale_rows(nc.gpsimd, tab_plane, tab_scales)
+        load_scale_rows(nc.gpsimd, wg_plane_raw, wg_scales)
+
+        def load_rows(w, a, name, pieces=1):
+            raw = keep.tile([P, PACK, w.shape[1]], F32, name=name, tag=name)
+            rows = w[a * K_PASS : (a + 1) * K_PASS, :].rearrange("(p j) c -> p j c", j=PACK)
+            width = w.shape[1] // pieces
+            for u in range(pieces):
+                nc.sync.dma_start(out=raw[:, :, u * width : (u + 1) * width], in_=rows[:, :, u * width : (u + 1) * width])
+            return raw
+
+        wc_raw = [load_rows(wc, a, f"wc_raw{a}") for a in range(PASSES)]
+        idx = lists.tile([P, S // 16], U16, name="idx")
+        nc.sync.dma_start(idx[:], offs)
+        table = []
+        wg_raw = keep.tile([P, PASSES, 2 * H // 4], I32, name="wg_raw")
+        gain_sb = keep.tile([P, PACK], F32, name="gain_sb")
+        nc.sync.dma_start(out=wg_raw[:], in_=wg_words.bitcast(I32).rearrange("a p w -> p a w"))
+        for a in range(PASSES):
+            words = keep.tile([P, T], I32, name=f"table{a}", tag=f"table{a}", align_bytes=64)
+            nc.sync.dma_start(out=words[:], in_=tab_words[a].rearrange("p t i -> p (t i)").bitcast(I32))
+            table.append(words)
+        nc.sync.dma_start(out=gain_sb[:], in_=gain.rearrange("(p t) -> p t", t=PACK))
+        wp_raw = [load_rows(wp, 0, "wp_raw0"), load_rows(wp, 1, "wp_raw1", pieces=2)]
+        wr_codes = keep.tile([P, PASSES, N], I32, name="wr_codes", align_bytes=64)
+        nc.sync.dma_start(out=wr_codes[:], in_=wr_words.rearrange("a p e i -> p a (e i)").bitcast(I32))
+        load_scale_rows(nc.sync, wr_plane, wr_scales)
+        wo_raw = load_rows(wo, 0, "wo_raw")
+        wgo_sb = keep.tile([P, S], F32, name="wgo_sb")
+        nc.sync.dma_start(out=wgo_sb[:], in_=wgo)
+        idx2 = lists.tile([P, S // 16], U16, name="idx2")
+        nc.sync.dma_start(idx2[:], offs2)
+
+        windows = []
+        for c in range(2):
+            window = keep.tile([P, T2], F32, name=f"window{c}")
+            nc.vector.memset(window[:, : T2 // 2 - 1], 0.0)
+            nc.vector.memset(window[:, T2 // 2 - 1 :], 0.0)
+            windows.append(window)
+
+        def cast_permuted(copy, raw, grouped, pieces=1):
+            dst = grouped.rearrange("p (t m j) -> p m j t", t=PACK, j=PACK)
+            src = raw[:].rearrange("p j (m t) -> p m j t", t=PACK)
+            width = P // pieces
+            for u in range(pieces):
+                copy(out=dst[:, u * width : (u + 1) * width], in_=src[:, u * width : (u + 1) * width])
+            return grouped
+
+        def quantize(grouped, name):
+            width = grouped.shape[1] // PACK
+            codes = keep.tile([P, width], U32, name=name + "_codes", align_bytes=64)
+            plane = keep.tile([P, width], U8, name=name + "_plane", align_bytes=64)
+            nc.vector.quantize_mx(out=codes[:].bitcast(FP8X4), scales=plane[:], in_=grouped)
+            return codes, plane
+
+        wc_q = []
+        for a in range(PASSES):
+            wc_bf = ring.tile([P, PACK * H], BF16, name=f"wc_bf{a}", tag="wc_bf", align_bytes=64)
+            wc_q.append(quantize(cast_permuted(nc.scalar.copy, wc_raw[a], wc_bf[:]), f"wc{a}"))
+            window = keep.tile([P, T2], F32, name=f"window{2 + a}", tag=f"wc_raw{a}")
+            nc.gpsimd.memset(window[:], 0.0)
+            windows.append(window)
+
+        wg_codes = keep.tile([P, PASSES, 2 * H], U8, name="wg_codes", align_bytes=64)
+        wg_plane = keep.tile([P, PASSES, H], U8, name="wg_plane", align_bytes=64)
+        for a in range(PASSES):
+            nc.vector.tensor_copy(
+                out=wg_plane[:, a, :].rearrange("p (t m) -> p m t", t=PACK),
+                in_=wg_plane_raw[:, a, :].bitcast(U8).rearrange("p (m t) -> p m t", t=PACK),
+            )
+            nc.vector.tensor_copy(
+                out=wg_codes[:, a, :].rearrange("p (t m b) -> p m t b", t=PACK, b=2),
+                in_=wg_raw[:, a, :].bitcast(U8).rearrange("p (m t b) -> p m t b", t=PACK, b=2),
+            )
+
+        v_plane = []
+        v_codes = {}
+        for a in range(PASSES):
+            plane = keep.tile([P, S], U8, name=f"v_plane{a}", align_bytes=64)
+            nc.vector.tensor_copy(out=plane[:], in_=tab_plane[:, a, :].bitcast(U8).indirect(idx[:]))
+            v_plane.append(plane)
+        for a in range(PASSES):
+            for s in range(HALVES):
+                slot = ("slot_a", "slot_b")[s] if a == 1 else f"v_codes{s}"
+                codes = keep.tile([P, HALF], U32, name=f"v_codes{a}_{s}", tag=slot, align_bytes=64)
+                nc.vector.tensor_copy(
+                    out=codes[:], in_=table[a][:].bitcast(U32).indirect(idx[:, s * COLS : (s + 1) * COLS])
+                )
+                v_codes[a, s] = codes
+
+        def times_table(acc, lhsT, lhsT_scale, a, s, start, stop):
+            nc.tensor.matmul_mx(
+                out=acc[:],
+                lhsT=lhsT,
+                lhsT_scale=lhsT_scale,
+                rhs=v_codes[a, s][:].bitcast(FP8X4),
+                rhs_scale=v_plane[a][:, s * HALF : (s + 1) * HALF],
+                start=start,
+                stop=stop,
+            )
+
+        def product(quantized, t, s, tag):
+            acc = psum.tile([P, HALF], F32, name=f"{tag}{s}_{t}", tag=tag, bufs=2 if tag == "y" else 3)
+            cols = slice(t * P, (t + 1) * P)
+            for a in range(PASSES):
+                codes, plane = quantized[a]
+                times_table(acc, codes[:, cols].bitcast(FP8X4), plane[:, cols], a, s, a == 0, a == PASSES - 1)
+            return acc
+
+        def gate_and_candidate(s, t):
+            acc = psum.tile([P, HALF], F32, name=f"g{s}_{t}", tag="act", bufs=3)
+            for a in range(PASSES):
+                times_table(
+                    acc,
+                    wg_codes[:, a, 2 * t * P : 2 * (t + 1) * P].bitcast(FP4X4),
+                    wg_plane[:, a, t * P : (t + 1) * P],
+                    a, s, a == 0, a == PASSES - 1,
+                )
+            g = ring.tile([P, HALF], F32, name=f"gate{s}_{t}", tag="gate", bufs=6)
+            nc.scalar.activation(out=g[:], in_=acc[:], func=ACT.Sigmoid)
+            acc = product(wc_q, t, s, "act")
+            if (s, t) == (0, 1):
+                c = keep.tile([P, HALF], F32, name=f"cand{s}_{t}", tag="slot_e", align_bytes=64)
+            else:
+                c = ring.tile([P, HALF], F32, name=f"cand{s}_{t}", tag="cand", bufs=6)
+            nc.scalar.activation(out=c[:], in_=acc[:], func=ACT.Tanh)
+            return g, c
+
+        gc = {}
+        for t in range(PACK):
+            gc[0, t] = gate_and_candidate(0, t)
+
+        wp_bf = keep.tile([P, PASSES, PACK * H], BF16, name="wp_bf", tag="table1", align_bytes=64)
+        wp_q = [
+            quantize(cast_permuted(nc.vector.tensor_copy, wp_raw[0], wp_bf[:, 0, :]), "wp0"),
+            quantize(cast_permuted(nc.vector.tensor_copy, wp_raw[1], wp_bf[:, 1, :], pieces=2), "wp1"),
+        ]
+
+        def gated_difference(s):
+            planes = ring.tile([P, PACK, HALF], BF16, name=f"h_planes{s}", tag="h_planes")
+            diffs = {}
+            for step in range(PACK + 1):
+                if step < PACK:
+                    t = step
+                    if (s, t) not in gc:
+                        gc[s, t] = gate_and_candidate(s, t)
+                    acc = product(wp_q, t, s, "y" if s == 0 and t < 2 else "present")
+                    diff = ring.tile([P, HALF], F32, name=f"diff{s}_{t}", tag="diff", bufs=3)
+                    nc.vector.tensor_tensor(out=diff[:], in0=gc[s, t][1][:], in1=acc[:], op=ALU.subtract)
+                    diffs[t] = diff
+                if step > 0:
+                    t = step - 1
+                    nc.vector.scalar_tensor_tensor(
+                        out=planes[:, t, :], in0=gc[s, t][0][:], scalar=gain_sb[:, t : t + 1], in1=diffs[t][:],
+                        op0=ALU.mult, op1=ALU.mult,
+                    )
+            return planes
+
+        def quantize_h(planes, s):
+            grouped = ring.tile([P, PACK * HALF], BF16, name=f"h_bf{s}", tag="h_bf", align_bytes=64)
+            codes = keep.tile([P, HALF], U32, name=f"h_codes{s}", align_bytes=64)
+            plane = keep.tile([P, HALF], U8, name=f"h_plane{s}", align_bytes=64)
+            dst = grouped[:].rearrange("p (c i t) -> p c t i", i=4, t=PACK)
+            src = planes[:].rearrange("p t (c i) -> p c t i", i=4)
+            for u in range(2):
+                nc.scalar.copy(out=dst[:, u * 64 : (u + 1) * 64], in_=src[:, u * 64 : (u + 1) * 64])
+                nc.vector.quantize_mx(
+                    out=codes[:, u * 256 : (u + 1) * 256].bitcast(FP8X4),
+                    scales=plane[:, u * 256 : (u + 1) * 256],
+                    in_=grouped[:, u * 1024 : (u + 1) * 1024],
+                )
+            return codes, plane
+
+        wo_codes = keep.tile([P, N], U32, name="wo_codes", align_bytes=64)
+        wo_plane = keep.tile([P, N], U8, name="wo_plane", align_bytes=64)
+
+        def quantize_wo(u):
+            wo_bf = keep.tile([P, PACK * N // 2], BF16, name=f"wo_bf{u}", tag="slot_e", align_bytes=64)
+            dst = wo_bf[:].rearrange("p (c i j) -> p c j i", i=4, j=PACK)
+            src = wo_raw[:].rearrange("p j (c i) -> p c j i", i=4)
+            nc.scalar.copy(out=dst, in_=src[:, u * 64 : (u + 1) * 64])
+            nc.vector.quantize_mx(
+                out=wo_codes[:, u * 256 : (u + 1) * 256].bitcast(FP8X4),
+                scales=wo_plane[:, u * 256 : (u + 1) * 256],
+                in_=wo_bf[:],
+            )
+
+        def new_state(h_q, s, c):
+            acc = psum.tile([P, HALF], F32, name=f"y{s}_{c}", tag="y", bufs=2)
+            cols = slice(c * P, (c + 1) * P)
+            for a in range(PASSES):
+                times_table(
+                    acc,
+                    wr_codes[:, a, cols].bitcast(FP8X4),
+                    wr_plane[:, a, c * 32 : (c + 1) * 32].bitcast(U8),
+                    a, s, a == 0, False,
+                )
+            nc.tensor.matmul_mx(
+                out=acc[:],
+                lhsT=wo_codes[:, cols].bitcast(FP8X4),
+                lhsT_scale=wo_plane[:, cols],
+                rhs=h_q[0][:].bitcast(FP8X4),
+                rhs_scale=h_q[1][:],
+                start=False,
+                stop=True,
+            )
+            y = ring.tile([P, HALF], F32, name=f"y_sb{s}_{c}", tag="y_sb", bufs=6)
+            nc.scalar.copy(out=y[:], in_=acc[:])
+            return y
+
+        def scatter(y, s, c):
+            nc.vector.tensor_tensor(
+                out=windows[c][:].indirect(idx2[:, s * COLS : (s + 1) * COLS]),
+                in0=y[:],
+                in1=wgo_sb[:, s * HALF : (s + 1) * HALF],
+                op=ALU.mult,
+            )
+
+        planes0 = gated_difference(0)
+        quantize_wo(0)
+        h0 = quantize_h(planes0, 0)
+        quantize_wo(1)
+        y0 = [new_state(h0, 0, c) for c in range(CHUNKS)]
+        h1 = quantize_h(gated_difference(1), 1)
+        for c in range(CHUNKS):
+            scatter(y0[c], 0, c)
+        for c in range(CHUNKS):
+            scatter(new_state(h1, 1, c), 1, c)
+            nc.sync.dma_start(out=out[c * P : (c + 1) * P, :], in_=windows[c][:])

@@ -48,6 +48,12 @@ def tile_list_gated_node_update_kernel(
             nc.vector.memset(plane[:], 0)
         load_scale_rows(nc.gpsimd, tab_plane, tab_scales)
         load_scale_rows(nc.gpsimd, wg_plane_raw, wg_scales)
+        gain_sb = keep.tile([P, PACK], F32, name="gain_sb")
+        gain_rows = gain.rearrange("(u t i) -> i u t", t=PACK, i=4)
+        with nc.allow_non_contiguous_dma(reason="512 gains, one element a descriptor"):
+            for i in range(4):
+                nc.gpsimd.dma_start(out=gain_sb[i:P:4, :], in_=gain_rows[i])
+        load_scale_rows(nc.gpsimd, wr_plane, wr_scales)
 
         def load_rows(w, a, name, pieces=1):
             raw = keep.tile([P, PACK, w.shape[1]], F32, name=name, tag=name)
@@ -62,18 +68,18 @@ def tile_list_gated_node_update_kernel(
         nc.sync.dma_start(idx[:], offs)
         table = []
         wg_raw = keep.tile([P, PASSES, 2 * H // 4], I32, name="wg_raw")
-        gain_sb = keep.tile([P, PACK], F32, name="gain_sb")
         nc.sync.dma_start(out=wg_raw[:], in_=wg_words.bitcast(I32).rearrange("a p w -> p a w"))
         for a in range(PASSES):
             words = keep.tile([P, T], I32, name=f"table{a}", tag=f"table{a}", align_bytes=64)
             nc.sync.dma_start(out=words[:], in_=tab_words[a].rearrange("p t i -> p (t i)").bitcast(I32))
             table.append(words)
-        nc.sync.dma_start(out=gain_sb[:], in_=gain.rearrange("(p t) -> p t", t=PACK))
         wp_raw = [load_rows(wp, 0, "wp_raw0"), load_rows(wp, 1, "wp_raw1", pieces=2)]
         wr_codes = keep.tile([P, PASSES, N], I32, name="wr_codes", align_bytes=64)
         nc.sync.dma_start(out=wr_codes[:], in_=wr_words.rearrange("a p e i -> p a (e i)").bitcast(I32))
-        load_scale_rows(nc.sync, wr_plane, wr_scales)
-        wo_raw = load_rows(wo, 0, "wo_raw")
+        wo_raw = keep.tile([P, PACK, N], F32, name="wo_raw")
+        wo_rows = wo.rearrange("(u t i) n -> i u t n", t=PACK, i=4)
+        for i in range(4):
+            nc.sync.dma_start(out=wo_raw[i:P:4, :, :], in_=wo_rows[i])
         wgo_sb = keep.tile([P, S], F32, name="wgo_sb")
         nc.sync.dma_start(out=wgo_sb[:], in_=wgo)
         idx2 = lists.tile([P, S // 16], U16, name="idx2")
@@ -87,16 +93,16 @@ def tile_list_gated_node_update_kernel(
             windows.append(window)
 
         def cast_permuted(copy, raw, grouped, pieces=1):
-            dst = grouped.rearrange("p (t m j) -> p m j t", t=PACK, j=PACK)
-            src = raw[:].rearrange("p j (m t) -> p m j t", t=PACK)
-            width = P // pieces
+            dst = grouped.rearrange("p (t u i j) -> p t u j i", t=PACK, i=4, j=PACK)
+            src = raw[:].rearrange("p j (u t i) -> p t u j i", t=PACK, i=4)
+            width = 32 // pieces
             for u in range(pieces):
-                copy(out=dst[:, u * width : (u + 1) * width], in_=src[:, u * width : (u + 1) * width])
+                copy(out=dst[:, :, u * width : (u + 1) * width], in_=src[:, :, u * width : (u + 1) * width])
             return grouped
 
-        def quantize(grouped, name):
+        def quantize(grouped, name, slot=None):
             width = grouped.shape[1] // PACK
-            codes = keep.tile([P, width], U32, name=name + "_codes", align_bytes=64)
+            codes = keep.tile([P, width], U32, name=name + "_codes", tag=slot or name + "_codes", align_bytes=64)
             plane = keep.tile([P, width], U8, name=name + "_plane", align_bytes=64)
             nc.vector.quantize_mx(out=codes[:].bitcast(FP8X4), scales=plane[:], in_=grouped)
             return codes, plane
@@ -105,21 +111,17 @@ def tile_list_gated_node_update_kernel(
         for a in range(PASSES):
             wc_bf = ring.tile([P, PACK * H], BF16, name=f"wc_bf{a}", tag="wc_bf", align_bytes=64)
             wc_q.append(quantize(cast_permuted(nc.scalar.copy, wc_raw[a], wc_bf[:]), f"wc{a}"))
-            window = keep.tile([P, T2], F32, name=f"window{2 + a}", tag=f"wc_raw{a}")
-            nc.gpsimd.memset(window[:], 0.0)
-            windows.append(window)
 
-        wg_codes = keep.tile([P, PASSES, 2 * H], U8, name="wg_codes", align_bytes=64)
-        wg_plane = keep.tile([P, PASSES, H], U8, name="wg_plane", align_bytes=64)
-        for a in range(PASSES):
-            nc.vector.tensor_copy(
-                out=wg_plane[:, a, :].rearrange("p (t m) -> p m t", t=PACK),
-                in_=wg_plane_raw[:, a, :].bitcast(U8).rearrange("p (m t) -> p m t", t=PACK),
-            )
-            nc.vector.tensor_copy(
-                out=wg_codes[:, a, :].rearrange("p (t m b) -> p m t b", t=PACK, b=2),
-                in_=wg_raw[:, a, :].bitcast(U8).rearrange("p (m t b) -> p m t b", t=PACK, b=2),
-            )
+        wg_codes = keep.tile([P, PASSES, 2 * H // 4], I32, name="wg_codes", align_bytes=64)
+        wg_plane = keep.tile([P, PASSES, H // 4], I32, name="wg_plane", align_bytes=64)
+        nc.vector.tensor_copy(
+            out=wg_codes[:].rearrange("p a (t u w) -> p a t u w", t=PACK, w=2),
+            in_=wg_raw[:].rearrange("p a (u t w) -> p a t u w", t=PACK, w=2),
+        )
+        nc.vector.tensor_copy(
+            out=wg_plane[:].rearrange("p a (t u) -> p a t u", t=PACK),
+            in_=wg_plane_raw[:].rearrange("p a (u t) -> p a t u", t=PACK),
+        )
 
         v_plane = []
         v_codes = {}
@@ -127,21 +129,20 @@ def tile_list_gated_node_update_kernel(
             plane = keep.tile([P, S], U8, name=f"v_plane{a}", align_bytes=64)
             nc.vector.tensor_copy(out=plane[:], in_=tab_plane[:, a, :].bitcast(U8).indirect(idx[:]))
             v_plane.append(plane)
+        v_words = keep.tile([P, PASSES, S], U32, name="v_words", tag="slot_a", align_bytes=64)
         for a in range(PASSES):
             for s in range(HALVES):
-                slot = ("slot_a", "slot_b")[s] if a == 1 else f"v_codes{s}"
-                codes = keep.tile([P, HALF], U32, name=f"v_codes{a}_{s}", tag=slot, align_bytes=64)
+                v_codes[a, s] = v_words[:, a, s * HALF : (s + 1) * HALF]
                 nc.vector.tensor_copy(
-                    out=codes[:], in_=table[a][:].bitcast(U32).indirect(idx[:, s * COLS : (s + 1) * COLS])
+                    out=v_codes[a, s], in_=table[a][:].bitcast(U32).indirect(idx[:, s * COLS : (s + 1) * COLS])
                 )
-                v_codes[a, s] = codes
 
         def times_table(acc, lhsT, lhsT_scale, a, s, start, stop):
             nc.tensor.matmul_mx(
                 out=acc[:],
                 lhsT=lhsT,
                 lhsT_scale=lhsT_scale,
-                rhs=v_codes[a, s][:].bitcast(FP8X4),
+                rhs=v_codes[a, s].bitcast(FP8X4),
                 rhs_scale=v_plane[a][:, s * HALF : (s + 1) * HALF],
                 start=start,
                 stop=stop,
@@ -155,51 +156,51 @@ def tile_list_gated_node_update_kernel(
                 times_table(acc, codes[:, cols].bitcast(FP8X4), plane[:, cols], a, s, a == 0, a == PASSES - 1)
             return acc
 
-        def gate_and_candidate(s, t):
+        def gate(s, t):
             acc = psum.tile([P, HALF], F32, name=f"g{s}_{t}", tag="act", bufs=3)
             for a in range(PASSES):
                 times_table(
                     acc,
-                    wg_codes[:, a, 2 * t * P : 2 * (t + 1) * P].bitcast(FP4X4),
-                    wg_plane[:, a, t * P : (t + 1) * P],
+                    wg_codes[:, a, t * 64 : (t + 1) * 64].bitcast(U8).bitcast(FP4X4),
+                    wg_plane[:, a, t * 32 : (t + 1) * 32].bitcast(U8),
                     a, s, a == 0, a == PASSES - 1,
                 )
             g = ring.tile([P, HALF], F32, name=f"gate{s}_{t}", tag="gate", bufs=6)
             nc.scalar.activation(out=g[:], in_=acc[:], func=ACT.Sigmoid)
+            return g
+
+        def candidate(s, t):
             acc = product(wc_q, t, s, "act")
-            if (s, t) == (0, 1):
-                c = keep.tile([P, HALF], F32, name=f"cand{s}_{t}", tag="slot_e", align_bytes=64)
+            if s == 0 and t < 2:
+                c = keep.tile([P, HALF], F32, name=f"cand{s}_{t}", tag=("slot_f", "slot_e")[t], align_bytes=64)
             else:
                 c = ring.tile([P, HALF], F32, name=f"cand{s}_{t}", tag="cand", bufs=6)
             nc.scalar.activation(out=c[:], in_=acc[:], func=ACT.Tanh)
-            return g, c
-
-        gc = {}
-        for t in range(PACK):
-            gc[0, t] = gate_and_candidate(0, t)
+            return c
 
         wp_bf = keep.tile([P, PASSES, PACK * H], BF16, name="wp_bf", tag="table1", align_bytes=64)
         wp_q = [
-            quantize(cast_permuted(nc.vector.tensor_copy, wp_raw[0], wp_bf[:, 0, :]), "wp0"),
+            quantize(cast_permuted(nc.vector.tensor_copy, wp_raw[0], wp_bf[:, 0, :]), "wp0", slot="slot_b"),
             quantize(cast_permuted(nc.vector.tensor_copy, wp_raw[1], wp_bf[:, 1, :], pieces=2), "wp1"),
         ]
 
         def gated_difference(s):
             planes = ring.tile([P, PACK, HALF], BF16, name=f"h_planes{s}", tag="h_planes")
+            gates = {}
             diffs = {}
             for step in range(PACK + 1):
                 if step < PACK:
                     t = step
-                    if (s, t) not in gc:
-                        gc[s, t] = gate_and_candidate(s, t)
+                    gates[t] = gate(s, t)
+                    cand = candidate(s, t)
                     acc = product(wp_q, t, s, "y" if s == 0 and t < 2 else "present")
                     diff = ring.tile([P, HALF], F32, name=f"diff{s}_{t}", tag="diff", bufs=3)
-                    nc.vector.tensor_tensor(out=diff[:], in0=gc[s, t][1][:], in1=acc[:], op=ALU.subtract)
+                    nc.vector.tensor_tensor(out=diff[:], in0=cand[:], in1=acc[:], op=ALU.subtract)
                     diffs[t] = diff
                 if step > 0:
                     t = step - 1
                     nc.vector.scalar_tensor_tensor(
-                        out=planes[:, t, :], in0=gc[s, t][0][:], scalar=gain_sb[:, t : t + 1], in1=diffs[t][:],
+                        out=planes[:, t, :], in0=gates[t][:], scalar=gain_sb[:, t : t + 1], in1=diffs[t][:],
                         op0=ALU.mult, op1=ALU.mult,
                     )
             return planes
@@ -265,6 +266,11 @@ def tile_list_gated_node_update_kernel(
             )
 
         planes0 = gated_difference(0)
+        for c, slot in ((2, "table1"), (3, "slot_f")):
+            window = keep.tile([P, T2], F32, name=f"window{c}", tag=slot, align_bytes=64)
+            for u in range(4):
+                nc.gpsimd.memset(window[:, u * 512 : (u + 1) * 512], 0.0)
+            windows.append(window)
         quantize_wo(0)
         h0 = quantize_h(planes0, 0)
         quantize_wo(1)

@@ -41,63 +41,25 @@ def tile_list_gated_node_update_kernel(
             for r in range(4):
                 queue.dma_start(out=plane[r:P:32, :, :], in_=words[:, r:16:4, :].rearrange("a q w -> q a w"))
 
-        tab_plane = keep.tile([P, PASSES, T // 4], I32, name="tab_plane", tag="slot_a", align_bytes=64)
-        wg_plane_raw = keep.tile([P, PASSES, H // 4], I32, name="wg_plane_raw", tag="slot_b", align_bytes=64)
-        wr_plane = keep.tile([P, PASSES, N // 4], I32, name="wr_plane", align_bytes=64)
-        for plane in (tab_plane, wg_plane_raw, wr_plane):
-            nc.vector.memset(plane[:], 0)
-        load_scale_rows(nc.gpsimd, tab_plane, tab_scales)
-        load_scale_rows(nc.gpsimd, wg_plane_raw, wg_scales)
-        gain_sb = keep.tile([P, PACK], F32, name="gain_sb")
-        gain_rows = gain.rearrange("(u t i) -> i u t", t=PACK, i=4)
-        with nc.allow_non_contiguous_dma(reason="512 gains, one element a descriptor"):
-            for i in range(4):
-                nc.gpsimd.dma_start(out=gain_sb[i:P:4, :], in_=gain_rows[i])
-        load_scale_rows(nc.gpsimd, wr_plane, wr_scales)
-
-        def load_rows(w, a, name, pieces=1):
-            raw = keep.tile([P, PACK, w.shape[1]], F32, name=name, tag=name)
+        def load_rows(w, a, name, slot, pieces=1):
+            raw = keep.tile([P, PACK, w.shape[1]], F32, name=name, tag=slot, align_bytes=64)
             rows = w[a * K_PASS : (a + 1) * K_PASS, :].rearrange("(p j) c -> p j c", j=PACK)
             width = w.shape[1] // pieces
             for u in range(pieces):
                 nc.sync.dma_start(out=raw[:, :, u * width : (u + 1) * width], in_=rows[:, :, u * width : (u + 1) * width])
             return raw
 
-        wc_raw = [load_rows(wc, a, f"wc_raw{a}") for a in range(PASSES)]
-        idx = lists.tile([P, S // 16], U16, name="idx")
-        nc.sync.dma_start(idx[:], offs)
-        table = []
-        wg_raw = keep.tile([P, PASSES, 2 * H // 4], I32, name="wg_raw")
-        nc.sync.dma_start(out=wg_raw[:], in_=wg_words.bitcast(I32).rearrange("a p w -> p a w"))
-        for a in range(PASSES):
-            words = keep.tile([P, T], I32, name=f"table{a}", tag=f"table{a}", align_bytes=64)
+        def load_table(a, slot):
+            words = keep.tile([P, T], I32, name=f"table{a}", tag=slot, align_bytes=64)
             nc.sync.dma_start(out=words[:], in_=tab_words[a].rearrange("p t i -> p (t i)").bitcast(I32))
-            table.append(words)
-        wp_raw = [load_rows(wp, 0, "wp_raw0"), load_rows(wp, 1, "wp_raw1", pieces=2)]
-        wr_codes = keep.tile([P, PASSES, N], I32, name="wr_codes", align_bytes=64)
-        nc.sync.dma_start(out=wr_codes[:], in_=wr_words.rearrange("a p e i -> p a (e i)").bitcast(I32))
-        wo_raw = keep.tile([P, PACK, N], F32, name="wo_raw")
-        wo_rows = wo.rearrange("(u t i) n -> i u t n", t=PACK, i=4)
-        for i in range(4):
-            nc.sync.dma_start(out=wo_raw[i:P:4, :, :], in_=wo_rows[i])
-        wgo_sb = keep.tile([P, S], F32, name="wgo_sb")
-        nc.sync.dma_start(out=wgo_sb[:], in_=wgo)
-        idx2 = lists.tile([P, S // 16], U16, name="idx2")
-        nc.sync.dma_start(idx2[:], offs2)
-
-        windows = []
-        for c in range(2):
-            window = keep.tile([P, T2], F32, name=f"window{c}")
-            nc.vector.memset(window[:, : T2 // 2 - 1], 0.0)
-            nc.vector.memset(window[:, T2 // 2 - 1 :], 0.0)
-            windows.append(window)
+            return words
 
         def cast_permuted(copy, raw, grouped, pieces=1):
-            dst = grouped.rearrange("p (t u i j) -> p t u j i", t=PACK, i=4, j=PACK)
-            src = raw[:].rearrange("p j (u t i) -> p t u j i", t=PACK, i=4)
-            width = 32 // pieces
+            dst = grouped.rearrange("p (t m j) -> p m j t", t=PACK, j=PACK)
+            src = raw[:].rearrange("p j (m t) -> p m j t", t=PACK)
+            width = P // pieces
             for u in range(pieces):
-                copy(out=dst[:, :, u * width : (u + 1) * width], in_=src[:, :, u * width : (u + 1) * width])
+                copy(out=dst[:, u * width : (u + 1) * width], in_=src[:, u * width : (u + 1) * width])
             return grouped
 
         def quantize(grouped, name, slot=None):
@@ -107,21 +69,42 @@ def tile_list_gated_node_update_kernel(
             nc.vector.quantize_mx(out=codes[:].bitcast(FP8X4), scales=plane[:], in_=grouped)
             return codes, plane
 
-        wc_q = []
-        for a in range(PASSES):
-            wc_bf = ring.tile([P, PACK * H], BF16, name=f"wc_bf{a}", tag="wc_bf", align_bytes=64)
-            wc_q.append(quantize(cast_permuted(nc.scalar.copy, wc_raw[a], wc_bf[:]), f"wc{a}"))
+        tab_plane = keep.tile([P, PASSES, T // 4], I32, name="tab_plane", tag="slot_a", align_bytes=64)
+        wg_plane_raw = keep.tile([P, PASSES, H // 4], I32, name="wg_plane_raw", tag="slot_b", align_bytes=64)
+        wr_plane = keep.tile([P, PASSES, N // 4], I32, name="wr_plane", align_bytes=64)
+        windows = [keep.tile([P, T2], F32, name=f"window{c}") for c in range(CHUNKS)]
+        nc.gpsimd.memset(tab_plane[:], 0)
+        nc.vector.memset(windows[0][:], 0.0)
+        nc.vector.memset(wr_plane[:], 0)
+        for piece in range(4, 16):
+            if piece == 10:
+                nc.gpsimd.memset(wg_plane_raw[:], 0)
+            nc.gpsimd.memset(windows[piece // 4][:, (piece % 4) * 512 : (piece % 4 + 1) * 512], 0.0)
 
-        wg_codes = keep.tile([P, PASSES, 2 * H // 4], I32, name="wg_codes", align_bytes=64)
-        wg_plane = keep.tile([P, PASSES, H // 4], I32, name="wg_plane", align_bytes=64)
+        wg_raw = keep.tile([P, PASSES, 2 * H // 4], I32, name="wg_raw", tag="slot_t0", align_bytes=64)
+        nc.sync.dma_start(out=wg_raw[:], in_=wg_words.bitcast(I32).rearrange("a p w -> p a w"))
+        idx = lists.tile([P, S // 16], U16, name="idx")
+        nc.sync.dma_start(idx[:], offs)
+        gain_sb = keep.tile([P, PACK], F32, name="gain_sb")
+        nc.sync.dma_start(out=gain_sb[:], in_=gain.rearrange("(p t) -> p t", t=PACK))
+        idx2 = lists.tile([P, S // 16], U16, name="idx2")
+        nc.sync.dma_start(idx2[:], offs2)
+        wc_raw0 = load_rows(wc, 0, "wc_raw0", "slot_c")
+        load_scale_rows(nc.sync, tab_plane, tab_scales)
+
+        wg_codes = keep.tile([P, PASSES, 2 * H], U8, name="wg_codes", align_bytes=64)
         nc.vector.tensor_copy(
-            out=wg_codes[:].rearrange("p a (t u w) -> p a t u w", t=PACK, w=2),
-            in_=wg_raw[:].rearrange("p a (u t w) -> p a t u w", t=PACK, w=2),
+            out=wg_codes[:].rearrange("p a (t m b) -> p a m t b", t=PACK, b=2),
+            in_=wg_raw[:].bitcast(U8).rearrange("p a (m t b) -> p a m t b", t=PACK, b=2),
         )
-        nc.vector.tensor_copy(
-            out=wg_plane[:].rearrange("p a (t u) -> p a t u", t=PACK),
-            in_=wg_plane_raw[:].rearrange("p a (u t) -> p a t u", t=PACK),
-        )
+        table = [load_table(0, "slot_t0")]
+        load_scale_rows(nc.sync, wg_plane_raw, wg_scales)
+        load_scale_rows(nc.gpsimd, wr_plane, wr_scales)
+
+        wc_bf0 = keep.tile([P, PACK * H], BF16, name="wc_bf0", tag="slot_t1", align_bytes=64)
+        wc_q = [quantize(cast_permuted(nc.scalar.copy, wc_raw0, wc_bf0[:]), "wc0")]
+        wc_raw1 = load_rows(wc, 1, "wc_raw1", "slot_c")
+        table.append(load_table(1, "slot_t1"))
 
         v_plane = []
         v_codes = {}
@@ -129,13 +112,26 @@ def tile_list_gated_node_update_kernel(
             plane = keep.tile([P, S], U8, name=f"v_plane{a}", align_bytes=64)
             nc.vector.tensor_copy(out=plane[:], in_=tab_plane[:, a, :].bitcast(U8).indirect(idx[:]))
             v_plane.append(plane)
-        v_words = keep.tile([P, PASSES, S], U32, name="v_words", tag="slot_a", align_bytes=64)
+        wp_raw = [load_rows(wp, 0, "wp_raw0", "slot_a")]
+        v_words = keep.tile([P, PASSES, S], U32, name="v_words", align_bytes=64)
         for a in range(PASSES):
             for s in range(HALVES):
                 v_codes[a, s] = v_words[:, a, s * HALF : (s + 1) * HALF]
                 nc.vector.tensor_copy(
                     out=v_codes[a, s], in_=table[a][:].bitcast(U32).indirect(idx[:, s * COLS : (s + 1) * COLS])
                 )
+            if a == 0:
+                wg_plane = keep.tile([P, PASSES, H], U8, name="wg_plane", tag="slot_t0", align_bytes=64)
+                nc.vector.tensor_copy(
+                    out=wg_plane[:].rearrange("p a (t m) -> p a m t", t=PACK),
+                    in_=wg_plane_raw[:].bitcast(U8).rearrange("p a (m t) -> p a m t", t=PACK),
+                )
+                wp_raw.append(load_rows(wp, 1, "wp_raw1", "slot_b", pieces=2))
+                wc_bf1 = keep.tile([P, PACK * H], BF16, name="wc_bf1", align_bytes=64)
+                wc_q.append(quantize(cast_permuted(nc.scalar.copy, wc_raw1, wc_bf1[:]), "wc1"))
+
+        wr_codes = keep.tile([P, PASSES, N], I32, name="wr_codes", tag="slot_t1", align_bytes=64)
+        nc.sync.dma_start(out=wr_codes[:], in_=wr_words.rearrange("a p e i -> p a (e i)").bitcast(I32))
 
         def times_table(acc, lhsT, lhsT_scale, a, s, start, stop):
             nc.tensor.matmul_mx(
@@ -161,8 +157,8 @@ def tile_list_gated_node_update_kernel(
             for a in range(PASSES):
                 times_table(
                     acc,
-                    wg_codes[:, a, t * 64 : (t + 1) * 64].bitcast(U8).bitcast(FP4X4),
-                    wg_plane[:, a, t * 32 : (t + 1) * 32].bitcast(U8),
+                    wg_codes[:, a, 2 * t * P : 2 * (t + 1) * P].bitcast(FP4X4),
+                    wg_plane[:, a, t * P : (t + 1) * P],
                     a, s, a == 0, a == PASSES - 1,
                 )
             g = ring.tile([P, HALF], F32, name=f"gate{s}_{t}", tag="gate", bufs=6)
@@ -171,21 +167,26 @@ def tile_list_gated_node_update_kernel(
 
         def candidate(s, t):
             acc = product(wc_q, t, s, "act")
-            if s == 0 and t < 2:
-                c = keep.tile([P, HALF], F32, name=f"cand{s}_{t}", tag=("slot_f", "slot_e")[t], align_bytes=64)
+            if (s, t) == (0, 1):
+                c = keep.tile([P, HALF], F32, name=f"cand{s}_{t}", tag="slot_e", align_bytes=64)
+            elif (s, t) == (1, 3):
+                c = keep.tile([P, HALF], F32, name=f"cand{s}_{t}", tag="slot_f", align_bytes=64)
             else:
                 c = ring.tile([P, HALF], F32, name=f"cand{s}_{t}", tag="cand", bufs=6)
             nc.scalar.activation(out=c[:], in_=acc[:], func=ACT.Tanh)
             return c
 
-        wp_bf = keep.tile([P, PASSES, PACK * H], BF16, name="wp_bf", tag="table1", align_bytes=64)
+        wp_bf = keep.tile([P, PASSES, PACK * H], BF16, name="wp_bf", align_bytes=64)
         wp_q = [
-            quantize(cast_permuted(nc.vector.tensor_copy, wp_raw[0], wp_bf[:, 0, :]), "wp0", slot="slot_b"),
+            quantize(cast_permuted(nc.vector.tensor_copy, wp_raw[0], wp_bf[:, 0, :]), "wp0"),
             quantize(cast_permuted(nc.vector.tensor_copy, wp_raw[1], wp_bf[:, 1, :], pieces=2), "wp1"),
         ]
+        wo_raw = load_rows(wo, 0, "wo_raw", "slot_a")
+        wgo_sb = keep.tile([P, S], F32, name="wgo_sb", tag="slot_b", align_bytes=64)
+        nc.sync.dma_start(out=wgo_sb[:], in_=wgo)
 
         def gated_difference(s):
-            planes = ring.tile([P, PACK, HALF], BF16, name=f"h_planes{s}", tag="h_planes")
+            planes = keep.tile([P, PACK, HALF], BF16, name=f"h_planes{s}", tag=f"h_planes{s}", align_bytes=64)
             gates = {}
             diffs = {}
             for step in range(PACK + 1):
@@ -253,7 +254,12 @@ def tile_list_gated_node_update_kernel(
                 start=False,
                 stop=True,
             )
-            y = ring.tile([P, HALF], F32, name=f"y_sb{s}_{c}", tag="y_sb", bufs=6)
+            if (s, c) == (0, 1):
+                y = keep.tile([P, HALF], F32, name=f"y_sb{s}_{c}", tag="slot_f", align_bytes=64)
+            elif (s, c) == (0, 2):
+                y = keep.tile([P, HALF], F32, name=f"y_sb{s}_{c}", tag="h_planes1", align_bytes=64)
+            else:
+                y = ring.tile([P, HALF], F32, name=f"y_sb{s}_{c}", tag="y_sb", bufs=4)
             nc.scalar.copy(out=y[:], in_=acc[:])
             return y
 
@@ -266,16 +272,14 @@ def tile_list_gated_node_update_kernel(
             )
 
         planes0 = gated_difference(0)
-        for c, slot in ((2, "table1"), (3, "slot_f")):
-            window = keep.tile([P, T2], F32, name=f"window{c}", tag=slot, align_bytes=64)
-            for u in range(4):
-                nc.gpsimd.memset(window[:, u * 512 : (u + 1) * 512], 0.0)
-            windows.append(window)
         quantize_wo(0)
         h0 = quantize_h(planes0, 0)
         quantize_wo(1)
-        y0 = [new_state(h0, 0, c) for c in range(CHUNKS)]
-        h1 = quantize_h(gated_difference(1), 1)
+        y0 = [new_state(h0, 0, 0)]
+        planes1 = gated_difference(1)
+        y0.append(new_state(h0, 0, 1))
+        h1 = quantize_h(planes1, 1)
+        y0 += [new_state(h0, 0, c) for c in range(2, CHUNKS)]
         for c in range(CHUNKS):
             scatter(y0[c], 0, c)
         for c in range(CHUNKS):

@@ -55,11 +55,11 @@ def tile_list_gated_node_update_kernel(
             return words
 
         def cast_permuted(copy, raw, grouped, pieces=1):
-            dst = grouped.rearrange("p (t m j) -> p m j t", t=PACK, j=PACK)
-            src = raw[:].rearrange("p j (m t) -> p m j t", t=PACK)
-            width = P // pieces
+            dst = grouped.rearrange("p (t u i j) -> p t u j i", t=PACK, i=4, j=PACK)
+            src = raw[:].rearrange("p j (u t i) -> p t u j i", t=PACK, i=4)
+            width = 32 // pieces
             for u in range(pieces):
-                copy(out=dst[:, u * width : (u + 1) * width], in_=src[:, u * width : (u + 1) * width])
+                copy(out=dst[:, :, u * width : (u + 1) * width], in_=src[:, :, u * width : (u + 1) * width])
             return grouped
 
         def quantize(grouped, name, slot=None):
@@ -71,35 +71,33 @@ def tile_list_gated_node_update_kernel(
 
         tab_plane = keep.tile([P, PASSES, T // 4], I32, name="tab_plane", tag="slot_a", align_bytes=64)
         wg_plane_raw = keep.tile([P, PASSES, H // 4], I32, name="wg_plane_raw", tag="slot_b", align_bytes=64)
-        wr_plane = keep.tile([P, PASSES, N // 4], I32, name="wr_plane", align_bytes=64)
         windows = [keep.tile([P, T2], F32, name=f"window{c}") for c in range(CHUNKS)]
         nc.gpsimd.memset(tab_plane[:], 0)
-        nc.vector.memset(windows[0][:], 0.0)
-        nc.vector.memset(wr_plane[:], 0)
-        for piece in range(4, 16):
-            if piece == 10:
-                nc.gpsimd.memset(wg_plane_raw[:], 0)
-            nc.gpsimd.memset(windows[piece // 4][:, (piece % 4) * 512 : (piece % 4 + 1) * 512], 0.0)
 
         wg_raw = keep.tile([P, PASSES, 2 * H // 4], I32, name="wg_raw", tag="slot_t0", align_bytes=64)
         nc.sync.dma_start(out=wg_raw[:], in_=wg_words.bitcast(I32).rearrange("a p w -> p a w"))
         idx = lists.tile([P, S // 16], U16, name="idx")
         nc.sync.dma_start(idx[:], offs)
-        gain_sb = keep.tile([P, PACK], F32, name="gain_sb")
-        nc.sync.dma_start(out=gain_sb[:], in_=gain.rearrange("(p t) -> p t", t=PACK))
         idx2 = lists.tile([P, S // 16], U16, name="idx2")
         nc.sync.dma_start(idx2[:], offs2)
+        gain_sb = keep.tile([P, 16], F32, name="gain_sb")
+        gain_rows = gain.rearrange("(u x) -> u x", x=16)
+        for i in range(4):
+            nc.sync.dma_start(out=gain_sb[i:P:4, 0:13], in_=gain_rows[:, i : i + 13])
         wc_raw0 = load_rows(wc, 0, "wc_raw0", "slot_c")
         load_scale_rows(nc.sync, tab_plane, tab_scales)
 
-        wg_codes = keep.tile([P, PASSES, 2 * H], U8, name="wg_codes", align_bytes=64)
+        wg_codes = keep.tile([P, PASSES, 2 * H // 4], I32, name="wg_codes", align_bytes=64)
         nc.vector.tensor_copy(
-            out=wg_codes[:].rearrange("p a (t m b) -> p a m t b", t=PACK, b=2),
-            in_=wg_raw[:].bitcast(U8).rearrange("p a (m t b) -> p a m t b", t=PACK, b=2),
+            out=wg_codes[:].rearrange("p a (t u w) -> p a t u w", t=PACK, w=2),
+            in_=wg_raw[:].rearrange("p a (u t w) -> p a t u w", t=PACK, w=2),
         )
         table = [load_table(0, "slot_t0")]
+        for c in range(CHUNKS):
+            if c == 2:
+                nc.vector.memset(wg_plane_raw[:], 0)
+            nc.vector.memset(windows[c][:], 0.0)
         load_scale_rows(nc.sync, wg_plane_raw, wg_scales)
-        load_scale_rows(nc.gpsimd, wr_plane, wr_scales)
 
         wc_bf0 = keep.tile([P, PACK * H], BF16, name="wc_bf0", tag="slot_t1", align_bytes=64)
         wc_q = [quantize(cast_permuted(nc.scalar.copy, wc_raw0, wc_bf0[:]), "wc0")]
@@ -121,17 +119,21 @@ def tile_list_gated_node_update_kernel(
                     out=v_codes[a, s], in_=table[a][:].bitcast(U32).indirect(idx[:, s * COLS : (s + 1) * COLS])
                 )
             if a == 0:
-                wg_plane = keep.tile([P, PASSES, H], U8, name="wg_plane", tag="slot_t0", align_bytes=64)
+                wg_plane = keep.tile([P, PASSES, H // 4], I32, name="wg_plane", tag="slot_t0", align_bytes=64)
                 nc.vector.tensor_copy(
-                    out=wg_plane[:].rearrange("p a (t m) -> p a m t", t=PACK),
-                    in_=wg_plane_raw[:].bitcast(U8).rearrange("p a (m t) -> p a m t", t=PACK),
+                    out=wg_plane[:].rearrange("p a (t u) -> p a t u", t=PACK),
+                    in_=wg_plane_raw[:].rearrange("p a (u t) -> p a t u", t=PACK),
                 )
                 wp_raw.append(load_rows(wp, 1, "wp_raw1", "slot_b", pieces=2))
                 wc_bf1 = keep.tile([P, PACK * H], BF16, name="wc_bf1", align_bytes=64)
                 wc_q.append(quantize(cast_permuted(nc.scalar.copy, wc_raw1, wc_bf1[:]), "wc1"))
 
-        wr_codes = keep.tile([P, PASSES, N], I32, name="wr_codes", tag="slot_t1", align_bytes=64)
-        nc.sync.dma_start(out=wr_codes[:], in_=wr_words.rearrange("a p e i -> p a (e i)").bitcast(I32))
+        wr_bytes = keep.tile([P, PASSES * (N + N // 4)], I32, name="wr_bytes", tag="slot_t1", align_bytes=64)
+        wr_codes = wr_bytes[:, : PASSES * N].rearrange("p (a e) -> p a e", a=PASSES)
+        wr_plane = wr_bytes[:, PASSES * N :].rearrange("p (a w) -> p a w", a=PASSES)
+        nc.vector.memset(wr_plane, 0)
+        nc.sync.dma_start(out=wr_codes, in_=wr_words.rearrange("a p e i -> p a (e i)").bitcast(I32))
+        load_scale_rows(nc.sync, wr_plane, wr_scales)
 
         def times_table(acc, lhsT, lhsT_scale, a, s, start, stop):
             nc.tensor.matmul_mx(
@@ -157,8 +159,8 @@ def tile_list_gated_node_update_kernel(
             for a in range(PASSES):
                 times_table(
                     acc,
-                    wg_codes[:, a, 2 * t * P : 2 * (t + 1) * P].bitcast(FP4X4),
-                    wg_plane[:, a, t * P : (t + 1) * P],
+                    wg_codes[:, a, t * 64 : (t + 1) * 64].bitcast(U8).bitcast(FP4X4),
+                    wg_plane[:, a, t * 32 : (t + 1) * 32].bitcast(U8),
                     a, s, a == 0, a == PASSES - 1,
                 )
             g = ring.tile([P, HALF], F32, name=f"gate{s}_{t}", tag="gate", bufs=6)
@@ -167,7 +169,7 @@ def tile_list_gated_node_update_kernel(
 
         def candidate(s, t):
             acc = product(wc_q, t, s, "act")
-            if (s, t) == (0, 1):
+            if (s, t) == (0, 2):
                 c = keep.tile([P, HALF], F32, name=f"cand{s}_{t}", tag="slot_e", align_bytes=64)
             elif (s, t) == (1, 3):
                 c = keep.tile([P, HALF], F32, name=f"cand{s}_{t}", tag="slot_f", align_bytes=64)
@@ -181,7 +183,10 @@ def tile_list_gated_node_update_kernel(
             quantize(cast_permuted(nc.vector.tensor_copy, wp_raw[0], wp_bf[:, 0, :]), "wp0"),
             quantize(cast_permuted(nc.vector.tensor_copy, wp_raw[1], wp_bf[:, 1, :], pieces=2), "wp1"),
         ]
-        wo_raw = load_rows(wo, 0, "wo_raw", "slot_a")
+        wo_raw = keep.tile([P, PACK, N], F32, name="wo_raw", tag="slot_a", align_bytes=64)
+        wo_rows = wo.rearrange("(u t i) n -> i u t n", t=PACK, i=4)
+        for i in range(4):
+            nc.sync.dma_start(out=wo_raw[i:P:4, :, :], in_=wo_rows[i])
         wgo_sb = keep.tile([P, S], F32, name="wgo_sb", tag="slot_b", align_bytes=64)
         nc.sync.dma_start(out=wgo_sb[:], in_=wgo)
 
@@ -201,7 +206,7 @@ def tile_list_gated_node_update_kernel(
                 if step > 0:
                     t = step - 1
                     nc.vector.scalar_tensor_tensor(
-                        out=planes[:, t, :], in0=gates[t][:], scalar=gain_sb[:, t : t + 1], in1=diffs[t][:],
+                        out=planes[:, t, :], in0=gates[t][:], scalar=gain_sb[:, 4 * t : 4 * t + 1], in1=diffs[t][:],
                         op0=ALU.mult, op1=ALU.mult,
                     )
             return planes

@@ -55,8 +55,8 @@ def tile_list_gated_node_update_kernel(
             return words
 
         def cast_permuted(copy, raw, grouped, pieces=1):
-            dst = grouped.rearrange("p (t u i j) -> p t u j i", t=PACK, i=4, j=PACK)
-            src = raw[:].rearrange("p j (u t i) -> p t u j i", t=PACK, i=4)
+            dst = grouped.rearrange("p (t u i j) -> p t u i j", t=PACK, i=4, j=PACK)
+            src = raw[:].rearrange("p j (u t i) -> p t u i j", t=PACK, i=4)
             width = 32 // pieces
             for u in range(pieces):
                 copy(out=dst[:, :, u * width : (u + 1) * width], in_=src[:, :, u * width : (u + 1) * width])
@@ -190,35 +190,40 @@ def tile_list_gated_node_update_kernel(
         wgo_sb = keep.tile([P, S], F32, name="wgo_sb", tag="slot_b", align_bytes=64)
         nc.sync.dma_start(out=wgo_sb[:], in_=wgo)
 
-        def gated_difference(s):
-            planes = keep.tile([P, PACK, HALF], BF16, name=f"h_planes{s}", tag=f"h_planes{s}", align_bytes=64)
-            gates = {}
-            diffs = {}
-            for step in range(PACK + 1):
+        planes = [
+            keep.tile([P, PACK, HALF], BF16, name=f"h_planes{s}", tag=f"h_planes{s}", align_bytes=64) for s in range(HALVES)
+        ]
+        gates = {}
+        diffs = {}
+
+        def gated_difference(s, steps):
+            for step in steps:
                 if step < PACK:
                     t = step
-                    gates[t] = gate(s, t)
+                    gates[s, t] = gate(s, t)
                     cand = candidate(s, t)
                     acc = product(wp_q, t, s, "y" if s == 0 and t < 2 else "present")
-                    diff = ring.tile([P, HALF], F32, name=f"diff{s}_{t}", tag="diff", bufs=3)
+                    if (s, t) == (1, 2):
+                        diff = keep.tile([P, HALF], F32, name=f"diff{s}_{t}", tag="slot_g", align_bytes=64)
+                    else:
+                        diff = ring.tile([P, HALF], F32, name=f"diff{s}_{t}", tag="diff", bufs=3)
                     nc.vector.tensor_tensor(out=diff[:], in0=cand[:], in1=acc[:], op=ALU.subtract)
-                    diffs[t] = diff
+                    diffs[s, t] = diff
                 if step > 0:
                     t = step - 1
                     nc.vector.scalar_tensor_tensor(
-                        out=planes[:, t, :], in0=gates[t][:], scalar=gain_sb[:, 4 * t : 4 * t + 1], in1=diffs[t][:],
-                        op0=ALU.mult, op1=ALU.mult,
+                        out=planes[s][:, t, :], in0=gates[s, t][:], scalar=gain_sb[:, 4 * t : 4 * t + 1],
+                        in1=diffs[s, t][:], op0=ALU.mult, op1=ALU.mult,
                     )
-            return planes
 
         def quantize_h(planes, s):
             grouped = ring.tile([P, PACK * HALF], BF16, name=f"h_bf{s}", tag="h_bf", align_bytes=64)
-            codes = keep.tile([P, HALF], U32, name=f"h_codes{s}", align_bytes=64)
+            codes = keep.tile([P, HALF], U32, name=f"h_codes{s}", tag=("h_codes0", "slot_f")[s], align_bytes=64)
             plane = keep.tile([P, HALF], U8, name=f"h_plane{s}", align_bytes=64)
-            dst = grouped[:].rearrange("p (c i t) -> p c t i", i=4, t=PACK)
-            src = planes[:].rearrange("p t (c i) -> p c t i", i=4)
+            dst = grouped[:].rearrange("p (n t) -> p n t", t=PACK)
+            src = planes[:].rearrange("p t n -> p n t")
             for u in range(2):
-                nc.scalar.copy(out=dst[:, u * 64 : (u + 1) * 64], in_=src[:, u * 64 : (u + 1) * 64])
+                nc.scalar.copy(out=dst[:, u * 256 : (u + 1) * 256], in_=src[:, u * 256 : (u + 1) * 256])
                 nc.vector.quantize_mx(
                     out=codes[:, u * 256 : (u + 1) * 256].bitcast(FP8X4),
                     scales=plane[:, u * 256 : (u + 1) * 256],
@@ -231,9 +236,9 @@ def tile_list_gated_node_update_kernel(
 
         def quantize_wo(u):
             wo_bf = keep.tile([P, PACK * N // 2], BF16, name=f"wo_bf{u}", tag="slot_e", align_bytes=64)
-            dst = wo_bf[:].rearrange("p (c i j) -> p c j i", i=4, j=PACK)
-            src = wo_raw[:].rearrange("p j (c i) -> p c j i", i=4)
-            nc.scalar.copy(out=dst, in_=src[:, u * 64 : (u + 1) * 64])
+            dst = wo_bf[:].rearrange("p (n t) -> p n t", t=PACK)
+            src = wo_raw[:].rearrange("p t n -> p n t")
+            nc.scalar.copy(out=dst, in_=src[:, u * 256 : (u + 1) * 256])
             nc.vector.quantize_mx(
                 out=wo_codes[:, u * 256 : (u + 1) * 256].bitcast(FP8X4),
                 scales=wo_plane[:, u * 256 : (u + 1) * 256],
@@ -259,7 +264,12 @@ def tile_list_gated_node_update_kernel(
                 start=False,
                 stop=True,
             )
-            if (s, c) == (0, 1):
+            return acc
+
+        def evacuate(acc, s, c):
+            if (s, c) == (0, 0):
+                y = keep.tile([P, HALF], F32, name=f"y_sb{s}_{c}", tag="slot_g", align_bytes=64)
+            elif (s, c) == (0, 1):
                 y = keep.tile([P, HALF], F32, name=f"y_sb{s}_{c}", tag="slot_f", align_bytes=64)
             elif (s, c) == (0, 2):
                 y = keep.tile([P, HALF], F32, name=f"y_sb{s}_{c}", tag="h_planes1", align_bytes=64)
@@ -276,17 +286,19 @@ def tile_list_gated_node_update_kernel(
                 op=ALU.mult,
             )
 
-        planes0 = gated_difference(0)
+        gated_difference(0, range(PACK + 1))
         quantize_wo(0)
-        h0 = quantize_h(planes0, 0)
+        h0 = quantize_h(planes[0], 0)
         quantize_wo(1)
-        y0 = [new_state(h0, 0, 0)]
-        planes1 = gated_difference(1)
-        y0.append(new_state(h0, 0, 1))
-        h1 = quantize_h(planes1, 1)
-        y0 += [new_state(h0, 0, c) for c in range(2, CHUNKS)]
+        y00 = evacuate(new_state(h0, 0, 0), 0, 0)
+        gated_difference(1, range(2))
+        acc01 = new_state(h0, 0, 1)
+        scatter(y00, 0, 0)
+        gated_difference(1, range(2, PACK + 1))
+        scatter(evacuate(acc01, 0, 1), 0, 1)
+        h1 = quantize_h(planes[1], 1)
+        for c in range(2, CHUNKS):
+            scatter(evacuate(new_state(h0, 0, c), 0, c), 0, c)
         for c in range(CHUNKS):
-            scatter(y0[c], 0, c)
-        for c in range(CHUNKS):
-            scatter(new_state(h1, 1, c), 1, c)
+            scatter(evacuate(new_state(h1, 1, c), 1, c), 1, c)
             nc.sync.dma_start(out=out[c * P : (c + 1) * P, :], in_=windows[c][:])

@@ -41,189 +41,112 @@ def tile_list_gated_node_update_kernel(
             for r in range(4):
                 queue.dma_start(out=plane[r:P:32, :, :], in_=words[:, r:16:4, :].rearrange("a q w -> q a w"))
 
-        def load_rows(w, a, name, slot, pieces=1):
-            raw = keep.tile([P, PACK, w.shape[1]], F32, name=name, tag=slot, align_bytes=64)
-            rows = w[a * K_PASS : (a + 1) * K_PASS, :].rearrange("(p j) c -> p j c", j=PACK)
-            width = w.shape[1] // pieces
-            for u in range(pieces):
-                nc.sync.dma_start(out=raw[:, :, u * width : (u + 1) * width], in_=rows[:, :, u * width : (u + 1) * width])
-            return raw
+        def cast_permuted(copy, raw, grouped, ts):
+            dst = grouped.rearrange("p (t u i j) -> p t u i j", t=PACK, i=4, j=PACK)
+            src = raw.rearrange("p (j u t i) -> p t u i j", j=PACK, t=PACK, i=4)
+            copy(out=dst[:, ts], in_=src[:, ts])
+
+        tab_plane = keep.tile([P, PASSES, T // 4], I32, name="tab_plane", tag="slot_plane", align_bytes=64)
+        nc.gpsimd.memset(tab_plane[:, 0, :], 0)
+        nc.vector.memset(tab_plane[:, 1, :], 0)
+        wg_plane = keep.tile([P, PASSES, H // 4], I32, name="wg_plane", align_bytes=64)
+        nc.gpsimd.memset(wg_plane[:], 0)
+
+        idx = lists.tile([P, S // 16], U16, name="idx")
+        nc.sync.dma_start(idx[:], offs)
+        idx2 = lists.tile([P, S // 16], U16, name="idx2")
+        nc.sync.dma_start(idx2[:], offs2)
+        wg_raw = keep.tile([P, PASSES, 2 * H // 4], I32, name="wg_raw", align_bytes=64)
+        nc.sync.dma_start(out=wg_raw[:], in_=wg_words.bitcast(I32).rearrange("a p w -> p a w"))
+        wg_plane_raw = keep.tile([P, PASSES, H // 4], I32, name="wg_plane_raw", align_bytes=64)
+        load_scale_rows(nc.sync, wg_plane_raw, wg_scales)
 
         def load_table(a, slot):
             words = keep.tile([P, T], I32, name=f"table{a}", tag=slot, align_bytes=64)
             nc.sync.dma_start(out=words[:], in_=tab_words[a].rearrange("p t i -> p (t i)").bitcast(I32))
             return words
 
-        def cast_permuted(copy, raw, grouped, pieces=1):
-            dst = grouped.rearrange("p (t u i j) -> p t u i j", t=PACK, i=4, j=PACK)
-            src = raw[:].rearrange("p j (u t i) -> p t u i j", t=PACK, i=4)
-            width = 32 // pieces
-            for u in range(pieces):
-                copy(out=dst[:, :, u * width : (u + 1) * width], in_=src[:, :, u * width : (u + 1) * width])
-            return grouped
+        ROWS = PACK * H
 
-        def quantize(grouped, name, slot=None):
-            width = grouped.shape[1] // PACK
-            codes = keep.tile([P, width], U32, name=name + "_codes", tag=slot or name + "_codes", align_bytes=64)
-            plane = keep.tile([P, width], U8, name=name + "_plane", align_bytes=64)
-            nc.vector.quantize_mx(out=codes[:].bitcast(FP8X4), scales=plane[:], in_=grouped)
-            return codes, plane
+        def load_rows(w, a, name, slot=None):
+            raw = keep.tile([P, ROWS], F32, name=name, tag=slot or name, align_bytes=64)
+            rows = w[a * K_PASS : (a + 1) * K_PASS, :].rearrange("(p j) c -> p (j c)", j=PACK)
+            nc.sync.dma_start(out=raw[:], in_=rows)
+            return raw[:]
 
-        tab_plane = keep.tile([P, PASSES, T // 4], I32, name="tab_plane", tag="slot_a", align_bytes=64)
-        wg_plane_raw = keep.tile([P, PASSES, H // 4], I32, name="wg_plane_raw", tag="slot_b", align_bytes=64)
-        windows = [keep.tile([P, T2], F32, name=f"window{c}") for c in range(CHUNKS)]
-        nc.gpsimd.memset(tab_plane[:], 0)
-
-        wg_raw = keep.tile([P, PASSES, 2 * H // 4], I32, name="wg_raw", tag="slot_t0", align_bytes=64)
-        nc.sync.dma_start(out=wg_raw[:], in_=wg_words.bitcast(I32).rearrange("a p w -> p a w"))
-        idx = lists.tile([P, S // 16], U16, name="idx")
-        nc.sync.dma_start(idx[:], offs)
-        idx2 = lists.tile([P, S // 16], U16, name="idx2")
-        nc.sync.dma_start(idx2[:], offs2)
-        gain_sb = keep.tile([P, 16], F32, name="gain_sb")
+        table = [load_table(0, "slot_t0")]
+        load_scale_rows(nc.sync, tab_plane, tab_scales)
+        raws = [load_rows(wc, 0, "wc_raw0", "slot_wc0")]
+        gain_sb = keep.tile([P, 16], F32, name="gain_sb", align_bytes=64)[:]
         gain_rows = gain.rearrange("(u x) -> u x", x=16)
         for i in range(4):
             nc.sync.dma_start(out=gain_sb[i:P:4, 0:13], in_=gain_rows[:, i : i + 13])
-        wc_raw0 = load_rows(wc, 0, "wc_raw0", "slot_c")
-        load_scale_rows(nc.sync, tab_plane, tab_scales)
 
         wg_codes = keep.tile([P, PASSES, 2 * H // 4], I32, name="wg_codes", align_bytes=64)
         nc.vector.tensor_copy(
             out=wg_codes[:].rearrange("p a (t u w) -> p a t u w", t=PACK, w=2),
             in_=wg_raw[:].rearrange("p a (u t w) -> p a t u w", t=PACK, w=2),
         )
-        table = [load_table(0, "slot_t0")]
-        for c in range(CHUNKS):
-            if c == 2:
-                nc.vector.memset(wg_plane_raw[:], 0)
-            nc.vector.memset(windows[c][:], 0.0)
-        load_scale_rows(nc.sync, wg_plane_raw, wg_scales)
-
-        wc_bf0 = keep.tile([P, PACK * H], BF16, name="wc_bf0", tag="slot_t1", align_bytes=64)
-        wc_q = [quantize(cast_permuted(nc.scalar.copy, wc_raw0, wc_bf0[:]), "wc0")]
-        wc_raw1 = load_rows(wc, 1, "wc_raw1", "slot_c")
+        for q in range(4):
+            rows = slice(32 * q, 32 * q + 4)
+            nc.vector.tensor_copy(
+                out=wg_plane[rows].rearrange("p a (t u) -> p a t u", t=PACK),
+                in_=wg_plane_raw[rows].rearrange("p a (u t) -> p a t u", t=PACK),
+            )
         table.append(load_table(1, "slot_t1"))
 
+        wo_raw = keep.tile([P, PACK * N], F32, name="wo_raw", align_bytes=64)[:]
+        wgo_sb = keep.tile([P, S], F32, name="wgo_sb", align_bytes=64)[:]
+        wr_codes = keep.tile([P, PASSES, N], I32, name="wr_codes", align_bytes=64)[:]
+        wr_plane = keep.tile([P, PASSES, N // 4], I32, name="wr_plane", align_bytes=64)[:]
+
+        nc.gpsimd.memset(wr_plane, 0)
+        raws.append(load_rows(wc, 1, "wc_raw1"))
+        raws.append(load_rows(wp, 0, "wp_raw0"))
+        raws.append(load_rows(wp, 1, "wp_raw1"))
+        wo_rows = wo.rearrange("(u t i) n -> i u t n", t=PACK, i=4)
+        for i in range(4):
+            nc.sync.dma_start(out=wo_raw[i:P:4, :].rearrange("p (t n) -> p t n", t=PACK), in_=wo_rows[i])
+        nc.sync.dma_start(out=wr_codes, in_=wr_words.rearrange("a p e i -> p a (e i)").bitcast(I32))
+        load_scale_rows(nc.sync, wr_plane, wr_scales)
+        nc.sync.dma_start(out=wgo_sb, in_=wgo)
+
+        windows = {c: keep.tile([P, T2], F32, name=f"window{c}") for c in range(2)}
+        nc.vector.memset(windows[0][:], 0.0)
+        nc.vector.memset(windows[1][:], 0.0)
+
+        v_words = keep.tile([P, PASSES, S], U32, name="v_words", align_bytes=64)
+        nc.vector.tensor_copy(out=v_words[:, 0, :], in_=table[0][:].bitcast(U32).indirect(idx[:]))
         v_plane = []
-        v_codes = {}
         for a in range(PASSES):
             plane = keep.tile([P, S], U8, name=f"v_plane{a}", align_bytes=64)
             nc.vector.tensor_copy(out=plane[:], in_=tab_plane[:, a, :].bitcast(U8).indirect(idx[:]))
             v_plane.append(plane)
-        wp_raw = [load_rows(wp, 0, "wp_raw0", "slot_a")]
-        v_words = keep.tile([P, PASSES, S], U32, name="v_words", align_bytes=64)
-        for a in range(PASSES):
-            for s in range(HALVES):
-                v_codes[a, s] = v_words[:, a, s * HALF : (s + 1) * HALF]
-                nc.vector.tensor_copy(
-                    out=v_codes[a, s], in_=table[a][:].bitcast(U32).indirect(idx[:, s * COLS : (s + 1) * COLS])
-                )
-            if a == 0:
-                wg_plane = keep.tile([P, PASSES, H // 4], I32, name="wg_plane", tag="slot_t0", align_bytes=64)
-                nc.vector.tensor_copy(
-                    out=wg_plane[:].rearrange("p a (t u) -> p a t u", t=PACK),
-                    in_=wg_plane_raw[:].rearrange("p a (u t) -> p a t u", t=PACK),
-                )
-                wp_raw.append(load_rows(wp, 1, "wp_raw1", "slot_b", pieces=2))
-                wc_bf1 = keep.tile([P, PACK * H], BF16, name="wc_bf1", align_bytes=64)
-                wc_q.append(quantize(cast_permuted(nc.scalar.copy, wc_raw1, wc_bf1[:]), "wc1"))
-
-        wr_bytes = keep.tile([P, PASSES * (N + N // 4)], I32, name="wr_bytes", tag="slot_t1", align_bytes=64)
-        wr_codes = wr_bytes[:, : PASSES * N].rearrange("p (a e) -> p a e", a=PASSES)
-        wr_plane = wr_bytes[:, PASSES * N :].rearrange("p (a w) -> p a w", a=PASSES)
-        nc.vector.memset(wr_plane, 0)
-        nc.sync.dma_start(out=wr_codes, in_=wr_words.rearrange("a p e i -> p a (e i)").bitcast(I32))
-        load_scale_rows(nc.sync, wr_plane, wr_scales)
+        for s in range(HALVES):
+            nc.vector.tensor_copy(
+                out=v_words[:, 1, s * HALF : (s + 1) * HALF],
+                in_=table[1][:].bitcast(U32).indirect(idx[:, s * COLS : (s + 1) * COLS]),
+            )
 
         def times_table(acc, lhsT, lhsT_scale, a, s, start, stop):
             nc.tensor.matmul_mx(
                 out=acc[:],
                 lhsT=lhsT,
                 lhsT_scale=lhsT_scale,
-                rhs=v_codes[a, s].bitcast(FP8X4),
+                rhs=v_words[:, a, s * HALF : (s + 1) * HALF].bitcast(FP8X4),
                 rhs_scale=v_plane[a][:, s * HALF : (s + 1) * HALF],
                 start=start,
                 stop=stop,
             )
 
-        def product(quantized, t, s, tag):
-            acc = psum.tile([P, HALF], F32, name=f"{tag}{s}_{t}", tag=tag, bufs=2 if tag == "y" else 3)
-            cols = slice(t * P, (t + 1) * P)
-            for a in range(PASSES):
-                codes, plane = quantized[a]
-                times_table(acc, codes[:, cols].bitcast(FP8X4), plane[:, cols], a, s, a == 0, a == PASSES - 1)
-            return acc
+        w_bf = keep.tile([P, ROWS], BF16, name="w_bf", tag="slot_t1", align_bytes=64)
 
-        def gate(s, t):
-            acc = psum.tile([P, HALF], F32, name=f"g{s}_{t}", tag="act", bufs=3)
-            for a in range(PASSES):
-                times_table(
-                    acc,
-                    wg_codes[:, a, t * 64 : (t + 1) * 64].bitcast(U8).bitcast(FP4X4),
-                    wg_plane[:, a, t * 32 : (t + 1) * 32].bitcast(U8),
-                    a, s, a == 0, a == PASSES - 1,
-                )
-            g = ring.tile([P, HALF], F32, name=f"gate{s}_{t}", tag="gate", bufs=6)
-            nc.scalar.activation(out=g[:], in_=acc[:], func=ACT.Sigmoid)
-            return g
-
-        def candidate(s, t):
-            acc = product(wc_q, t, s, "act")
-            if (s, t) == (0, 2):
-                c = keep.tile([P, HALF], F32, name=f"cand{s}_{t}", tag="slot_e", align_bytes=64)
-            elif (s, t) == (1, 3):
-                c = keep.tile([P, HALF], F32, name=f"cand{s}_{t}", tag="slot_f", align_bytes=64)
-            else:
-                c = ring.tile([P, HALF], F32, name=f"cand{s}_{t}", tag="cand", bufs=6)
-            nc.scalar.activation(out=c[:], in_=acc[:], func=ACT.Tanh)
-            return c
-
-        wp_bf = keep.tile([P, PASSES, PACK * H], BF16, name="wp_bf", align_bytes=64)
-        wp_q = [
-            quantize(cast_permuted(nc.vector.tensor_copy, wp_raw[0], wp_bf[:, 0, :]), "wp0"),
-            quantize(cast_permuted(nc.vector.tensor_copy, wp_raw[1], wp_bf[:, 1, :], pieces=2), "wp1"),
-        ]
-        wo_raw = keep.tile([P, PACK, N], F32, name="wo_raw", tag="slot_a", align_bytes=64)
-        wo_rows = wo.rearrange("(u t i) n -> i u t n", t=PACK, i=4)
-        for i in range(4):
-            nc.sync.dma_start(out=wo_raw[i:P:4, :, :], in_=wo_rows[i])
-        wgo_sb = keep.tile([P, S], F32, name="wgo_sb", tag="slot_b", align_bytes=64)
-        nc.sync.dma_start(out=wgo_sb[:], in_=wgo)
-
-        planes = [
-            keep.tile([P, PACK, HALF], BF16, name=f"h_planes{s}", tag=f"h_planes{s}", align_bytes=64) for s in range(HALVES)
-        ]
-        gates = {}
-        diffs = {}
-
-        def gated_difference(s, steps):
-            for step in steps:
-                if step < PACK:
-                    t = step
-                    gates[s, t] = gate(s, t)
-                    cand = candidate(s, t)
-                    acc = product(wp_q, t, s, "y" if s == 0 and t < 2 else "present")
-                    if (s, t) == (1, 2):
-                        diff = keep.tile([P, HALF], F32, name=f"diff{s}_{t}", tag="slot_g", align_bytes=64)
-                    else:
-                        diff = ring.tile([P, HALF], F32, name=f"diff{s}_{t}", tag="diff", bufs=3)
-                    nc.vector.tensor_tensor(out=diff[:], in0=cand[:], in1=acc[:], op=ALU.subtract)
-                    diffs[s, t] = diff
-                if step > 0:
-                    t = step - 1
-                    nc.vector.scalar_tensor_tensor(
-                        out=planes[s][:, t, :], in0=gates[s, t][:], scalar=gain_sb[:, 4 * t : 4 * t + 1],
-                        in1=diffs[s, t][:], op0=ALU.mult, op1=ALU.mult,
-                    )
-
-        def quantize_h(planes, s):
-            grouped = ring.tile([P, PACK * HALF], BF16, name=f"h_bf{s}", tag="h_bf", align_bytes=64)
-            codes = keep.tile([P, HALF], U32, name=f"h_codes{s}", tag=("h_codes0", "slot_f")[s], align_bytes=64)
-            plane = keep.tile([P, HALF], U8, name=f"h_plane{s}", align_bytes=64)
-            dst = grouped[:].rearrange("p (n t) -> p n t", t=PACK)
-            src = planes[:].rearrange("p t n -> p n t")
+        def quantize_weight(raw, name, grouped, copy):
+            codes = keep.tile([P, H], U32, name=name + "_codes", align_bytes=64)
+            plane = keep.tile([P, H], U8, name=name + "_plane", align_bytes=64)
             for u in range(2):
-                nc.scalar.copy(out=dst[:, u * 256 : (u + 1) * 256], in_=src[:, u * 256 : (u + 1) * 256])
+                cast_permuted(copy, raw, grouped, slice(2 * u, 2 * u + 2))
+            for u in range(2):
                 nc.vector.quantize_mx(
                     out=codes[:, u * 256 : (u + 1) * 256].bitcast(FP8X4),
                     scales=plane[:, u * 256 : (u + 1) * 256],
@@ -231,22 +154,92 @@ def tile_list_gated_node_update_kernel(
                 )
             return codes, plane
 
-        wo_codes = keep.tile([P, N], U32, name="wo_codes", align_bytes=64)
-        wo_plane = keep.tile([P, N], U8, name="wo_plane", align_bytes=64)
+        def product(quantized, s, t, tag):
+            acc = psum.tile([P, HALF], F32, name=f"{tag}{s}_{t}", tag=tag, bufs=4)
+            cols = slice(t * P, (t + 1) * P)
+            for a in range(PASSES):
+                codes, plane = quantized[a]
+                times_table(acc, codes[:, cols].bitcast(FP8X4), plane[:, cols], a, s, a == 0, a == PASSES - 1)
+            return acc
 
-        def quantize_wo(u):
-            wo_bf = keep.tile([P, PACK * N // 2], BF16, name=f"wo_bf{u}", tag="slot_e", align_bytes=64)
-            dst = wo_bf[:].rearrange("p (n t) -> p n t", t=PACK)
-            src = wo_raw[:].rearrange("p t n -> p n t")
-            nc.scalar.copy(out=dst, in_=src[:, u * 256 : (u + 1) * 256])
-            nc.vector.quantize_mx(
-                out=wo_codes[:, u * 256 : (u + 1) * 256].bitcast(FP8X4),
-                scales=wo_plane[:, u * 256 : (u + 1) * 256],
-                in_=wo_bf[:],
+        def gate(s, t):
+            acc = psum.tile([P, HALF], F32, name=f"g{s}_{t}", tag="act", bufs=4)
+            for a in range(PASSES):
+                times_table(
+                    acc,
+                    wg_codes[:, a, t * 64 : (t + 1) * 64].bitcast(U8).bitcast(FP4X4),
+                    wg_plane[:, a, t * 32 : (t + 1) * 32].bitcast(U8),
+                    a, s, a == 0, a == PASSES - 1,
+                )
+            g = ring.tile([P, HALF], F32, name=f"gate{s}_{t}", tag="gate", bufs=8)
+            nc.scalar.activation(out=g[:], in_=acc[:], func=ACT.Sigmoid)
+            return g
+
+        def candidate(s, t, tag):
+            acc = product(wc_q, s, t, tag)
+            if (s, t) == (0, 2):
+                c = keep.tile([P, HALF], F32, name=f"cand{s}_{t}", tag="slot_wo", align_bytes=64)
+            else:
+                c = ring.tile([P, HALF], F32, name=f"cand{s}_{t}", tag="cand", bufs=7)
+            nc.scalar.activation(out=c[:], in_=acc[:], func=ACT.Tanh)
+            return c
+
+        tiles = [(s, t) for s in range(HALVES) for t in range(PACK)]
+        wc0_bf = keep.tile([P, ROWS], BF16, name="wc0_bf", align_bytes=64)
+        wc_q = [quantize_weight(raws[0], "wc0", wc0_bf[:], nc.scalar.copy)]
+        for c, slot in ((2, "slot_t0"), (3, "slot_wc0")):
+            windows[c] = keep.tile([P, T2], F32, name=f"window{c}", tag=slot, align_bytes=64)
+            nc.gpsimd.memset(windows[c][:], 0.0)
+        gates = {st: gate(*st) for st in tiles}
+        wc_q.append(quantize_weight(raws[1], "wc1", w_bf[:], nc.vector.tensor_copy))
+        cands = {st: candidate(*st, "act") for st in tiles[:6]}
+        wp_q = [quantize_weight(raws[2 + a], f"wp{a}", w_bf[:], nc.vector.tensor_copy) for a in range(PASSES)]
+
+        planes = [
+            keep.tile([P, PACK, HALF], BF16, name=f"h_planes{s}", tag=f"h_planes{s}", align_bytes=64) for s in range(HALVES)
+        ]
+        present = {}
+        diffs = {}
+
+        def difference(s, t):
+            diff = ring.tile([P, HALF], F32, name=f"diff{s}_{t}", tag="diff", bufs=3)
+            nc.vector.tensor_tensor(out=diff[:], in0=cands[s, t][:], in1=present[s, t][:], op=ALU.subtract)
+            diffs[s, t] = diff
+
+        def gated(s, t):
+            nc.vector.scalar_tensor_tensor(
+                out=planes[s][:, t, :], in0=gates[s, t][:], scalar=gain_sb[:, 4 * t : 4 * t + 1],
+                in1=diffs[s, t][:], op0=ALU.mult, op1=ALU.mult,
             )
 
+        def elementwise(steps):
+            for step in steps:
+                if step < len(tiles):
+                    difference(*tiles[step])
+                if step > 0:
+                    gated(*tiles[step - 1])
+
+        def interleave(s):
+            grouped = ring.tile([P, PACK * HALF], BF16, name=f"h_bf{s}", tag="h_bf", align_bytes=64)
+            dst = grouped[:].rearrange("p (n t) -> p n t", t=PACK)
+            src = planes[s][:].rearrange("p t n -> p n t")
+            for u in range(2):
+                nc.scalar.copy(out=dst[:, u * 256 : (u + 1) * 256], in_=src[:, u * 256 : (u + 1) * 256])
+            return grouped
+
+        def quantize(grouped, name):
+            codes = keep.tile([P, HALF], U32, name=name + "_codes", align_bytes=64)
+            plane = keep.tile([P, HALF], U8, name=name + "_plane", align_bytes=64)
+            for u in range(2):
+                nc.vector.quantize_mx(
+                    out=codes[:, u * 256 : (u + 1) * 256].bitcast(FP8X4),
+                    scales=plane[:, u * 256 : (u + 1) * 256],
+                    in_=grouped[:, u * 1024 : (u + 1) * 1024],
+                )
+            return codes, plane
+
         def new_state(h_q, s, c):
-            acc = psum.tile([P, HALF], F32, name=f"y{s}_{c}", tag="y", bufs=2)
+            acc = psum.tile([P, HALF], F32, name=f"y{s}_{c}", tag="act", bufs=4)
             cols = slice(c * P, (c + 1) * P)
             for a in range(PASSES):
                 times_table(
@@ -257,24 +250,17 @@ def tile_list_gated_node_update_kernel(
                 )
             nc.tensor.matmul_mx(
                 out=acc[:],
-                lhsT=wo_codes[:, cols].bitcast(FP8X4),
-                lhsT_scale=wo_plane[:, cols],
+                lhsT=wo_q[0][:, cols].bitcast(FP8X4),
+                lhsT_scale=wo_q[1][:, cols],
                 rhs=h_q[0][:].bitcast(FP8X4),
                 rhs_scale=h_q[1][:],
                 start=False,
                 stop=True,
             )
-            return acc
-
-        def evacuate(acc, s, c):
-            if (s, c) == (0, 0):
-                y = keep.tile([P, HALF], F32, name=f"y_sb{s}_{c}", tag="slot_g", align_bytes=64)
-            elif (s, c) == (0, 1):
-                y = keep.tile([P, HALF], F32, name=f"y_sb{s}_{c}", tag="slot_f", align_bytes=64)
-            elif (s, c) == (0, 2):
+            if (s, c) == (0, 2):
                 y = keep.tile([P, HALF], F32, name=f"y_sb{s}_{c}", tag="h_planes1", align_bytes=64)
             else:
-                y = ring.tile([P, HALF], F32, name=f"y_sb{s}_{c}", tag="y_sb", bufs=4)
+                y = ring.tile([P, HALF], F32, name=f"y_sb{s}_{c}", tag="gate", bufs=8)
             nc.scalar.copy(out=y[:], in_=acc[:])
             return y
 
@@ -286,19 +272,28 @@ def tile_list_gated_node_update_kernel(
                 op=ALU.mult,
             )
 
-        gated_difference(0, range(PACK + 1))
-        quantize_wo(0)
-        h0 = quantize_h(planes[0], 0)
-        quantize_wo(1)
-        y00 = evacuate(new_state(h0, 0, 0), 0, 0)
-        gated_difference(1, range(2))
-        acc01 = new_state(h0, 0, 1)
-        scatter(y00, 0, 0)
-        gated_difference(1, range(2, PACK + 1))
-        scatter(evacuate(acc01, 0, 1), 0, 1)
-        h1 = quantize_h(planes[1], 1)
-        for c in range(2, CHUNKS):
-            scatter(evacuate(new_state(h0, 0, c), 0, c), 0, c)
+        for t in range(PACK):
+            present[0, t] = product(wp_q, 0, t, "present")
+        elementwise(range(PACK))
+        for st in tiles[6:]:
+            cands[st] = candidate(*st, "present")
+        for t in range(PACK):
+            present[1, t] = product(wp_q, 1, t, "present")
+        wo_bf = keep.tile([P, PACK * N], BF16, name="wo_bf", tag="slot_wo", align_bytes=64)
+        nc.scalar.copy(
+            out=wo_bf[:].rearrange("p (n t) -> p n t", t=PACK), in_=wo_raw.rearrange("p (t n) -> p n t", t=PACK)
+        )
+        elementwise([PACK])
+        h_bf0 = interleave(0)
+        wo_q = quantize(wo_bf[:], "wo")
+        h0 = quantize(h_bf0[:], "h0")
+        ys = [new_state(h0, 0, c) for c in range(2)]
+        elementwise(range(PACK + 1, 2 * PACK + 1))
+        h_bf1 = interleave(1)
+        h1 = quantize(h_bf1[:], "h1")
+        ys.extend(new_state(h0, 0, c) for c in range(2, CHUNKS))
         for c in range(CHUNKS):
-            scatter(evacuate(new_state(h1, 1, c), 1, c), 1, c)
+            scatter(ys[c], 0, c)
+        for c in range(CHUNKS):
+            scatter(new_state(h1, 1, c), 1, c)
             nc.sync.dma_start(out=out[c * P : (c + 1) * P, :], in_=windows[c][:])

@@ -46,9 +46,10 @@ def tile_list_gated_node_update_kernel(
             src = raw.rearrange("p (j u t i) -> p t u i j", j=PACK, t=PACK, i=4)
             copy(out=dst[:, ts], in_=src[:, ts])
 
-        tab_plane = keep.tile([P, PASSES, T // 4], I32, name="tab_plane", tag="slot_plane", align_bytes=64)
-        nc.gpsimd.memset(tab_plane[:, 0, :], 0)
-        nc.vector.memset(tab_plane[:, 1, :], 0)
+        tab_plane = keep.tile([P, T // 4], I32, name="tab_plane", tag="slot_plane", align_bytes=64)
+        nc.vector.memset(tab_plane[:], 0)
+        moved_plane = keep.tile([P, S // 4], I32, name="moved_plane", align_bytes=64)
+        nc.gpsimd.memset(moved_plane[:], 0)
         wg_plane = keep.tile([P, PASSES, H // 4], I32, name="wg_plane", align_bytes=64)
         nc.gpsimd.memset(wg_plane[:], 0)
 
@@ -75,7 +76,9 @@ def tile_list_gated_node_update_kernel(
             return raw[:]
 
         table = [load_table(0, "slot_t0")]
-        load_scale_rows(nc.sync, tab_plane, tab_scales)
+        scale_words = tab_scales.bitcast(I32)
+        for q in range(4):
+            nc.sync.dma_start(out=tab_plane[32 * q : 32 * q + 8, :], in_=scale_words[:, 4 * q : 4 * q + 4, :])
         raws = [load_rows(wc, 0, "wc_raw0", "slot_wc0")]
         gain_sb = keep.tile([P, 16], F32, name="gain_sb", align_bytes=64)[:]
         gain_rows = gain.rearrange("(u x) -> u x", x=16)
@@ -95,33 +98,20 @@ def tile_list_gated_node_update_kernel(
             )
         table.append(load_table(1, "slot_t1"))
 
-        wo_raw = keep.tile([P, PACK * N], F32, name="wo_raw", align_bytes=64)[:]
-        wgo_sb = keep.tile([P, S], F32, name="wgo_sb", align_bytes=64)[:]
-        wr_codes = keep.tile([P, PASSES, N], I32, name="wr_codes", align_bytes=64)[:]
-        wr_plane = keep.tile([P, PASSES, N // 4], I32, name="wr_plane", align_bytes=64)[:]
-
-        nc.gpsimd.memset(wr_plane, 0)
-        raws.append(load_rows(wc, 1, "wc_raw1"))
-        raws.append(load_rows(wp, 0, "wp_raw0"))
-        raws.append(load_rows(wp, 1, "wp_raw1"))
-        wo_rows = wo.rearrange("(u t i) n -> i u t n", t=PACK, i=4)
-        for i in range(4):
-            nc.sync.dma_start(out=wo_raw[i:P:4, :].rearrange("p (t n) -> p t n", t=PACK), in_=wo_rows[i])
-        nc.sync.dma_start(out=wr_codes, in_=wr_words.rearrange("a p e i -> p a (e i)").bitcast(I32))
-        load_scale_rows(nc.sync, wr_plane, wr_scales)
-        nc.sync.dma_start(out=wgo_sb, in_=wgo)
-
-        windows = {c: keep.tile([P, T2], F32, name=f"window{c}") for c in range(2)}
-        nc.vector.memset(windows[0][:], 0.0)
-        nc.vector.memset(windows[1][:], 0.0)
+        windows = [keep.tile([P, T2], F32, name=f"window{c}") for c in range(CHUNKS)]
+        for c in range(CHUNKS):
+            (nc.vector if c < 2 else nc.gpsimd).memset(windows[c][:].bitcast(I32), 0)
 
         v_words = keep.tile([P, PASSES, S], U32, name="v_words", align_bytes=64)
         nc.vector.tensor_copy(out=v_words[:, 0, :], in_=table[0][:].bitcast(U32).indirect(idx[:]))
-        v_plane = []
-        for a in range(PASSES):
-            plane = keep.tile([P, S], U8, name=f"v_plane{a}", align_bytes=64)
-            nc.vector.tensor_copy(out=plane[:], in_=tab_plane[:, a, :].bitcast(U8).indirect(idx[:]))
-            v_plane.append(plane)
+        gathered_plane = keep.tile([P, S], U8, name="gathered_plane", align_bytes=64)
+        nc.vector.tensor_copy(out=gathered_plane[:], in_=tab_plane[:].bitcast(U8).indirect(idx[:]))
+        for q in range(4):
+            nc.sync.dma_start(
+                out=moved_plane[32 * q : 32 * q + 4, :], in_=gathered_plane[32 * q + 4 : 32 * q + 8, :].bitcast(I32)
+            )
+        v_plane = [gathered_plane[:], moved_plane[:].bitcast(U8)]
+        raws.append(load_rows(wc, 1, "wc_raw1", "slot_plane"))
         for s in range(HALVES):
             nc.vector.tensor_copy(
                 out=v_words[:, 1, s * HALF : (s + 1) * HALF],
@@ -185,15 +175,27 @@ def tile_list_gated_node_update_kernel(
             return c
 
         tiles = [(s, t) for s in range(HALVES) for t in range(PACK)]
-        wc0_bf = keep.tile([P, ROWS], BF16, name="wc0_bf", align_bytes=64)
+        wc0_bf = keep.tile([P, ROWS], BF16, name="wc0_bf", tag="slot_bf", align_bytes=64)
         wc_q = [quantize_weight(raws[0], "wc0", wc0_bf[:], nc.scalar.copy)]
-        for c, slot in ((2, "slot_t0"), (3, "slot_wc0")):
-            windows[c] = keep.tile([P, T2], F32, name=f"window{c}", tag=slot, align_bytes=64)
-            nc.gpsimd.memset(windows[c][:], 0.0)
+        raws.append(load_rows(wp, 0, "wp_raw0", "slot_wc0"))
+        raws.append(load_rows(wp, 1, "wp_raw1", "slot_bf"))
         gates = {st: gate(*st) for st in tiles}
         wc_q.append(quantize_weight(raws[1], "wc1", w_bf[:], nc.vector.tensor_copy))
+        wo_raw = keep.tile([P, PACK * N], F32, name="wo_raw", tag="slot_plane", align_bytes=64)[:]
+        wo_rows = wo.rearrange("(u t i) n -> i u t n", t=PACK, i=4)
+        for i in range(4):
+            nc.sync.dma_start(out=wo_raw[i:P:4, :].rearrange("p (t n) -> p t n", t=PACK), in_=wo_rows[i])
         cands = {st: candidate(*st, "act") for st in tiles[:6]}
-        wp_q = [quantize_weight(raws[2 + a], f"wp{a}", w_bf[:], nc.vector.tensor_copy) for a in range(PASSES)]
+        wp_q = [quantize_weight(raws[2], "wp0", w_bf[:], nc.vector.tensor_copy)]
+        wr_bytes = keep.tile([P, PASSES * (N + N // 4)], I32, name="wr_bytes", tag="slot_wc0", align_bytes=64)
+        wr_codes = wr_bytes[:, : PASSES * N].rearrange("p (a e) -> p a e", a=PASSES)
+        wr_plane = wr_bytes[:, PASSES * N :].rearrange("p (a w) -> p a w", a=PASSES)
+        nc.gpsimd.memset(wr_plane, 0)
+        nc.sync.dma_start(out=wr_codes, in_=wr_words.rearrange("a p e i -> p a (e i)").bitcast(I32))
+        load_scale_rows(nc.sync, wr_plane, wr_scales)
+        wp_q.append(quantize_weight(raws[3], "wp1", w_bf[:], nc.vector.tensor_copy))
+        wgo_sb = keep.tile([P, S], F32, name="wgo_sb", tag="slot_bf", align_bytes=64)[:]
+        nc.sync.dma_start(out=wgo_sb, in_=wgo)
 
         planes = [
             keep.tile([P, PACK, HALF], BF16, name=f"h_planes{s}", tag=f"h_planes{s}", align_bytes=64) for s in range(HALVES)

@@ -77,8 +77,9 @@ def tile_list_gated_node_update_kernel(
 
         table = [load_table(0, "slot_t0")]
         scale_words = tab_scales.bitcast(I32)
-        for q in range(4):
-            nc.sync.dma_start(out=tab_plane[32 * q : 32 * q + 8, :], in_=scale_words[:, 4 * q : 4 * q + 4, :])
+        nc.sync.dma_start(out=tab_plane[4:P:8, :], in_=scale_words[1])
+        for r in range(4):
+            nc.sync.dma_start(out=tab_plane[r:P:32, :], in_=scale_words[0, r:16:4, :])
         raws = [load_rows(wc, 0, "wc_raw0", "slot_wc0")]
         gain_sb = keep.tile([P, 16], F32, name="gain_sb", align_bytes=64)[:]
         gain_rows = gain.rearrange("(u x) -> u x", x=16)
@@ -106,10 +107,8 @@ def tile_list_gated_node_update_kernel(
         nc.vector.tensor_copy(out=v_words[:, 0, :], in_=table[0][:].bitcast(U32).indirect(idx[:]))
         gathered_plane = keep.tile([P, S], U8, name="gathered_plane", align_bytes=64)
         nc.vector.tensor_copy(out=gathered_plane[:], in_=tab_plane[:].bitcast(U8).indirect(idx[:]))
-        for q in range(4):
-            nc.sync.dma_start(
-                out=moved_plane[32 * q : 32 * q + 4, :], in_=gathered_plane[32 * q + 4 : 32 * q + 8, :].bitcast(I32)
-            )
+        for r in range(4):
+            nc.sync.dma_start(out=moved_plane[r:P:32, :], in_=gathered_plane[4 + 8 * r : P : 32, :].bitcast(I32))
         v_plane = [gathered_plane[:], moved_plane[:].bitcast(U8)]
         raws.append(load_rows(wc, 1, "wc_raw1", "slot_plane"))
         for s in range(HALVES):
@@ -153,7 +152,7 @@ def tile_list_gated_node_update_kernel(
             return acc
 
         def gate(s, t):
-            acc = psum.tile([P, HALF], F32, name=f"g{s}_{t}", tag="act", bufs=4)
+            acc = psum.tile([P, HALF], F32, name=f"g{s}_{t}", tag=("act", "present")[s], bufs=4)
             for a in range(PASSES):
                 times_table(
                     acc,
@@ -185,7 +184,7 @@ def tile_list_gated_node_update_kernel(
         wo_rows = wo.rearrange("(u t i) n -> i u t n", t=PACK, i=4)
         for i in range(4):
             nc.sync.dma_start(out=wo_raw[i:P:4, :].rearrange("p (t n) -> p t n", t=PACK), in_=wo_rows[i])
-        cands = {st: candidate(*st, "act") for st in tiles[:6]}
+        cands = {st: candidate(*st, "act") for st in tiles[:PACK]}
         wp_q = [quantize_weight(raws[2], "wp0", w_bf[:], nc.vector.tensor_copy)]
         wr_bytes = keep.tile([P, PASSES * (N + N // 4)], I32, name="wr_bytes", tag="slot_wc0", align_bytes=64)
         wr_codes = wr_bytes[:, : PASSES * N].rearrange("p (a e) -> p a e", a=PASSES)
@@ -222,7 +221,7 @@ def tile_list_gated_node_update_kernel(
                     gated(*tiles[step - 1])
 
         def interleave(s):
-            grouped = ring.tile([P, PACK * HALF], BF16, name=f"h_bf{s}", tag="h_bf", align_bytes=64)
+            grouped = keep.tile([P, PACK * HALF], BF16, name=f"h_bf{s}", tag=("h_bf0", "slot_y00")[s], align_bytes=64)
             dst = grouped[:].rearrange("p (n t) -> p n t", t=PACK)
             src = planes[s][:].rearrange("p t n -> p n t")
             for u in range(2):
@@ -259,7 +258,9 @@ def tile_list_gated_node_update_kernel(
                 start=False,
                 stop=True,
             )
-            if (s, c) == (0, 2):
+            if (s, c) == (0, 0):
+                y = keep.tile([P, HALF], F32, name=f"y_sb{s}_{c}", tag="slot_y00", align_bytes=64)
+            elif (s, c) == (0, 2):
                 y = keep.tile([P, HALF], F32, name=f"y_sb{s}_{c}", tag="h_planes1", align_bytes=64)
             else:
                 y = ring.tile([P, HALF], F32, name=f"y_sb{s}_{c}", tag="gate", bufs=8)
@@ -277,7 +278,7 @@ def tile_list_gated_node_update_kernel(
         for t in range(PACK):
             present[0, t] = product(wp_q, 0, t, "present")
         elementwise(range(PACK))
-        for st in tiles[6:]:
+        for st in tiles[PACK:]:
             cands[st] = candidate(*st, "present")
         for t in range(PACK):
             present[1, t] = product(wp_q, 1, t, "present")
@@ -291,10 +292,11 @@ def tile_list_gated_node_update_kernel(
         h0 = quantize(h_bf0[:], "h0")
         ys = [new_state(h0, 0, c) for c in range(2)]
         elementwise(range(PACK + 1, 2 * PACK + 1))
+        scatter(ys[0], 0, 0)
         h_bf1 = interleave(1)
         h1 = quantize(h_bf1[:], "h1")
         ys.extend(new_state(h0, 0, c) for c in range(2, CHUNKS))
-        for c in range(CHUNKS):
+        for c in range(1, CHUNKS):
             scatter(ys[c], 0, c)
         for c in range(CHUNKS):
             scatter(new_state(h1, 1, c), 1, c)

@@ -42,8 +42,8 @@ def tile_list_gated_node_update_kernel(
                 queue.dma_start(out=plane[r:P:32, :, :], in_=words[:, r:16:4, :].rearrange("a q w -> q a w"))
 
         def cast_permuted(copy, raw, grouped, ts):
-            dst = grouped.rearrange("p (t u i j) -> p t u i j", t=PACK, i=4, j=PACK)
-            src = raw.rearrange("p (j u t i) -> p t u i j", j=PACK, t=PACK, i=4)
+            dst = grouped.rearrange("p (t u i j) -> p t u j i", t=PACK, i=4, j=PACK)
+            src = raw.rearrange("p (j u t i) -> p t u j i", j=PACK, t=PACK, i=4)
             copy(out=dst[:, ts], in_=src[:, ts])
 
         tab_plane = keep.tile([P, T // 4], I32, name="tab_plane", tag="slot_plane", align_bytes=64)
@@ -222,10 +222,10 @@ def tile_list_gated_node_update_kernel(
 
         def interleave(s):
             grouped = keep.tile([P, PACK * HALF], BF16, name=f"h_bf{s}", tag=("h_bf0", "slot_y00")[s], align_bytes=64)
-            dst = grouped[:].rearrange("p (n t) -> p n t", t=PACK)
-            src = planes[s][:].rearrange("p t n -> p n t")
+            dst = grouped[:].rearrange("p (n i t) -> p n t i", i=4, t=PACK)
+            src = planes[s][:].rearrange("p t (n i) -> p n t i", i=4)
             for u in range(2):
-                nc.scalar.copy(out=dst[:, u * 256 : (u + 1) * 256], in_=src[:, u * 256 : (u + 1) * 256])
+                nc.scalar.copy(out=dst[:, u * 64 : (u + 1) * 64], in_=src[:, u * 64 : (u + 1) * 64])
             return grouped
 
         def quantize(grouped, name):
@@ -284,7 +284,8 @@ def tile_list_gated_node_update_kernel(
             present[1, t] = product(wp_q, 1, t, "present")
         wo_bf = keep.tile([P, PACK * N], BF16, name="wo_bf", tag="slot_wo", align_bytes=64)
         nc.scalar.copy(
-            out=wo_bf[:].rearrange("p (n t) -> p n t", t=PACK), in_=wo_raw.rearrange("p (t n) -> p n t", t=PACK)
+            out=wo_bf[:].rearrange("p (n i t) -> p n t i", i=4, t=PACK),
+            in_=wo_raw.rearrange("p (t n i) -> p n t i", t=PACK, i=4),
         )
         elementwise([PACK])
         h_bf0 = interleave(0)

@@ -1,6 +1,7 @@
 from contextlib import ExitStack
 
 import concourse.mybir as mybir
+from concourse.masks import make_identity
 
 K, T, S, H, N, T2 = 1024, 4096, 1024, 512, 512, 2048
 FLOPS = 2 * S * (3 * K * H + K * N + H * N)
@@ -24,6 +25,13 @@ HALF = 512
 HALVES = S // HALF
 CHUNKS = N // P
 COLS = HALF // 16
+BANK = 2048
+KB = 1024
+ROWS = PACK * H
+SCALE_ROWS = 16
+TOP = P - PASSES * SCALE_ROWS
+TAB_W, WG_W, WR_W = S // 4, H // 4, N // 4
+PLANE_W = TAB_W + WG_W + WR_W
 
 
 def tile_list_gated_node_update_kernel(
@@ -34,271 +42,324 @@ def tile_list_gated_node_update_kernel(
         lists = ctx.enter_context(tc.tile_pool(name="lists", bufs=1))
         keep = ctx.enter_context(tc.tile_pool(name="keep", bufs=1))
         ring = ctx.enter_context(tc.tile_pool(name="ring", bufs=2))
+        arena = ctx.enter_context(tc.tile_pool(name="arena", bufs=1))
         psum = ctx.enter_context(tc.psum_pool(name="psum", bufs=1))
 
-        def load_scale_rows(queue, plane, rows):
-            words = rows.bitcast(I32)
-            for r in range(4):
-                queue.dma_start(out=plane[r:P:32, :, :], in_=words[:, r:16:4, :].rearrange("a q w -> q a w"))
+        def placed(name, width, dtype, offset):
+            return arena.tile([P, width], dtype, name=name, offset=offset, align_bytes=64)
 
-        def cast_permuted(copy, raw, grouped, ts):
-            dst = grouped.rearrange("p (t u i j) -> p t u j i", t=PACK, i=4, j=PACK)
-            src = raw.rearrange("p (j u t i) -> p t u j i", j=PACK, t=PACK, i=4)
-            copy(out=dst[:, ts], in_=src[:, ts])
+        def scale_rows(scales):
+            return scales.bitcast(I32).rearrange("a q w -> (a q) w")
 
-        tab_plane = keep.tile([P, T // 4], I32, name="tab_plane", tag="slot_plane", align_bytes=64)
-        nc.vector.memset(tab_plane[:], 0)
-        moved_plane = keep.tile([P, S // 4], I32, name="moved_plane", align_bytes=64)
-        nc.gpsimd.memset(moved_plane[:], 0)
-        wg_plane = keep.tile([P, PASSES, H // 4], I32, name="wg_plane", align_bytes=64)
-        nc.gpsimd.memset(wg_plane[:], 0)
+        tab_rows = keep.tile([P, T // 4], I32, name="tab_rows", align_bytes=64)
+        nc.gpsimd.memset(tab_rows[0:TOP, :], 0)
+        wg_rows = keep.tile([P, WG_W], I32, name="wg_rows", align_bytes=64)
+        nc.gpsimd.memset(wg_rows[0:TOP, :], 0)
+        planes = [keep.tile([P, PLANE_W], I32, name=f"planes{a}", align_bytes=64) for a in range(PASSES)]
+        for a in range(PASSES):
+            nc.gpsimd.memset(planes[a][:], 0)
+        ident = keep.tile([P, P], F32, name="ident", align_bytes=64)
+        make_identity(nc, ident[:])
+
+        def zeroed_window(c, offset, engine):
+            window = placed(f"window{c}", T2, F32, offset)
+            engine.memset(window[:].bitcast(I32), 0)
+            return window
+
+
+        windows = [zeroed_window(0, 99 * KB, nc.gpsimd)]
 
         idx = lists.tile([P, S // 16], U16, name="idx")
         nc.sync.dma_start(idx[:], offs)
+        nc.sync.dma_start(out=tab_rows[TOP:P, :], in_=scale_rows(tab_scales))
+        nc.sync.dma_start(out=wg_rows[TOP:P, :], in_=scale_rows(wg_scales))
+        staged = keep.tile([P, PLANE_W], I32, name="staged", align_bytes=64)
+        nc.sync.dma_start(out=staged[TOP:P, TAB_W + WG_W :], in_=scale_rows(wr_scales))
         idx2 = lists.tile([P, S // 16], U16, name="idx2")
         nc.sync.dma_start(idx2[:], offs2)
-        wg_raw = keep.tile([P, PASSES, 2 * H // 4], I32, name="wg_raw", align_bytes=64)
-        nc.sync.dma_start(out=wg_raw[:], in_=wg_words.bitcast(I32).rearrange("a p w -> p a w"))
-        wg_plane_raw = keep.tile([P, PASSES, H // 4], I32, name="wg_plane_raw", align_bytes=64)
-        load_scale_rows(nc.sync, wg_plane_raw, wg_scales)
 
-        def load_table(a, slot):
-            words = keep.tile([P, T], I32, name=f"table{a}", tag=slot, align_bytes=64)
+        gain_sb = keep.tile([P, PACK], F32, name="gain_sb", align_bytes=64)
+        nc.sync.dma_start(out=gain_sb[:], in_=gain.rearrange("(p t) -> p t", t=PACK))
+
+        def load_table(a, offset):
+            words = placed(f"table{a}", T, I32, offset)
             nc.sync.dma_start(out=words[:], in_=tab_words[a].rearrange("p t i -> p (t i)").bitcast(I32))
             return words
 
-        ROWS = PACK * H
-
-        def load_rows(w, a, name, slot=None):
-            raw = keep.tile([P, ROWS], F32, name=name, tag=slot or name, align_bytes=64)
+        def load_rows(w, a, name, offset):
+            raw = placed(name, ROWS, F32, offset)
             rows = w[a * K_PASS : (a + 1) * K_PASS, :].rearrange("(p j) c -> p (j c)", j=PACK)
             nc.sync.dma_start(out=raw[:], in_=rows)
             return raw[:]
 
-        table = [load_table(0, "slot_t0")]
-        scale_words = tab_scales.bitcast(I32)
-        nc.sync.dma_start(out=tab_plane[4:P:8, :], in_=scale_words[1])
-        for r in range(4):
-            nc.sync.dma_start(out=tab_plane[r:P:32, :], in_=scale_words[0, r:16:4, :])
-        raws = [load_rows(wc, 0, "wc_raw0", "slot_wc0")]
-        gain_sb = keep.tile([P, 16], F32, name="gain_sb", align_bytes=64)[:]
-        gain_rows = gain.rearrange("(u x) -> u x", x=16)
-        for i in range(4):
-            nc.sync.dma_start(out=gain_sb[i:P:4, 0:13], in_=gain_rows[:, i : i + 13])
+        def halves(raw):
+            rows = raw.rearrange("p (j n i) -> p n j i", i=4, j=PACK)
+            return [rows[:, u * 64 : (u + 1) * 64] for u in range(2)]
 
-        wg_codes = keep.tile([P, PASSES, 2 * H // 4], I32, name="wg_codes", align_bytes=64)
+        def cast(copy, raw, grouped, u):
+            copy(out=grouped.rearrange("p (n i j) -> p n j i", i=4, j=PACK), in_=raw[u])
+
+        def mx_tiles(name, width, codes=None):
+            if codes is None:
+                codes = keep.tile([P, width], U32, name=name + "_codes", align_bytes=64)
+            return codes, keep.tile([P, width], U8, name=name + "_plane", align_bytes=64)
+
+        def quantize_part(tiles, grouped, u):
+            nc.vector.quantize_mx(
+                out=tiles[0][:, u * 256 : (u + 1) * 256].bitcast(FP8X4),
+                scales=tiles[1][:, u * 256 : (u + 1) * 256],
+                in_=grouped,
+            )
+
+        def quantize(grouped, name, width, codes=None):
+            tiles = mx_tiles(name, width, codes)
+            for u in range(width // 256):
+                quantize_part(tiles, grouped[:, u * 1024 : (u + 1) * 1024], u)
+            return tiles
+
+        def quantize_weight(raw, name, w_bf, codes=None):
+            for u in range(2):
+                cast(nc.vector.tensor_copy, raw, w_bf[:, u * 1024 : (u + 1) * 1024], u)
+            return quantize(w_bf, name, H, codes)
+
+        wg_raw = arena.tile([P, PASSES, 2 * H // 4], I32, name="wg_raw", offset=107 * KB, align_bytes=64)
+        nc.sync.dma_start(out=wg_raw[:], in_=wg_words.bitcast(I32).rearrange("a p w -> p a w"))
+        table = [load_table(0, 20 * KB)]
+
+        table.append(load_table(1, 0))
+
+        gathered = keep.tile([P, S], U8, name="gathered", align_bytes=64)
+        nc.vector.tensor_copy(out=gathered[:], in_=tab_rows[:].bitcast(U8).indirect(idx[:]))
         nc.vector.tensor_copy(
-            out=wg_codes[:].rearrange("p a (t u w) -> p a t u w", t=PACK, w=2),
-            in_=wg_raw[:].rearrange("p a (u t w) -> p a t u w", t=PACK, w=2),
+            out=staged[:, TAB_W : TAB_W + WG_W].bitcast(U8).rearrange("p (t m) -> p t m", t=PACK),
+            in_=wg_rows[:].bitcast(U8).rearrange("p (m t) -> p t m", t=PACK),
         )
-        for q in range(4):
-            rows = slice(32 * q, 32 * q + 4)
-            nc.vector.tensor_copy(
-                out=wg_plane[rows].rearrange("p a (t u) -> p a t u", t=PACK),
-                in_=wg_plane_raw[rows].rearrange("p a (u t) -> p a t u", t=PACK),
-            )
-        table.append(load_table(1, "slot_t1"))
+        nc.vector.tensor_copy(out=staged[TOP:P, 0:TAB_W], in_=gathered[TOP:P, :].bitcast(I32))
 
-        windows = [keep.tile([P, T2], F32, name=f"window{c}") for c in range(CHUNKS)]
-        for c in range(CHUNKS):
-            (nc.vector if c < 2 else nc.gpsimd).memset(windows[c][:].bitcast(I32), 0)
 
-        v_words = keep.tile([P, PASSES, S], U32, name="v_words", align_bytes=64)
-        nc.vector.tensor_copy(out=v_words[:, 0, :], in_=table[0][:].bitcast(U32).indirect(idx[:]))
-        gathered_plane = keep.tile([P, S], U8, name="gathered_plane", align_bytes=64)
-        nc.vector.tensor_copy(out=gathered_plane[:], in_=tab_plane[:].bitcast(U8).indirect(idx[:]))
-        for r in range(4):
-            nc.sync.dma_start(out=moved_plane[r:P:32, :], in_=gathered_plane[4 + 8 * r : P : 32, :].bitcast(I32))
-        v_plane = [gathered_plane[:], moved_plane[:].bitcast(U8)]
-        raws.append(load_rows(wc, 1, "wc_raw1", "slot_plane"))
+        def move_rows(a, queue):
+            first = TOP + SCALE_ROWS * a
+            for r in range(4):
+                queue.dma_start(out=planes[a][r:P:32, :], in_=staged[first + r : first + SCALE_ROWS : 4, :])
+
+        move_rows(0, nc.scalar)
+        move_rows(1, nc.sync)
+        raws = [halves(load_rows(wc, a, f"wc_raw{a}", (132 + 8 * a) * KB)) for a in range(PASSES)]
+        v_plane = [planes[a][:, 0:TAB_W].bitcast(U8) for a in range(PASSES)]
+        wg_plane = [planes[a][:, TAB_W : TAB_W + WG_W].bitcast(U8) for a in range(PASSES)]
+        wr_plane = [planes[a][:, TAB_W + WG_W :].bitcast(U8) for a in range(PASSES)]
+
+        half_gain = keep.tile([P, PACK], F32, name="half_gain", align_bytes=64)
+        nc.vector.tensor_scalar(out=half_gain[:], in0=gain_sb[:], scalar1=0.5, scalar2=0.0, op0=ALU.mult, op1=ALU.add)
+        v_words = {}
+
+        def gather_words(a, s, words):
+            nc.vector.tensor_copy(out=words[:], in_=table[a][:].bitcast(U32).indirect(idx[:, s * COLS : (s + 1) * COLS]))
+            v_words[a, s] = words
+
+        def picked(a, entries):
+            s = entries.start // HALF
+            return v_words[a, s][:, entries.start - s * HALF : entries.stop - s * HALF].bitcast(FP8X4)
+
         for s in range(HALVES):
-            nc.vector.tensor_copy(
-                out=v_words[:, 1, s * HALF : (s + 1) * HALF],
-                in_=table[1][:].bitcast(U32).indirect(idx[:, s * COLS : (s + 1) * COLS]),
-            )
+            gather_words(0, s, keep.tile([P, HALF], U32, name=f"v_words0{s}", align_bytes=64))
+        raws.extend(halves(load_rows(wp, a, f"wp_raw{a}", (20 + 8 * a) * KB)) for a in range(PASSES))
+        wg_codes = keep.tile([P, PASSES, 2 * H], U8, name="wg_codes", align_bytes=64)
+        nc.vector.tensor_copy(
+            out=wg_codes[:].bitcast(U16).rearrange("p a (t n i) -> p a n t i", t=PACK, i=8),
+            in_=wg_raw[:].bitcast(U16).rearrange("p a (n i t) -> p a n t i", t=PACK, i=8),
+        )
+        windows.append(zeroed_window(1, 107 * KB, nc.vector))
+        for s in range(HALVES):
+            gather_words(1, s, keep.tile([P, HALF], U32, name=f"v_words1{s}", align_bytes=64))
 
-        def times_table(acc, lhsT, lhsT_scale, a, s, start, stop):
+        def times_table(acc, lhsT, lhsT_scale, a, entries, start, stop):
             nc.tensor.matmul_mx(
-                out=acc[:],
+                out=acc,
                 lhsT=lhsT,
                 lhsT_scale=lhsT_scale,
-                rhs=v_words[:, a, s * HALF : (s + 1) * HALF].bitcast(FP8X4),
-                rhs_scale=v_plane[a][:, s * HALF : (s + 1) * HALF],
+                rhs=picked(a, entries),
+                rhs_scale=v_plane[a][:, entries],
                 start=start,
                 stop=stop,
             )
 
-        w_bf = keep.tile([P, ROWS], BF16, name="w_bf", tag="slot_t1", align_bytes=64)
+        def bank_tile(name, bank):
+            return psum.tile([P, HALF], F32, name=name, offset=bank * BANK)
 
-        def quantize_weight(raw, name, grouped, copy):
-            codes = keep.tile([P, H], U32, name=name + "_codes", align_bytes=64)
-            plane = keep.tile([P, H], U8, name=name + "_plane", align_bytes=64)
-            for u in range(2):
-                cast_permuted(copy, raw, grouped, slice(2 * u, 2 * u + 2))
-            for u in range(2):
-                nc.vector.quantize_mx(
-                    out=codes[:, u * 256 : (u + 1) * 256].bitcast(FP8X4),
-                    scales=plane[:, u * 256 : (u + 1) * 256],
-                    in_=grouped[:, u * 1024 : (u + 1) * 1024],
-                )
-            return codes, plane
-
-        def product(quantized, s, t, tag):
-            acc = psum.tile([P, HALF], F32, name=f"{tag}{s}_{t}", tag=tag, bufs=4)
-            cols = slice(t * P, (t + 1) * P)
+        def product(quantized, b, name, bank):
+            acc = bank_tile(f"{name}{b}", bank)
+            cols = slice(b * P, (b + 1) * P)
             for a in range(PASSES):
                 codes, plane = quantized[a]
-                times_table(acc, codes[:, cols].bitcast(FP8X4), plane[:, cols], a, s, a == 0, a == PASSES - 1)
+                nc.tensor.matmul_mx(
+                    out=acc[:],
+                    lhsT=picked(a, cols),
+                    lhsT_scale=v_plane[a][:, cols],
+                    rhs=codes[:].bitcast(FP8X4),
+                    rhs_scale=plane[:],
+                    start=a == 0,
+                    stop=a == PASSES - 1,
+                )
             return acc
 
-        def gate(s, t):
-            acc = psum.tile([P, HALF], F32, name=f"g{s}_{t}", tag=("act", "present")[s], bufs=4)
+        def gate(s, t, bank, g):
+            acc = bank_tile(f"g{s}_{t}", bank)
             for a in range(PASSES):
                 times_table(
-                    acc,
-                    wg_codes[:, a, t * 64 : (t + 1) * 64].bitcast(U8).bitcast(FP4X4),
-                    wg_plane[:, a, t * 32 : (t + 1) * 32].bitcast(U8),
-                    a, s, a == 0, a == PASSES - 1,
+                    acc[:],
+                    wg_codes[:, a, t * 2 * P : (t + 1) * 2 * P].bitcast(FP4X4),
+                    wg_plane[a][:, t * P : (t + 1) * P],
+                    a, slice(s * HALF, (s + 1) * HALF), a == 0, a == PASSES - 1,
                 )
-            g = ring.tile([P, HALF], F32, name=f"gate{s}_{t}", tag="gate", bufs=8)
-            nc.scalar.activation(out=g[:], in_=acc[:], func=ACT.Sigmoid)
+            nc.scalar.activation(out=g, in_=acc[:], func=ACT.Tanh, scale=0.5)
             return g
 
-        def candidate(s, t, tag):
-            acc = product(wc_q, s, t, tag)
-            if (s, t) == (0, 2):
-                c = keep.tile([P, HALF], F32, name=f"cand{s}_{t}", tag="slot_wo", align_bytes=64)
-            else:
-                c = ring.tile([P, HALF], F32, name=f"cand{s}_{t}", tag="cand", bufs=7)
-            nc.scalar.activation(out=c[:], in_=acc[:], func=ACT.Tanh)
+        def scale_gates(gates, scaled, lo, hi):
+            for t in range(PACK):
+                nc.scalar.activation(
+                    out=scaled[:].rearrange("p (n t i) -> p n t i", t=PACK, i=4)[:, :, t, :],
+                    in_=gates[t][:, lo:hi].rearrange("p (n i) -> p n i", i=4),
+                    func=ACT.Identity,
+                    scale=half_gain[:, t : t + 1],
+                    bias=half_gain[:, t : t + 1],
+                )
+
+        def leave_dealt(dst, acc, func, scale):
+            nc.scalar.activation(
+                out=dst.rearrange("p (t m) -> p t m", t=PACK),
+                in_=acc[:].rearrange("p (m t) -> p t m", t=PACK),
+                func=func,
+                scale=scale,
+            )
+
+        def candidate(b, bank, c):
+            leave_dealt(c, product(wc_q, b, "c", bank), ACT.Tanh, 1.0)
             return c
 
-        tiles = [(s, t) for s in range(HALVES) for t in range(PACK)]
-        wc0_bf = keep.tile([P, ROWS], BF16, name="wc0_bf", tag="slot_bf", align_bytes=64)
-        wc_q = [quantize_weight(raws[0], "wc0", wc0_bf[:], nc.scalar.copy)]
-        raws.append(load_rows(wp, 0, "wp_raw0", "slot_wc0"))
-        raws.append(load_rows(wp, 1, "wp_raw1", "slot_bf"))
-        gates = {st: gate(*st) for st in tiles}
-        wc_q.append(quantize_weight(raws[1], "wc1", w_bf[:], nc.vector.tensor_copy))
-        wo_raw = keep.tile([P, PACK * N], F32, name="wo_raw", tag="slot_plane", align_bytes=64)[:]
-        wo_rows = wo.rearrange("(u t i) n -> i u t n", t=PACK, i=4)
-        for i in range(4):
-            nc.sync.dma_start(out=wo_raw[i:P:4, :].rearrange("p (t n) -> p t n", t=PACK), in_=wo_rows[i])
-        cands = {st: candidate(*st, "act") for st in tiles[:PACK]}
-        wp_q = [quantize_weight(raws[2], "wp0", w_bf[:], nc.vector.tensor_copy)]
-        wr_bytes = keep.tile([P, PASSES * (N + N // 4)], I32, name="wr_bytes", tag="slot_wc0", align_bytes=64)
-        wr_codes = wr_bytes[:, : PASSES * N].rearrange("p (a e) -> p a e", a=PASSES)
-        wr_plane = wr_bytes[:, PASSES * N :].rearrange("p (a w) -> p a w", a=PASSES)
-        nc.gpsimd.memset(wr_plane, 0)
-        nc.sync.dma_start(out=wr_codes, in_=wr_words.rearrange("a p e i -> p a (e i)").bitcast(I32))
-        load_scale_rows(nc.sync, wr_plane, wr_scales)
-        wp_q.append(quantize_weight(raws[3], "wp1", w_bf[:], nc.vector.tensor_copy))
-        wgo_sb = keep.tile([P, S], F32, name="wgo_sb", tag="slot_bf", align_bytes=64)[:]
-        nc.sync.dma_start(out=wgo_sb, in_=wgo)
-
-        planes = [
-            keep.tile([P, PACK, HALF], BF16, name=f"h_planes{s}", tag=f"h_planes{s}", align_bytes=64) for s in range(HALVES)
-        ]
-        present = {}
-        diffs = {}
-
-        def difference(s, t):
-            diff = ring.tile([P, HALF], F32, name=f"diff{s}_{t}", tag="diff", bufs=3)
-            nc.vector.tensor_tensor(out=diff[:], in0=cands[s, t][:], in1=present[s, t][:], op=ALU.subtract)
-            diffs[s, t] = diff
-
-        def gated(s, t):
-            nc.vector.scalar_tensor_tensor(
-                out=planes[s][:, t, :], in0=gates[s, t][:], scalar=gain_sb[:, 4 * t : 4 * t + 1],
-                in1=diffs[s, t][:], op0=ALU.mult, op1=ALU.mult,
-            )
-
-        def elementwise(steps):
-            for step in steps:
-                if step < len(tiles):
-                    difference(*tiles[step])
-                if step > 0:
-                    gated(*tiles[step - 1])
-
-        def interleave(s):
-            grouped = keep.tile([P, PACK * HALF], BF16, name=f"h_bf{s}", tag=("h_bf0", "slot_y00")[s], align_bytes=64)
-            dst = grouped[:].rearrange("p (n i t) -> p n t i", i=4, t=PACK)
-            src = planes[s][:].rearrange("p t (n i) -> p n t i", i=4)
-            for u in range(2):
-                nc.scalar.copy(out=dst[:, u * 64 : (u + 1) * 64], in_=src[:, u * 64 : (u + 1) * 64])
-            return grouped
-
-        def quantize(grouped, name):
-            codes = keep.tile([P, HALF], U32, name=name + "_codes", align_bytes=64)
-            plane = keep.tile([P, HALF], U8, name=name + "_plane", align_bytes=64)
-            for u in range(2):
-                nc.vector.quantize_mx(
-                    out=codes[:, u * 256 : (u + 1) * 256].bitcast(FP8X4),
-                    scales=plane[:, u * 256 : (u + 1) * 256],
-                    in_=grouped[:, u * 1024 : (u + 1) * 1024],
+        def turn(diff, rows, opens):
+            for t in range(PACK):
+                cols = slice(t * P, (t + 1) * P)
+                nc.tensor.matmul(
+                    out=diff[:, cols], lhsT=rows[:, cols], rhs=ident[:], is_transpose=True,
+                    start=opens and t == 0, stop=not opens and t == PACK - 1,
                 )
-            return codes, plane
 
-        def new_state(h_q, s, c):
-            acc = psum.tile([P, HALF], F32, name=f"y{s}_{c}", tag="act", bufs=4)
-            cols = slice(c * P, (c + 1) * P)
-            for a in range(PASSES):
-                times_table(
-                    acc,
-                    wr_codes[:, a, cols].bitcast(FP8X4),
-                    wr_plane[:, a, c * 32 : (c + 1) * 32].bitcast(U8),
-                    a, s, a == 0, False,
-                )
-            nc.tensor.matmul_mx(
-                out=acc[:],
-                lhsT=wo_q[0][:, cols].bitcast(FP8X4),
-                lhsT_scale=wo_q[1][:, cols],
-                rhs=h_q[0][:].bitcast(FP8X4),
-                rhs_scale=h_q[1][:],
-                start=False,
-                stop=True,
-            )
-            if (s, c) == (0, 0):
-                y = keep.tile([P, HALF], F32, name=f"y_sb{s}_{c}", tag="slot_y00", align_bytes=64)
-            elif (s, c) == (0, 2):
-                y = keep.tile([P, HALF], F32, name=f"y_sb{s}_{c}", tag="h_planes1", align_bytes=64)
-            else:
-                y = ring.tile([P, HALF], F32, name=f"y_sb{s}_{c}", tag="gate", bufs=8)
-            nc.scalar.copy(out=y[:], in_=acc[:])
-            return y
+        def open_difference(c, b, bank):
+            diff = bank_tile(f"diff{b}", bank)
+            turn(diff, c, True)
+            return diff
 
-        def scatter(y, s, c):
+        def close_difference(diff, acc, neg):
+            leave_dealt(neg, acc, ACT.Copy, -1.0)
+            turn(diff, neg, False)
+            return diff
+
+        def gated(diff, scaled, h_bf, k):
+            cols = slice(k * HALF, (k + 1) * HALF)
             nc.vector.tensor_tensor(
-                out=windows[c][:].indirect(idx2[:, s * COLS : (s + 1) * COLS]),
-                in0=y[:],
-                in1=wgo_sb[:, s * HALF : (s + 1) * HALF],
+                out=h_bf[:, cols].rearrange("p (n i t) -> p n t i", i=4, t=PACK),
+                in0=diff[:].rearrange("p (t n i) -> p n t i", t=PACK, i=4),
+                in1=scaled.rearrange("p (n t i) -> p n t i", t=PACK, i=4),
                 op=ALU.mult,
             )
 
-        for t in range(PACK):
-            present[0, t] = product(wp_q, 0, t, "present")
-        elementwise(range(PACK))
-        for st in tiles[PACK:]:
-            cands[st] = candidate(*st, "present")
-        for t in range(PACK):
-            present[1, t] = product(wp_q, 1, t, "present")
-        wo_bf = keep.tile([P, PACK * N], BF16, name="wo_bf", tag="slot_wo", align_bytes=64)
-        nc.scalar.copy(
-            out=wo_bf[:].rearrange("p (n i t) -> p n t i", i=4, t=PACK),
-            in_=wo_raw.rearrange("p (t n i) -> p n t i", t=PACK, i=4),
+        early = keep.tile([P, PACK * HALF], F32, name="early", align_bytes=64)
+        gates = [[gate(0, t, t, early[:, t * HALF : (t + 1) * HALF]) for t in range(PACK)]]
+        scaled0 = placed("scaled0", PACK * HALF, F32, 72 * KB)
+        scale_gates(gates[0], scaled0, 0, HALF)
+        w_bf = placed("w_bf", ROWS, BF16, 8 * KB)
+        wc_q = [quantize_weight(raws[0], "wc0", w_bf)]
+        wo_raw = halves(load_rows(wo, 0, "wo_raw", 132 * KB))
+        wc_q.append(quantize_weight(raws[1], "wc1", w_bf))
+        cands = placed("cands", PACK * H, F32, 88 * KB)
+        diffs = [open_difference(candidate(b, b, cands[:, b * H : (b + 1) * H]), b, PACK + b) for b in range(PACK)]
+        wp_q = [quantize_weight(raws[2], "wp0", w_bf)]
+        wr_codes = placed("wr_codes", PASSES * N, I32, 140 * KB)
+        nc.sync.dma_start(
+            out=wr_codes[:].rearrange("p (a e) -> p a e", a=PASSES),
+            in_=wr_words.rearrange("a p e i -> p a (e i)").bitcast(I32),
         )
-        elementwise([PACK])
-        h_bf0 = interleave(0)
-        wo_q = quantize(wo_bf[:], "wo")
-        h0 = quantize(h_bf0[:], "h0")
-        ys = [new_state(h0, 0, c) for c in range(2)]
-        elementwise(range(PACK + 1, 2 * PACK + 1))
-        scatter(ys[0], 0, 0)
-        h_bf1 = interleave(1)
-        h1 = quantize(h_bf1[:], "h1")
-        ys.extend(new_state(h0, 0, c) for c in range(2, CHUNKS))
-        for c in range(1, CHUNKS):
-            scatter(ys[c], 0, c)
+        wgo_sb = placed("wgo_sb", S, F32, 144 * KB)
+        nc.sync.dma_start(out=wgo_sb[:], in_=wgo)
+        wp1_codes = placed("wp1_codes", H, U32, 88 * KB)
+        wp_q.append(quantize_weight(raws[3], "wp1", w_bf, wp1_codes))
+
+        def new_state(h_q, s, c, bank, lo=0, hi=HALF):
+            acc = bank_tile(f"y{s}_{c}_{lo}", bank)[:, lo:hi]
+            for a in range(PASSES):
+                times_table(
+                    acc,
+                    wr_codes[:, a * N + c * P : a * N + (c + 1) * P].bitcast(FP8X4),
+                    wr_plane[a][:, c * P : (c + 1) * P],
+                    a, slice(s * HALF + lo, s * HALF + hi), a == 0, False,
+                )
+            codes, plane = wo_q[c // 2]
+            cols = slice((c % 2) * P, (c % 2 + 1) * P)
+            nc.tensor.matmul_mx(
+                out=acc,
+                lhsT=codes[:, cols].bitcast(FP8X4),
+                lhsT_scale=plane[:, cols],
+                rhs=h_q[0][:, lo:hi].bitcast(FP8X4),
+                rhs_scale=h_q[1][:, lo:hi],
+                start=False,
+                stop=True,
+            )
+            if (s, c) == (0, CHUNKS - 1):
+                y = placed(f"y_sb{s}_{c}", HALF, F32, 64 * KB)
+            elif (s, c, lo) == (0, 0, 0):
+                y = placed(f"y_sb{s}_{c}", HALF, F32, 72 * KB)
+            elif (s, c) == (0, 0):
+                y = placed(f"y_sb{s}_{c}_{lo}", HALF, F32, 123 * KB)
+            else:
+                y = ring.tile([P, HALF], F32, name=f"y_sb{s}_{c}_{lo}", tag="y", bufs=4)
+            nc.scalar.copy(out=y[:, lo:hi], in_=acc)
+            return y
+
+        def scatter(y, s, c, lo=0, hi=HALF):
+            lo_all, hi_all = s * HALF + lo, s * HALF + hi
+            nc.vector.tensor_tensor(
+                out=windows[c][:].indirect(idx2[:, lo_all // 16 : hi_all // 16]),
+                in0=y[:, lo:hi],
+                in1=wgo_sb[:, lo_all:hi_all],
+                op=ALU.mult,
+            )
+
+        present = [product(wp_q, b, "p", b) for b in range(PACK)]
+        wo_bf0 = placed("wo_bf0", PACK * 256, BF16, 8 * KB)
+        cast(nc.vector.tensor_copy, wo_raw, wo_bf0[:], 0)
+        wo_q = [quantize(wo_bf0, "wo0", 256)]
+        h_bf0 = placed("h_bf0", PACK * HALF, BF16, 62 * KB)
+        for b in range(PACK):
+            if b == PACK - 1:
+                neg = placed(f"neg{b}", H, F32, 123 * KB)
+            else:
+                neg = ring.tile([P, H], F32, name=f"neg{b}", tag="neg", bufs=3)
+            gated(close_difference(diffs[b], present[b], neg[:]), scaled0[:, b * HALF : (b + 1) * HALF], h_bf0, b)
+        wo_bf1 = placed("wo_bf1", PACK * 256, BF16, 123 * KB)
+        cast(nc.scalar.copy, wo_raw, wo_bf1[:], 1)
+        wo_q.append(quantize(wo_bf1, "wo1", 256))
+        h0 = quantize(h_bf0, "h0", HALF)
+        first = [new_state(h0, 0, 0, (4, 7)[u], u * 256, (u + 1) * 256) for u in range(2)]
+        ys = [new_state(h0, 0, c, 7 - c) for c in range(1, CHUNKS - 1)]
+        for u in range(2):
+            scatter(first[u], 0, 0, u * 256, (u + 1) * 256)
+        windows.extend(zeroed_window(c, (116 + 8 * (c - 2)) * KB, nc.gpsimd) for c in range(2, CHUNKS))
+        for c in range(1, CHUNKS - 1):
+            scatter(ys[c - 1], 0, c)
+
+        held = placed("held", 3 * PACK * H, F32, 40 * KB)
+        parts = [held[:, j * H : (j + 1) * H] for j in range(3 * PACK)]
+        gates.append([gate(1, t, t, parts[2 * PACK + t]) for t in range(PACK)])
+        scaled1 = placed("scaled1", PACK * HALF, F32, 64 * KB)
+        scale_gates(gates[1], scaled1, 0, HALF)
+        diffs = [open_difference(candidate(PACK + k, (4, 7, 6, 5)[k], parts[k]), PACK + k, (4, 7, 6, 5)[k]) for k in range(PACK)]
+        present = [product(wp_q, PACK + k, "p", k) for k in range(PACK)]
+        h_bf1 = keep.tile([P, PACK * HALF], BF16, name="h_bf1", align_bytes=64)
+        for k in range(PACK):
+            gated(close_difference(diffs[k], present[k], parts[PACK + k]), scaled1[:, k * HALF : (k + 1) * HALF], h_bf1, k)
+        h1 = quantize(h_bf1, "h1", HALF)
+        scatter(new_state(h0, 0, CHUNKS - 1, 0), 0, CHUNKS - 1)
         for c in range(CHUNKS):
-            scatter(new_state(h1, 1, c), 1, c)
+            scatter(new_state(h1, 1, c, (1, 2, 3, 0)[c]), 1, c)
             nc.sync.dma_start(out=out[c * P : (c + 1) * P, :], in_=windows[c][:])

@@ -29,7 +29,7 @@ BANK = 2048
 KB = 1024
 ROWS = PACK * H
 SCALE_ROWS = 16
-TOP = P - PASSES * SCALE_ROWS
+TOP = P - SCALE_ROWS
 TAB_W, WG_W, WR_W = S // 4, H // 4, N // 4
 PLANE_W = TAB_W + WG_W + WR_W
 
@@ -49,15 +49,15 @@ def tile_list_gated_node_update_kernel(
             return arena.tile([P, width], dtype, name=name, offset=offset, align_bytes=64)
 
         def scale_rows(scales):
-            return scales.bitcast(I32).rearrange("a q w -> (a q) w")
+            return scales.bitcast(I32).rearrange("a q w -> q a w")
 
-        tab_rows = keep.tile([P, T // 4], I32, name="tab_rows", align_bytes=64)
-        nc.gpsimd.memset(tab_rows[0:TOP, :], 0)
-        wg_rows = keep.tile([P, WG_W], I32, name="wg_rows", align_bytes=64)
-        nc.gpsimd.memset(wg_rows[0:TOP, :], 0)
-        planes = [keep.tile([P, PLANE_W], I32, name=f"planes{a}", align_bytes=64) for a in range(PASSES)]
+        tab_rows = [placed(f"tab_rows{a}", T // 4, I32, (16, 80)[a] * KB) for a in range(PASSES)]
         for a in range(PASSES):
-            nc.gpsimd.memset(planes[a][:], 0)
+            nc.gpsimd.memset(tab_rows[a][0:TOP, :], 0)
+        wg_rows = placed("wg_rows", PASSES * WG_W, I32, 84 * KB)
+        nc.gpsimd.memset(wg_rows[0:TOP, :], 0)
+        planes = keep.tile([P, PASSES * PLANE_W], I32, name="planes", align_bytes=64)
+        nc.gpsimd.memset(planes[:], 0)
         ident = keep.tile([P, P], F32, name="ident", align_bytes=64)
         make_identity(nc, ident[:])
 
@@ -67,19 +67,12 @@ def tile_list_gated_node_update_kernel(
             return window
 
 
-        windows = [zeroed_window(0, 99 * KB, nc.gpsimd)]
+        windows = [zeroed_window(0, 99 * KB, nc.vector), zeroed_window(1, 107 * KB, nc.gpsimd)]
 
         idx = lists.tile([P, S // 16], U16, name="idx")
         nc.sync.dma_start(idx[:], offs)
-        nc.sync.dma_start(out=tab_rows[TOP:P, :], in_=scale_rows(tab_scales))
-        nc.sync.dma_start(out=wg_rows[TOP:P, :], in_=scale_rows(wg_scales))
-        staged = keep.tile([P, PLANE_W], I32, name="staged", align_bytes=64)
-        nc.sync.dma_start(out=staged[TOP:P, TAB_W + WG_W :], in_=scale_rows(wr_scales))
-        idx2 = lists.tile([P, S // 16], U16, name="idx2")
-        nc.sync.dma_start(idx2[:], offs2)
-
-        gain_sb = keep.tile([P, PACK], F32, name="gain_sb", align_bytes=64)
-        nc.sync.dma_start(out=gain_sb[:], in_=gain.rearrange("(p t) -> p t", t=PACK))
+        for a in range(PASSES):
+            nc.sync.dma_start(out=tab_rows[a][TOP:P, :], in_=tab_scales[a].bitcast(I32))
 
         def load_table(a, offset):
             words = placed(f"table{a}", T, I32, offset)
@@ -95,6 +88,17 @@ def tile_list_gated_node_update_kernel(
         def halves(raw):
             rows = raw.rearrange("p (j n i) -> p n j i", i=4, j=PACK)
             return [rows[:, u * 64 : (u + 1) * 64] for u in range(2)]
+
+        def load_halves(w, a, name, offset):
+            rows = w[a * K_PASS : (a + 1) * K_PASS, :].rearrange("(p j) c -> p j c", j=PACK)
+            parts = []
+            for u in range(2):
+                raw = placed(f"{name}_{u}", ROWS // 2, F32, offset + u * 4 * KB)
+                nc.sync.dma_start(
+                    out=raw[:].rearrange("p (j c) -> p j c", j=PACK), in_=rows[:, :, u * 256 : (u + 1) * 256]
+                )
+                parts.append(raw[:].rearrange("p (j n i) -> p n j i", i=4, j=PACK))
+            return parts
 
         def cast(copy, raw, grouped, u):
             copy(out=grouped.rearrange("p (n i j) -> p n j i", i=4, j=PACK), in_=raw[u])
@@ -122,32 +126,41 @@ def tile_list_gated_node_update_kernel(
                 cast(nc.vector.tensor_copy, raw, w_bf[:, u * 1024 : (u + 1) * 1024], u)
             return quantize(w_bf, name, H, codes)
 
-        wg_raw = arena.tile([P, PASSES, 2 * H // 4], I32, name="wg_raw", offset=107 * KB, align_bytes=64)
-        nc.sync.dma_start(out=wg_raw[:], in_=wg_words.bitcast(I32).rearrange("a p w -> p a w"))
+        nc.sync.dma_start(out=wg_rows[TOP:P, :].rearrange("q (a w) -> q a w", a=PASSES), in_=scale_rows(wg_scales))
+        staged = keep.tile([P, PASSES * PLANE_W], I32, name="staged", align_bytes=64)
+        by_pass = staged[:].rearrange("p (a w) -> p a w", a=PASSES)
+        nc.sync.dma_start(out=by_pass[TOP:P, :, TAB_W + WG_W :], in_=scale_rows(wr_scales))
         table = [load_table(0, 20 * KB)]
-
+        wg_raw = keep.tile([P, PASSES, 2 * H // 4], I32, name="wg_raw", align_bytes=64)
+        nc.sync.dma_start(out=wg_raw[:], in_=wg_words.bitcast(I32).rearrange("a p w -> p a w"))
         table.append(load_table(1, 0))
+        idx2 = lists.tile([P, S // 16], U16, name="idx2")
+        nc.sync.dma_start(idx2[:], offs2)
+        gain_sb = keep.tile([P, PACK], F32, name="gain_sb", align_bytes=64)
+        nc.sync.dma_start(out=gain_sb[:], in_=gain.rearrange("(p t) -> p t", t=PACK))
 
-        gathered = keep.tile([P, S], U8, name="gathered", align_bytes=64)
-        nc.vector.tensor_copy(out=gathered[:], in_=tab_rows[:].bitcast(U8).indirect(idx[:]))
+        gathered = placed("gathered", PASSES * S, U8, 139 * KB)
+        for a in range(PASSES):
+            nc.vector.tensor_copy(out=gathered[:, a * S : (a + 1) * S], in_=tab_rows[a][:].bitcast(U8).indirect(idx[:]))
+        for a in range(PASSES):
+            first = a * PLANE_W + TAB_W
+            nc.vector.tensor_copy(
+                out=staged[:, first : first + WG_W].bitcast(U8).rearrange("p (t m) -> p t m", t=PACK),
+                in_=wg_rows[:, a * WG_W : (a + 1) * WG_W].bitcast(U8).rearrange("p (m t) -> p t m", t=PACK),
+            )
         nc.vector.tensor_copy(
-            out=staged[:, TAB_W : TAB_W + WG_W].bitcast(U8).rearrange("p (t m) -> p t m", t=PACK),
-            in_=wg_rows[:].bitcast(U8).rearrange("p (m t) -> p t m", t=PACK),
+            out=by_pass[96:P, :, 0:TAB_W], in_=gathered[96:P, :].bitcast(I32).rearrange("p (a w) -> p a w", a=PASSES)
         )
-        nc.vector.tensor_copy(out=staged[TOP:P, 0:TAB_W], in_=gathered[TOP:P, :].bitcast(I32))
-
-
-        def move_rows(a, queue):
-            first = TOP + SCALE_ROWS * a
-            for r in range(4):
-                queue.dma_start(out=planes[a][r:P:32, :], in_=staged[first + r : first + SCALE_ROWS : 4, :])
-
-        move_rows(0, nc.scalar)
-        move_rows(1, nc.sync)
+        for r in range(4):
+            nc.sync.dma_start(out=planes[r:P:32, :], in_=staged[TOP + r : P : 4, :])
         raws = [halves(load_rows(wc, a, f"wc_raw{a}", (132 + 8 * a) * KB)) for a in range(PASSES)]
-        v_plane = [planes[a][:, 0:TAB_W].bitcast(U8) for a in range(PASSES)]
-        wg_plane = [planes[a][:, TAB_W : TAB_W + WG_W].bitcast(U8) for a in range(PASSES)]
-        wr_plane = [planes[a][:, TAB_W + WG_W :].bitcast(U8) for a in range(PASSES)]
+
+        def plane_of(a, lo, hi):
+            return planes[:, a * PLANE_W + lo : a * PLANE_W + hi].bitcast(U8)
+
+        v_plane = [plane_of(a, 0, TAB_W) for a in range(PASSES)]
+        wg_plane = [plane_of(a, TAB_W, TAB_W + WG_W) for a in range(PASSES)]
+        wr_plane = [plane_of(a, TAB_W + WG_W, PLANE_W) for a in range(PASSES)]
 
         half_gain = keep.tile([P, PACK], F32, name="half_gain", align_bytes=64)
         nc.vector.tensor_scalar(out=half_gain[:], in0=gain_sb[:], scalar1=0.5, scalar2=0.0, op0=ALU.mult, op1=ALU.add)
@@ -162,14 +175,14 @@ def tile_list_gated_node_update_kernel(
             return v_words[a, s][:, entries.start - s * HALF : entries.stop - s * HALF].bitcast(FP8X4)
 
         for s in range(HALVES):
-            gather_words(0, s, keep.tile([P, HALF], U32, name=f"v_words0{s}", align_bytes=64))
-        raws.extend(halves(load_rows(wp, a, f"wp_raw{a}", (20 + 8 * a) * KB)) for a in range(PASSES))
+            gather_words(0, s, placed(f"v_words0{s}", HALF, U32, (83 - 2 * s) * KB))
+        raws.append(halves(load_rows(wp, 0, "wp_raw0", 20 * KB)))
+        raws.append(load_halves(wp, 1, "wp_raw1", 28 * KB))
         wg_codes = keep.tile([P, PASSES, 2 * H], U8, name="wg_codes", align_bytes=64)
         nc.vector.tensor_copy(
             out=wg_codes[:].bitcast(U16).rearrange("p a (t n i) -> p a n t i", t=PACK, i=8),
             in_=wg_raw[:].bitcast(U16).rearrange("p a (n i t) -> p a n t i", t=PACK, i=8),
         )
-        windows.append(zeroed_window(1, 107 * KB, nc.vector))
         for s in range(HALVES):
             gather_words(1, s, keep.tile([P, HALF], U32, name=f"v_words1{s}", align_bytes=64))
 
@@ -264,16 +277,17 @@ def tile_list_gated_node_update_kernel(
                 op=ALU.mult,
             )
 
-        early = keep.tile([P, PACK * HALF], F32, name="early", align_bytes=64)
-        gates = [[gate(0, t, t, early[:, t * HALF : (t + 1) * HALF]) for t in range(PACK)]]
-        scaled0 = placed("scaled0", PACK * HALF, F32, 72 * KB)
-        scale_gates(gates[0], scaled0, 0, HALF)
+        early = [keep.tile([P, PACK * HALF], F32, name=f"early{s}", align_bytes=64) for s in range(HALVES)]
+        gates = [[gate(0, t, t, early[0][:, t * HALF : (t + 1) * HALF]) for t in range(PACK)]]
+        gates.append([gate(1, t, PACK + t, early[1][:, t * HALF : (t + 1) * HALF]) for t in range(2)])
         w_bf = placed("w_bf", ROWS, BF16, 8 * KB)
         wc_q = [quantize_weight(raws[0], "wc0", w_bf)]
-        wo_raw = halves(load_rows(wo, 0, "wo_raw", 132 * KB))
+        wo_raw = load_halves(wo, 0, "wo_raw", 132 * KB)
         wc_q.append(quantize_weight(raws[1], "wc1", w_bf))
         cands = placed("cands", PACK * H, F32, 88 * KB)
         diffs = [open_difference(candidate(b, b, cands[:, b * H : (b + 1) * H]), b, PACK + b) for b in range(PACK)]
+        scaled0 = placed("scaled0", PACK * HALF, F32, 72 * KB)
+        scale_gates(gates[0], scaled0, 0, HALF)
         wp_q = [quantize_weight(raws[2], "wp0", w_bf)]
         wr_codes = placed("wr_codes", PASSES * N, I32, 140 * KB)
         nc.sync.dma_start(
@@ -282,39 +296,33 @@ def tile_list_gated_node_update_kernel(
         )
         wgo_sb = placed("wgo_sb", S, F32, 144 * KB)
         nc.sync.dma_start(out=wgo_sb[:], in_=wgo)
-        wp1_codes = placed("wp1_codes", H, U32, 88 * KB)
-        wp_q.append(quantize_weight(raws[3], "wp1", w_bf, wp1_codes))
+        wp_q.append(quantize_weight(raws[3], "wp1", w_bf))
+        wo_q = quantize_weight(wo_raw, "wo", w_bf)
 
-        def new_state(h_q, s, c, bank, lo=0, hi=HALF):
+        def new_state(h_q, s, c, bank, y, lo=0, hi=HALF):
             acc = bank_tile(f"y{s}_{c}_{lo}", bank)[:, lo:hi]
+            cols = slice(c * P, (c + 1) * P)
             for a in range(PASSES):
                 times_table(
                     acc,
                     wr_codes[:, a * N + c * P : a * N + (c + 1) * P].bitcast(FP8X4),
-                    wr_plane[a][:, c * P : (c + 1) * P],
+                    wr_plane[a][:, cols],
                     a, slice(s * HALF + lo, s * HALF + hi), a == 0, False,
                 )
-            codes, plane = wo_q[c // 2]
-            cols = slice((c % 2) * P, (c % 2 + 1) * P)
             nc.tensor.matmul_mx(
                 out=acc,
-                lhsT=codes[:, cols].bitcast(FP8X4),
-                lhsT_scale=plane[:, cols],
+                lhsT=wo_q[0][:, cols].bitcast(FP8X4),
+                lhsT_scale=wo_q[1][:, cols],
                 rhs=h_q[0][:, lo:hi].bitcast(FP8X4),
                 rhs_scale=h_q[1][:, lo:hi],
                 start=False,
                 stop=True,
             )
-            if (s, c) == (0, CHUNKS - 1):
-                y = placed(f"y_sb{s}_{c}", HALF, F32, 64 * KB)
-            elif (s, c, lo) == (0, 0, 0):
-                y = placed(f"y_sb{s}_{c}", HALF, F32, 72 * KB)
-            elif (s, c) == (0, 0):
-                y = placed(f"y_sb{s}_{c}_{lo}", HALF, F32, 123 * KB)
-            else:
-                y = ring.tile([P, HALF], F32, name=f"y_sb{s}_{c}_{lo}", tag="y", bufs=4)
             nc.scalar.copy(out=y[:, lo:hi], in_=acc)
             return y
+
+        def y_tile(s, c):
+            return ring.tile([P, HALF], F32, name=f"y_sb{s}_{c}", tag="y", bufs=4)
 
         def scatter(y, s, c, lo=0, hi=HALF):
             lo_all, hi_all = s * HALF + lo, s * HALF + hi
@@ -326,40 +334,42 @@ def tile_list_gated_node_update_kernel(
             )
 
         present = [product(wp_q, b, "p", b) for b in range(PACK)]
-        wo_bf0 = placed("wo_bf0", PACK * 256, BF16, 8 * KB)
-        cast(nc.vector.tensor_copy, wo_raw, wo_bf0[:], 0)
-        wo_q = [quantize(wo_bf0, "wo0", 256)]
         h_bf0 = placed("h_bf0", PACK * HALF, BF16, 62 * KB)
+        h0 = mx_tiles("h0", HALF)
         for b in range(PACK):
             if b == PACK - 1:
                 neg = placed(f"neg{b}", H, F32, 123 * KB)
             else:
                 neg = ring.tile([P, H], F32, name=f"neg{b}", tag="neg", bufs=3)
             gated(close_difference(diffs[b], present[b], neg[:]), scaled0[:, b * HALF : (b + 1) * HALF], h_bf0, b)
-        wo_bf1 = placed("wo_bf1", PACK * 256, BF16, 123 * KB)
-        cast(nc.scalar.copy, wo_raw, wo_bf1[:], 1)
-        wo_q.append(quantize(wo_bf1, "wo1", 256))
-        h0 = quantize(h_bf0, "h0", HALF)
-        first = [new_state(h0, 0, 0, (4, 7)[u], u * 256, (u + 1) * 256) for u in range(2)]
-        ys = [new_state(h0, 0, c, 7 - c) for c in range(1, CHUNKS - 1)]
+            if b % 2 == 1:
+                quantize_part(h0, h_bf0[:, (b // 2) * 1024 : (b // 2 + 1) * 1024], b // 2)
+        first = [
+            new_state(h0, 0, 0, 0, placed("y_first", HALF, F32, 123 * KB), 0, 256),
+            new_state(h0, 0, 0, 1, y_tile(0, 0), 256, HALF),
+        ]
+        gates[1].extend(gate(1, t, t, early[1][:, t * HALF : (t + 1) * HALF]) for t in range(2, PACK))
+        ys = [new_state(h0, 0, c, c + 1, y_tile(0, c)) for c in range(1, CHUNKS - 1)]
         for u in range(2):
             scatter(first[u], 0, 0, u * 256, (u + 1) * 256)
         windows.extend(zeroed_window(c, (116 + 8 * (c - 2)) * KB, nc.gpsimd) for c in range(2, CHUNKS))
         for c in range(1, CHUNKS - 1):
             scatter(ys[c - 1], 0, c)
 
-        held = placed("held", 3 * PACK * H, F32, 40 * KB)
-        parts = [held[:, j * H : (j + 1) * H] for j in range(3 * PACK)]
-        gates.append([gate(1, t, t, parts[2 * PACK + t]) for t in range(PACK)])
+        cands1 = placed("cands1", PACK * H, F32, 40 * KB)
+        diffs = [
+            open_difference(candidate(PACK + k, PACK + k, cands1[:, k * H : (k + 1) * H]), PACK + k, PACK + k)
+            for k in range(PACK)
+        ]
         scaled1 = placed("scaled1", PACK * HALF, F32, 64 * KB)
         scale_gates(gates[1], scaled1, 0, HALF)
-        diffs = [open_difference(candidate(PACK + k, (4, 7, 6, 5)[k], parts[k]), PACK + k, (4, 7, 6, 5)[k]) for k in range(PACK)]
         present = [product(wp_q, PACK + k, "p", k) for k in range(PACK)]
         h_bf1 = keep.tile([P, PACK * HALF], BF16, name="h_bf1", align_bytes=64)
         for k in range(PACK):
-            gated(close_difference(diffs[k], present[k], parts[PACK + k]), scaled1[:, k * HALF : (k + 1) * HALF], h_bf1, k)
+            neg = placed(f"neg{PACK + k}", H, F32, (48 + 2 * k) * KB)
+            gated(close_difference(diffs[k], present[k], neg[:]), scaled1[:, k * HALF : (k + 1) * HALF], h_bf1, k)
         h1 = quantize(h_bf1, "h1", HALF)
-        scatter(new_state(h0, 0, CHUNKS - 1, 0), 0, CHUNKS - 1)
+        scatter(new_state(h0, 0, CHUNKS - 1, 0, placed("y_held", HALF, F32, 54 * KB)), 0, CHUNKS - 1)
         for c in range(CHUNKS):
-            scatter(new_state(h1, 1, c, (1, 2, 3, 0)[c]), 1, c)
+            scatter(new_state(h1, 1, c, (1, 2, 3, 0)[c], y_tile(1, c)), 1, c)
             nc.sync.dma_start(out=out[c * P : (c + 1) * P, :], in_=windows[c][:])

@@ -67,7 +67,7 @@ def tile_list_gated_node_update_kernel(
             return window
 
 
-        windows = [zeroed_window(0, 99 * KB, nc.vector), zeroed_window(1, 107 * KB, nc.gpsimd)]
+        windows = [zeroed_window(0, 99 * KB, nc.gpsimd)]
 
         idx = lists.tile([P, S // 16], U16, name="idx")
         nc.sync.dma_start(idx[:], offs)
@@ -277,17 +277,17 @@ def tile_list_gated_node_update_kernel(
                 op=ALU.mult,
             )
 
-        early = [keep.tile([P, PACK * HALF], F32, name=f"early{s}", align_bytes=64) for s in range(HALVES)]
-        gates = [[gate(0, t, t, early[0][:, t * HALF : (t + 1) * HALF]) for t in range(PACK)]]
-        gates.append([gate(1, t, PACK + t, early[1][:, t * HALF : (t + 1) * HALF]) for t in range(2)])
+        early = keep.tile([P, PACK * HALF], F32, name="early", align_bytes=64)
+        gates = [[gate(0, t, t, placed(f"gate{t}", HALF, F32, (88 + 2 * t) * KB)[:]) for t in range(PACK)]]
+        gates.append([gate(1, t, PACK + t, early[:, t * HALF : (t + 1) * HALF]) for t in range(2)])
         w_bf = placed("w_bf", ROWS, BF16, 8 * KB)
         wc_q = [quantize_weight(raws[0], "wc0", w_bf)]
         wo_raw = load_halves(wo, 0, "wo_raw", 132 * KB)
         wc_q.append(quantize_weight(raws[1], "wc1", w_bf))
-        cands = placed("cands", PACK * H, F32, 88 * KB)
-        diffs = [open_difference(candidate(b, b, cands[:, b * H : (b + 1) * H]), b, PACK + b) for b in range(PACK)]
         scaled0 = placed("scaled0", PACK * HALF, F32, 72 * KB)
         scale_gates(gates[0], scaled0, 0, HALF)
+        cands = [placed(f"cand{b}", H, F32, (88 + 2 * b) * KB) for b in range(PACK)]
+        diffs = [open_difference(candidate(b, b, cands[b][:]), b, PACK + b) for b in range(PACK)]
         wp_q = [quantize_weight(raws[2], "wp0", w_bf)]
         wr_codes = placed("wr_codes", PASSES * N, I32, 140 * KB)
         nc.sync.dma_start(
@@ -348,10 +348,11 @@ def tile_list_gated_node_update_kernel(
             new_state(h0, 0, 0, 0, placed("y_first", HALF, F32, 123 * KB), 0, 256),
             new_state(h0, 0, 0, 1, y_tile(0, 0), 256, HALF),
         ]
-        gates[1].extend(gate(1, t, t, early[1][:, t * HALF : (t + 1) * HALF]) for t in range(2, PACK))
+        gates[1].extend(gate(1, t, t, early[:, t * HALF : (t + 1) * HALF]) for t in range(2, PACK))
         ys = [new_state(h0, 0, c, c + 1, y_tile(0, c)) for c in range(1, CHUNKS - 1)]
         for u in range(2):
             scatter(first[u], 0, 0, u * 256, (u + 1) * 256)
+        windows.append(zeroed_window(1, 56 * KB, nc.gpsimd))
         windows.extend(zeroed_window(c, (116 + 8 * (c - 2)) * KB, nc.gpsimd) for c in range(2, CHUNKS))
         for c in range(1, CHUNKS - 1):
             scatter(ys[c - 1], 0, c)

@@ -57,17 +57,19 @@ def tile_list_gated_node_update_kernel(
         wg_rows = placed("wg_rows", PASSES * WG_W, I32, 84 * KB)
         nc.gpsimd.memset(wg_rows[0:TOP, :], 0)
         planes = keep.tile([P, PASSES * PLANE_W], I32, name="planes", align_bytes=64)
-        nc.gpsimd.memset(planes[:], 0)
+        by_pass = planes[:].rearrange("p (a w) -> p a w", a=PASSES)
+        nc.gpsimd.memset(by_pass[0:TOP, :, TAB_W + WG_W :], 0)
         ident = keep.tile([P, P], F32, name="ident", align_bytes=64)
         make_identity(nc, ident[:])
 
-        def zeroed_window(c, offset, engine):
+        def zeroed_window(c, offset, engine, parts=(slice(0, T2),)):
             window = placed(f"window{c}", T2, F32, offset)
-            engine.memset(window[:].bitcast(I32), 0)
+            for cols in parts:
+                engine.memset(window[:, cols].bitcast(I32), 0)
             return window
 
 
-        windows = [zeroed_window(0, 99 * KB, nc.gpsimd)]
+        windows = [zeroed_window(0, 99 * KB, nc.vector, (slice(0, T2 - 1), slice(T2 - 1, T2)))]
 
         idx = lists.tile([P, S // 16], U16, name="idx")
         nc.sync.dma_start(idx[:], offs)
@@ -126,11 +128,9 @@ def tile_list_gated_node_update_kernel(
                 cast(nc.vector.tensor_copy, raw, w_bf[:, u * 1024 : (u + 1) * 1024], u)
             return quantize(w_bf, name, H, codes)
 
-        nc.sync.dma_start(out=wg_rows[TOP:P, :].rearrange("q (a w) -> q a w", a=PASSES), in_=scale_rows(wg_scales))
-        staged = keep.tile([P, PASSES * PLANE_W], I32, name="staged", align_bytes=64)
-        by_pass = staged[:].rearrange("p (a w) -> p a w", a=PASSES)
-        nc.sync.dma_start(out=by_pass[TOP:P, :, TAB_W + WG_W :], in_=scale_rows(wr_scales))
         table = [load_table(0, 20 * KB)]
+        nc.sync.dma_start(out=wg_rows[TOP:P, :].rearrange("q (a w) -> q a w", a=PASSES), in_=scale_rows(wg_scales))
+        nc.sync.dma_start(out=by_pass[TOP:P, :, TAB_W + WG_W :], in_=scale_rows(wr_scales))
         wg_raw = keep.tile([P, PASSES, 2 * H // 4], I32, name="wg_raw", align_bytes=64)
         nc.sync.dma_start(out=wg_raw[:], in_=wg_words.bitcast(I32).rearrange("a p w -> p a w"))
         table.append(load_table(1, 0))
@@ -145,14 +145,14 @@ def tile_list_gated_node_update_kernel(
         for a in range(PASSES):
             first = a * PLANE_W + TAB_W
             nc.vector.tensor_copy(
-                out=staged[:, first : first + WG_W].bitcast(U8).rearrange("p (t m) -> p t m", t=PACK),
+                out=planes[:, first : first + WG_W].bitcast(U8).rearrange("p (t m) -> p t m", t=PACK),
                 in_=wg_rows[:, a * WG_W : (a + 1) * WG_W].bitcast(U8).rearrange("p (m t) -> p t m", t=PACK),
             )
         nc.vector.tensor_copy(
-            out=by_pass[96:P, :, 0:TAB_W], in_=gathered[96:P, :].bitcast(I32).rearrange("p (a w) -> p a w", a=PASSES)
+            out=by_pass[:, :, 0:TAB_W], in_=gathered[:].bitcast(I32).rearrange("p (a w) -> p a w", a=PASSES)
         )
         for r in range(4):
-            nc.sync.dma_start(out=planes[r:P:32, :], in_=staged[TOP + r : P : 4, :])
+            nc.sync.dma_start(out=planes[r:P:32, :], in_=planes[TOP + r : P : 4, :])
         raws = [halves(load_rows(wc, a, f"wc_raw{a}", (132 + 8 * a) * KB)) for a in range(PASSES)]
 
         def plane_of(a, lo, hi):
@@ -177,7 +177,7 @@ def tile_list_gated_node_update_kernel(
         for s in range(HALVES):
             gather_words(0, s, placed(f"v_words0{s}", HALF, U32, (83 - 2 * s) * KB))
         raws.append(halves(load_rows(wp, 0, "wp_raw0", 20 * KB)))
-        raws.append(load_halves(wp, 1, "wp_raw1", 28 * KB))
+        raws.append(halves(load_rows(wp, 1, "wp_raw1", 28 * KB)))
         wg_codes = keep.tile([P, PASSES, 2 * H], U8, name="wg_codes", align_bytes=64)
         nc.vector.tensor_copy(
             out=wg_codes[:].bitcast(U16).rearrange("p a (t n i) -> p a n t i", t=PACK, i=8),
@@ -279,7 +279,6 @@ def tile_list_gated_node_update_kernel(
 
         early = keep.tile([P, PACK * HALF], F32, name="early", align_bytes=64)
         gates = [[gate(0, t, t, placed(f"gate{t}", HALF, F32, (88 + 2 * t) * KB)[:]) for t in range(PACK)]]
-        gates.append([gate(1, t, PACK + t, early[:, t * HALF : (t + 1) * HALF]) for t in range(2)])
         w_bf = placed("w_bf", ROWS, BF16, 8 * KB)
         wc_q = [quantize_weight(raws[0], "wc0", w_bf)]
         wo_raw = load_halves(wo, 0, "wo_raw", 132 * KB)
@@ -348,14 +347,14 @@ def tile_list_gated_node_update_kernel(
             new_state(h0, 0, 0, 0, placed("y_first", HALF, F32, 123 * KB), 0, 256),
             new_state(h0, 0, 0, 1, y_tile(0, 0), 256, HALF),
         ]
-        gates[1].extend(gate(1, t, t, early[:, t * HALF : (t + 1) * HALF]) for t in range(2, PACK))
-        ys = [new_state(h0, 0, c, c + 1, y_tile(0, c)) for c in range(1, CHUNKS - 1)]
+        ys = [new_state(h0, 0, c, (c + 1) % PACK, y_tile(0, c)) for c in range(1, CHUNKS)]
         for u in range(2):
             scatter(first[u], 0, 0, u * 256, (u + 1) * 256)
         windows.append(zeroed_window(1, 56 * KB, nc.gpsimd))
         windows.extend(zeroed_window(c, (116 + 8 * (c - 2)) * KB, nc.gpsimd) for c in range(2, CHUNKS))
-        for c in range(1, CHUNKS - 1):
+        for c in range(1, CHUNKS):
             scatter(ys[c - 1], 0, c)
+        gates.append([gate(1, t, PACK + t, early[:, t * HALF : (t + 1) * HALF]) for t in range(PACK)])
 
         cands1 = placed("cands1", PACK * H, F32, 40 * KB)
         diffs = [
@@ -364,13 +363,21 @@ def tile_list_gated_node_update_kernel(
         ]
         scaled1 = placed("scaled1", PACK * HALF, F32, 64 * KB)
         scale_gates(gates[1], scaled1, 0, HALF)
-        present = [product(wp_q, PACK + k, "p", k) for k in range(PACK)]
+        present = [product(wp_q, PACK + k, "p", (k + 1) % PACK) for k in range(PACK)]
         h_bf1 = keep.tile([P, PACK * HALF], BF16, name="h_bf1", align_bytes=64)
+        h1 = mx_tiles("h1", HALF)
         for k in range(PACK):
             neg = placed(f"neg{PACK + k}", H, F32, (48 + 2 * k) * KB)
             gated(close_difference(diffs[k], present[k], neg[:]), scaled1[:, k * HALF : (k + 1) * HALF], h_bf1, k)
-        h1 = quantize(h_bf1, "h1", HALF)
-        scatter(new_state(h0, 0, CHUNKS - 1, 0, placed("y_held", HALF, F32, 54 * KB)), 0, CHUNKS - 1)
-        for c in range(CHUNKS):
-            scatter(new_state(h1, 1, c, (1, 2, 3, 0)[c], y_tile(1, c)), 1, c)
+            if k % 2 == 1:
+                quantize_part(h1, h_bf1[:, (k // 2) * 1024 : (k // 2 + 1) * 1024], k // 2)
+        first = [
+            new_state(h1, 1, 0, 1, placed("y_first1", HALF, F32, 54 * KB), 0, 256),
+            new_state(h1, 1, 0, 2, y_tile(1, 0), 256, HALF),
+        ]
+        for u in range(2):
+            scatter(first[u], 1, 0, u * 256, (u + 1) * 256)
+        nc.sync.dma_start(out=out[0:P, :], in_=windows[0][:])
+        for c in range(1, CHUNKS):
+            scatter(new_state(h1, 1, c, (c + 2) % PACK, y_tile(1, c)), 1, c)
             nc.sync.dma_start(out=out[c * P : (c + 1) * P, :], in_=windows[c][:])

@@ -29,7 +29,7 @@ BANK = 2048
 KB = 1024
 ROWS = PACK * H
 SCALE_ROWS = 16
-TOP = P - SCALE_ROWS
+TOP = P - PASSES * SCALE_ROWS
 TAB_W, WG_W, WR_W = S // 4, H // 4, N // 4
 PLANE_W = TAB_W + WG_W + WR_W
 
@@ -49,16 +49,12 @@ def tile_list_gated_node_update_kernel(
             return arena.tile([P, width], dtype, name=name, offset=offset, align_bytes=64)
 
         def scale_rows(scales):
-            return scales.bitcast(I32).rearrange("a q w -> q a w")
+            return scales.bitcast(I32).rearrange("a q w -> (a q) w")
 
-        tab_rows = [placed(f"tab_rows{a}", T // 4, I32, (16, 80)[a] * KB) for a in range(PASSES)]
-        for a in range(PASSES):
-            nc.gpsimd.memset(tab_rows[a][0:TOP, :], 0)
-        wg_rows = placed("wg_rows", PASSES * WG_W, I32, 84 * KB)
+        tab_rows = placed("tab_rows", T // 4, I32, 80 * KB)
+        nc.gpsimd.memset(tab_rows[0:TOP, :], 0)
+        wg_rows = placed("wg_rows", WG_W, I32, 84 * KB)
         nc.gpsimd.memset(wg_rows[0:TOP, :], 0)
-        planes = keep.tile([P, PASSES * PLANE_W], I32, name="planes", align_bytes=64)
-        by_pass = planes[:].rearrange("p (a w) -> p a w", a=PASSES)
-        nc.gpsimd.memset(by_pass[0:TOP, :, TAB_W + WG_W :], 0)
         ident = keep.tile([P, P], F32, name="ident", align_bytes=64)
         make_identity(nc, ident[:])
 
@@ -73,8 +69,7 @@ def tile_list_gated_node_update_kernel(
 
         idx = lists.tile([P, S // 16], U16, name="idx")
         nc.sync.dma_start(idx[:], offs)
-        for a in range(PASSES):
-            nc.sync.dma_start(out=tab_rows[a][TOP:P, :], in_=tab_scales[a].bitcast(I32))
+        nc.sync.dma_start(out=tab_rows[TOP:P, :], in_=scale_rows(tab_scales))
 
         def load_table(a, offset):
             words = placed(f"table{a}", T, I32, offset)
@@ -129,8 +124,9 @@ def tile_list_gated_node_update_kernel(
             return quantize(w_bf, name, H, codes)
 
         table = [load_table(0, 20 * KB)]
-        nc.sync.dma_start(out=wg_rows[TOP:P, :].rearrange("q (a w) -> q a w", a=PASSES), in_=scale_rows(wg_scales))
-        nc.sync.dma_start(out=by_pass[TOP:P, :, TAB_W + WG_W :], in_=scale_rows(wr_scales))
+        nc.sync.dma_start(out=wg_rows[TOP:P, :], in_=scale_rows(wg_scales))
+        staged = keep.tile([P, PLANE_W], I32, name="staged", align_bytes=64)
+        nc.sync.dma_start(out=staged[TOP:P, TAB_W + WG_W :], in_=scale_rows(wr_scales))
         wg_raw = keep.tile([P, PASSES, 2 * H // 4], I32, name="wg_raw", align_bytes=64)
         nc.sync.dma_start(out=wg_raw[:], in_=wg_words.bitcast(I32).rearrange("a p w -> p a w"))
         table.append(load_table(1, 0))
@@ -139,24 +135,23 @@ def tile_list_gated_node_update_kernel(
         gain_sb = keep.tile([P, PACK], F32, name="gain_sb", align_bytes=64)
         nc.sync.dma_start(out=gain_sb[:], in_=gain.rearrange("(p t) -> p t", t=PACK))
 
-        gathered = placed("gathered", PASSES * S, U8, 139 * KB)
-        for a in range(PASSES):
-            nc.vector.tensor_copy(out=gathered[:, a * S : (a + 1) * S], in_=tab_rows[a][:].bitcast(U8).indirect(idx[:]))
-        for a in range(PASSES):
-            first = a * PLANE_W + TAB_W
-            nc.vector.tensor_copy(
-                out=planes[:, first : first + WG_W].bitcast(U8).rearrange("p (t m) -> p t m", t=PACK),
-                in_=wg_rows[:, a * WG_W : (a + 1) * WG_W].bitcast(U8).rearrange("p (m t) -> p t m", t=PACK),
-            )
+        gathered = placed("gathered", S, U8, 139 * KB + 512)
+        nc.vector.tensor_copy(out=gathered[:], in_=tab_rows[:].bitcast(U8).indirect(idx[:]))
         nc.vector.tensor_copy(
-            out=by_pass[:, :, 0:TAB_W], in_=gathered[:].bitcast(I32).rearrange("p (a w) -> p a w", a=PASSES)
+            out=staged[:, TAB_W : TAB_W + WG_W].bitcast(U8).rearrange("p (t m) -> p t m", t=PACK),
+            in_=wg_rows[:].bitcast(U8).rearrange("p (m t) -> p t m", t=PACK),
         )
-        for r in range(4):
-            nc.sync.dma_start(out=planes[r:P:32, :], in_=planes[TOP + r : P : 4, :])
-        raws = [halves(load_rows(wc, a, f"wc_raw{a}", (132 + 8 * a) * KB)) for a in range(PASSES)]
+        nc.vector.tensor_copy(out=staged[TOP:P, 0:TAB_W], in_=gathered[TOP:P, :].bitcast(I32))
+        planes, raws = [], []
+        for a in range(PASSES):
+            planes.append(placed(f"planes{a}", PLANE_W, I32, (80 + 2 * a) * KB))
+            first = TOP + SCALE_ROWS * a
+            for r in range(4):
+                nc.sync.dma_start(out=planes[a][r:P:32, :], in_=staged[first + r : first + SCALE_ROWS : 4, :])
+            raws.append(halves(load_rows(wc, a, f"wc_raw{a}", (132 + 8 * a) * KB)))
 
         def plane_of(a, lo, hi):
-            return planes[:, a * PLANE_W + lo : a * PLANE_W + hi].bitcast(U8)
+            return planes[a][:, lo:hi].bitcast(U8)
 
         v_plane = [plane_of(a, 0, TAB_W) for a in range(PASSES)]
         wg_plane = [plane_of(a, TAB_W, TAB_W + WG_W) for a in range(PASSES)]
@@ -175,7 +170,7 @@ def tile_list_gated_node_update_kernel(
             return v_words[a, s][:, entries.start - s * HALF : entries.stop - s * HALF].bitcast(FP8X4)
 
         for s in range(HALVES):
-            gather_words(0, s, placed(f"v_words0{s}", HALF, U32, (83 - 2 * s) * KB))
+            gather_words(0, s, placed(f"v_words0{s}", HALF, U32, (84 + 2 * s) * KB))
         raws.append(halves(load_rows(wp, 0, "wp_raw0", 20 * KB)))
         raws.append(halves(load_rows(wp, 1, "wp_raw1", 28 * KB)))
         wg_codes = keep.tile([P, PASSES, 2 * H], U8, name="wg_codes", align_bytes=64)

@@ -66,6 +66,7 @@ def tile_list_gated_node_update_kernel(
 
 
         windows = [zeroed_window(0, 99 * KB, nc.vector, (slice(0, T2 - 1), slice(T2 - 1, T2)))]
+        windows.extend(zeroed_window(c, (108 + 8 * c) * KB, nc.gpsimd) for c in (1, 2))
 
         idx = lists.tile([P, S // 16], U16, name="idx")
         nc.sync.dma_start(idx[:], offs)
@@ -127,7 +128,7 @@ def tile_list_gated_node_update_kernel(
         nc.sync.dma_start(out=wg_rows[TOP:P, :], in_=scale_rows(wg_scales))
         staged = keep.tile([P, PLANE_W], I32, name="staged", align_bytes=64)
         nc.sync.dma_start(out=staged[TOP:P, TAB_W + WG_W :], in_=scale_rows(wr_scales))
-        wg_raw = keep.tile([P, PASSES, 2 * H // 4], I32, name="wg_raw", align_bytes=64)
+        wg_raw = arena.tile([P, PASSES, 2 * H // 4], I32, name="wg_raw", offset=56 * KB, align_bytes=64)
         nc.sync.dma_start(out=wg_raw[:], in_=wg_words.bitcast(I32).rearrange("a p w -> p a w"))
         table.append(load_table(1, 0))
         idx2 = lists.tile([P, S // 16], U16, name="idx2")
@@ -178,6 +179,7 @@ def tile_list_gated_node_update_kernel(
             out=wg_codes[:].bitcast(U16).rearrange("p a (t n i) -> p a n t i", t=PACK, i=8),
             in_=wg_raw[:].bitcast(U16).rearrange("p a (n i t) -> p a n t i", t=PACK, i=8),
         )
+        windows.append(zeroed_window(3, 56 * KB, nc.vector))
         for s in range(HALVES):
             gather_words(1, s, keep.tile([P, HALF], U32, name=f"v_words1{s}", align_bytes=64))
 
@@ -258,8 +260,15 @@ def tile_list_gated_node_update_kernel(
             turn(diff, c, True)
             return diff
 
-        def close_difference(diff, acc, neg):
-            leave_dealt(neg, acc, ACT.Copy, -1.0)
+        def close_difference(diff, acc, neg, pieces=1):
+            step = PACK // pieces
+            for lo in range(0, PACK, step):
+                nc.scalar.activation(
+                    out=neg.rearrange("p (t m) -> p t m", t=PACK)[:, lo : lo + step],
+                    in_=acc[:].rearrange("p (m t) -> p t m", t=PACK)[:, lo : lo + step],
+                    func=ACT.Copy,
+                    scale=-1.0,
+                )
             turn(diff, neg, False)
             return diff
 
@@ -278,10 +287,10 @@ def tile_list_gated_node_update_kernel(
         wc_q = [quantize_weight(raws[0], "wc0", w_bf)]
         wo_raw = load_halves(wo, 0, "wo_raw", 132 * KB)
         wc_q.append(quantize_weight(raws[1], "wc1", w_bf))
+        cands = [placed(f"cand{b}", H, F32, (107 + 2 * b) * KB) for b in range(PACK)]
+        diffs = [open_difference(candidate(b, b, cands[b][:]), b, PACK + b) for b in range(PACK)]
         scaled0 = placed("scaled0", PACK * HALF, F32, 72 * KB)
         scale_gates(gates[0], scaled0, 0, HALF)
-        cands = [placed(f"cand{b}", H, F32, (88 + 2 * b) * KB) for b in range(PACK)]
-        diffs = [open_difference(candidate(b, b, cands[b][:]), b, PACK + b) for b in range(PACK)]
         wp_q = [quantize_weight(raws[2], "wp0", w_bf)]
         wr_codes = placed("wr_codes", PASSES * N, I32, 140 * KB)
         nc.sync.dma_start(
@@ -328,25 +337,23 @@ def tile_list_gated_node_update_kernel(
             )
 
         present = [product(wp_q, b, "p", b) for b in range(PACK)]
-        h_bf0 = placed("h_bf0", PACK * HALF, BF16, 62 * KB)
+        h_bf0 = placed("h_bf0", PACK * HALF, BF16, 64 * KB)
         h0 = mx_tiles("h0", HALF)
         for b in range(PACK):
             if b == PACK - 1:
-                neg = placed(f"neg{b}", H, F32, 123 * KB)
+                neg = placed(f"neg{b}", H, F32, 96 * KB)
             else:
                 neg = ring.tile([P, H], F32, name=f"neg{b}", tag="neg", bufs=3)
-            gated(close_difference(diffs[b], present[b], neg[:]), scaled0[:, b * HALF : (b + 1) * HALF], h_bf0, b)
+            gated(close_difference(diffs[b], present[b], neg[:], 2 if b in (0, PACK - 1) else 1), scaled0[:, b * HALF : (b + 1) * HALF], h_bf0, b)
             if b % 2 == 1:
                 quantize_part(h0, h_bf0[:, (b // 2) * 1024 : (b // 2 + 1) * 1024], b // 2)
         first = [
-            new_state(h0, 0, 0, 0, placed("y_first", HALF, F32, 123 * KB), 0, 256),
+            new_state(h0, 0, 0, 0, placed("y_first", HALF, F32, 96 * KB), 0, 256),
             new_state(h0, 0, 0, 1, y_tile(0, 0), 256, HALF),
         ]
         ys = [new_state(h0, 0, c, (c + 1) % PACK, y_tile(0, c)) for c in range(1, CHUNKS)]
         for u in range(2):
             scatter(first[u], 0, 0, u * 256, (u + 1) * 256)
-        windows.append(zeroed_window(1, 56 * KB, nc.gpsimd))
-        windows.extend(zeroed_window(c, (116 + 8 * (c - 2)) * KB, nc.gpsimd) for c in range(2, CHUNKS))
         for c in range(1, CHUNKS):
             scatter(ys[c - 1], 0, c)
         gates.append([gate(1, t, PACK + t, early[:, t * HALF : (t + 1) * HALF]) for t in range(PACK)])
@@ -364,8 +371,8 @@ def tile_list_gated_node_update_kernel(
         for k in range(PACK):
             neg = placed(f"neg{PACK + k}", H, F32, (48 + 2 * k) * KB)
             gated(close_difference(diffs[k], present[k], neg[:]), scaled1[:, k * HALF : (k + 1) * HALF], h_bf1, k)
-            if k % 2 == 1:
-                quantize_part(h1, h_bf1[:, (k // 2) * 1024 : (k // 2 + 1) * 1024], k // 2)
+            if k >= 2:
+                quantize_part(h1, h_bf1[:, (k - 2) * 1024 : (k - 1) * 1024], k - 2)
         first = [
             new_state(h1, 1, 0, 1, placed("y_first1", HALF, F32, 54 * KB), 0, 256),
             new_state(h1, 1, 0, 2, y_tile(1, 0), 256, HALF),

@@ -22,16 +22,17 @@ PACK = 4
 K_PASS = P * PACK
 PASSES = K // K_PASS
 HALF = 512
-HALVES = S // HALF
+QUARTER = 256
 CHUNKS = N // P
-COLS = HALF // 16
 BANK = 2048
 KB = 1024
 ROWS = PACK * H
 SCALE_ROWS = 16
-TOP = P - PASSES * SCALE_ROWS
+TOP = P - SCALE_ROWS
 TAB_W, WG_W, WR_W = S // 4, H // 4, N // 4
-PLANE_W = TAB_W + WG_W + WR_W
+WG_AT = PASSES * TAB_W
+WR_AT = WG_AT + PASSES * WG_W
+PLANE_W = WR_AT + PASSES * WR_W
 
 
 def tile_list_gated_node_update_kernel(
@@ -41,345 +42,365 @@ def tile_list_gated_node_update_kernel(
     with ExitStack() as ctx:
         lists = ctx.enter_context(tc.tile_pool(name="lists", bufs=1))
         keep = ctx.enter_context(tc.tile_pool(name="keep", bufs=1))
-        ring = ctx.enter_context(tc.tile_pool(name="ring", bufs=2))
+        ring = ctx.enter_context(tc.tile_pool(name="ring", bufs=3))
         arena = ctx.enter_context(tc.tile_pool(name="arena", bufs=1))
         psum = ctx.enter_context(tc.psum_pool(name="psum", bufs=1))
 
-        def placed(name, width, dtype, offset):
-            return arena.tile([P, width], dtype, name=name, offset=offset, align_bytes=64)
+        def kept(name, width, dtype):
+            return keep.tile([P, width], dtype, name=name, align_bytes=64)
 
-        def scale_rows(scales):
-            return scales.bitcast(I32).rearrange("a q w -> (a q) w")
+        def placed(name, width, dtype, kib):
+            return arena.tile([P, width], dtype, name=name, offset=int(kib * KB), align_bytes=64)
 
-        tab_rows = placed("tab_rows", T // 4, I32, 80 * KB)
-        nc.gpsimd.memset(tab_rows[0:TOP, :], 0)
-        wg_rows = placed("wg_rows", WG_W, I32, 84 * KB)
+        def bank_tile(name, bank):
+            return psum.tile([P, HALF], F32, name=name, offset=bank * BANK)
+
+        def side_by_side(scales):
+            return scales.bitcast(I32).rearrange("a q w -> q a w")
+
+        tab_rows = [placed(f"tab_rows{a}", T // 4, I32, 80 + 4 * a) for a in range(PASSES)]
+        for rows in tab_rows:
+            nc.gpsimd.memset(rows[0:TOP, :], 0)
+        wg_rows = placed("wg_rows", PASSES * WG_W, I32, 88)
         nc.gpsimd.memset(wg_rows[0:TOP, :], 0)
-        ident = keep.tile([P, P], F32, name="ident", align_bytes=64)
+        ident = kept("ident", P, F32)
         make_identity(nc, ident[:])
 
-        def zeroed_window(c, offset, engine, parts=(slice(0, T2),)):
-            window = placed(f"window{c}", T2, F32, offset)
+        def zeroed_window(c, kib, engine, parts=(slice(0, T2),)):
+            window = placed(f"window{c}", T2, F32, kib)
             for cols in parts:
                 engine.memset(window[:, cols].bitcast(I32), 0)
             return window
 
-
-        windows = [zeroed_window(0, 99 * KB, nc.vector, (slice(0, T2 - 1), slice(T2 - 1, T2)))]
-        windows.extend(zeroed_window(c, (108 + 8 * c) * KB, nc.gpsimd) for c in (1, 2))
+        windows = [zeroed_window(0, 99, nc.vector, (slice(0, T2 - 1), slice(T2 - 1, T2)))]
+        windows.append(zeroed_window(1, 116, nc.gpsimd))
 
         idx = lists.tile([P, S // 16], U16, name="idx")
         nc.sync.dma_start(idx[:], offs)
-        nc.sync.dma_start(out=tab_rows[TOP:P, :], in_=scale_rows(tab_scales))
+        for a in range(PASSES):
+            nc.sync.dma_start(out=tab_rows[a][TOP:P, :], in_=tab_scales[a].bitcast(I32))
 
-        def load_table(a, offset):
-            words = placed(f"table{a}", T, I32, offset)
+        def load_table(a, kib):
+            words = placed(f"table{a}", T, I32, kib)
             nc.sync.dma_start(out=words[:], in_=tab_words[a].rearrange("p t i -> p (t i)").bitcast(I32))
             return words
 
-        def load_rows(w, a, name, offset):
-            raw = placed(name, ROWS, F32, offset)
+        def load_whole(w, a, name, kib):
+            raw = placed(name, ROWS, F32, kib)
             rows = w[a * K_PASS : (a + 1) * K_PASS, :].rearrange("(p j) c -> p (j c)", j=PACK)
             nc.sync.dma_start(out=raw[:], in_=rows)
-            return raw[:]
+            view = raw[:].rearrange("p (j n i) -> p n j i", i=4, j=PACK)
+            return [view[:, u * 64 : (u + 1) * 64] for u in range(2)]
 
-        def halves(raw):
-            rows = raw.rearrange("p (j n i) -> p n j i", i=4, j=PACK)
-            return [rows[:, u * 64 : (u + 1) * 64] for u in range(2)]
-
-        def load_halves(w, a, name, offset):
+        def load_half(w, a, u, name, kib):
             rows = w[a * K_PASS : (a + 1) * K_PASS, :].rearrange("(p j) c -> p j c", j=PACK)
-            parts = []
-            for u in range(2):
-                raw = placed(f"{name}_{u}", ROWS // 2, F32, offset + u * 4 * KB)
-                nc.sync.dma_start(
-                    out=raw[:].rearrange("p (j c) -> p j c", j=PACK), in_=rows[:, :, u * 256 : (u + 1) * 256]
-                )
-                parts.append(raw[:].rearrange("p (j n i) -> p n j i", i=4, j=PACK))
-            return parts
-
-        def cast(copy, raw, grouped, u):
-            copy(out=grouped.rearrange("p (n i j) -> p n j i", i=4, j=PACK), in_=raw[u])
-
-        def mx_tiles(name, width, codes=None):
-            if codes is None:
-                codes = keep.tile([P, width], U32, name=name + "_codes", align_bytes=64)
-            return codes, keep.tile([P, width], U8, name=name + "_plane", align_bytes=64)
-
-        def quantize_part(tiles, grouped, u):
-            nc.vector.quantize_mx(
-                out=tiles[0][:, u * 256 : (u + 1) * 256].bitcast(FP8X4),
-                scales=tiles[1][:, u * 256 : (u + 1) * 256],
-                in_=grouped,
+            raw = placed(f"{name}_{u}", ROWS // 2, F32, kib)
+            nc.sync.dma_start(
+                out=raw[:].rearrange("p (j c) -> p j c", j=PACK), in_=rows[:, :, u * QUARTER : (u + 1) * QUARTER]
             )
+            return raw[:].rearrange("p (j n i) -> p n j i", i=4, j=PACK)
 
-        def quantize(grouped, name, width, codes=None):
-            tiles = mx_tiles(name, width, codes)
-            for u in range(width // 256):
-                quantize_part(tiles, grouped[:, u * 1024 : (u + 1) * 1024], u)
-            return tiles
-
-        def quantize_weight(raw, name, w_bf, codes=None):
-            for u in range(2):
-                cast(nc.vector.tensor_copy, raw, w_bf[:, u * 1024 : (u + 1) * 1024], u)
-            return quantize(w_bf, name, H, codes)
-
-        table = [load_table(0, 20 * KB)]
-        nc.sync.dma_start(out=wg_rows[TOP:P, :], in_=scale_rows(wg_scales))
-        staged = keep.tile([P, PLANE_W], I32, name="staged", align_bytes=64)
-        nc.sync.dma_start(out=staged[TOP:P, TAB_W + WG_W :], in_=scale_rows(wr_scales))
+        table = [load_table(0, 20)]
+        nc.sync.dma_start(out=wg_rows[TOP:P, :].rearrange("q (a w) -> q a w", a=PASSES), in_=side_by_side(wg_scales))
+        staged = kept("staged", PLANE_W, I32)
+        nc.sync.dma_start(
+            out=staged[TOP:P, WR_AT:].rearrange("q (a w) -> q a w", a=PASSES), in_=side_by_side(wr_scales)
+        )
         wg_raw = arena.tile([P, PASSES, 2 * H // 4], I32, name="wg_raw", offset=56 * KB, align_bytes=64)
         nc.sync.dma_start(out=wg_raw[:], in_=wg_words.bitcast(I32).rearrange("a p w -> p a w"))
         table.append(load_table(1, 0))
+
+        gathered = placed("gathered", PASSES * S, U8, 131)
+        for a in range(PASSES):
+            nc.vector.tensor_copy(
+                out=gathered[:, a * S : (a + 1) * S], in_=tab_rows[a][:].bitcast(U8).indirect(idx[:])
+            )
+        nc.vector.tensor_copy(
+            out=staged[:, WG_AT:WR_AT].bitcast(U8).rearrange("p (a t m) -> p a t m", a=PASSES, t=PACK),
+            in_=wg_rows[:].bitcast(U8).rearrange("p (a m t) -> p a t m", a=PASSES, t=PACK),
+        )
+        nc.vector.tensor_copy(out=staged[96:P, 0:WG_AT], in_=gathered[96:P, :].bitcast(I32))
+        windows.append(zeroed_window(2, 124, nc.gpsimd))
+        planes = placed("planes", PLANE_W, I32, 80)
+        for r in range(4):
+            nc.sync.dma_start(out=planes[r:P:32, :], in_=staged[TOP + r : P : 4, :])
+        wc_raw = [load_whole(wc, 0, "wc_raw0", 132)]
         idx2 = lists.tile([P, S // 16], U16, name="idx2")
         nc.sync.dma_start(idx2[:], offs2)
-        gain_sb = keep.tile([P, PACK], F32, name="gain_sb", align_bytes=64)
-        nc.sync.dma_start(out=gain_sb[:], in_=gain.rearrange("(p t) -> p t", t=PACK))
+        gains = kept("gains", PACK, F32)
+        nc.sync.dma_start(out=gains[:], in_=gain.rearrange("(p t) -> p t", t=PACK))
 
-        gathered = placed("gathered", S, U8, 139 * KB + 512)
-        nc.vector.tensor_copy(out=gathered[:], in_=tab_rows[:].bitcast(U8).indirect(idx[:]))
-        nc.vector.tensor_copy(
-            out=staged[:, TAB_W : TAB_W + WG_W].bitcast(U8).rearrange("p (t m) -> p t m", t=PACK),
-            in_=wg_rows[:].bitcast(U8).rearrange("p (m t) -> p t m", t=PACK),
-        )
-        nc.vector.tensor_copy(out=staged[TOP:P, 0:TAB_W], in_=gathered[TOP:P, :].bitcast(I32))
-        planes, raws = [], []
-        for a in range(PASSES):
-            planes.append(placed(f"planes{a}", PLANE_W, I32, (80 + 2 * a) * KB))
-            first = TOP + SCALE_ROWS * a
-            for r in range(4):
-                nc.sync.dma_start(out=planes[a][r:P:32, :], in_=staged[first + r : first + SCALE_ROWS : 4, :])
-            raws.append(halves(load_rows(wc, a, f"wc_raw{a}", (132 + 8 * a) * KB)))
+        def plane_of(at, width, a):
+            return planes[:, at + a * width : at + (a + 1) * width].bitcast(U8)
 
-        def plane_of(a, lo, hi):
-            return planes[a][:, lo:hi].bitcast(U8)
+        v_plane = [plane_of(0, TAB_W, a) for a in range(PASSES)]
+        wg_plane = [plane_of(WG_AT, WG_W, a) for a in range(PASSES)]
+        wr_plane = [plane_of(WR_AT, WR_W, a) for a in range(PASSES)]
 
-        v_plane = [plane_of(a, 0, TAB_W) for a in range(PASSES)]
-        wg_plane = [plane_of(a, TAB_W, TAB_W + WG_W) for a in range(PASSES)]
-        wr_plane = [plane_of(a, TAB_W + WG_W, PLANE_W) for a in range(PASSES)]
-
-        half_gain = keep.tile([P, PACK], F32, name="half_gain", align_bytes=64)
-        nc.vector.tensor_scalar(out=half_gain[:], in0=gain_sb[:], scalar1=0.5, scalar2=0.0, op0=ALU.mult, op1=ALU.add)
         v_words = {}
 
         def gather_words(a, s, words):
-            nc.vector.tensor_copy(out=words[:], in_=table[a][:].bitcast(U32).indirect(idx[:, s * COLS : (s + 1) * COLS]))
+            offsets = idx[:, s * HALF // 16 : (s + 1) * HALF // 16]
+            nc.vector.tensor_copy(out=words[:], in_=table[a][:].bitcast(U32).indirect(offsets))
             v_words[a, s] = words
 
         def picked(a, entries):
             s = entries.start // HALF
             return v_words[a, s][:, entries.start - s * HALF : entries.stop - s * HALF].bitcast(FP8X4)
 
-        for s in range(HALVES):
-            gather_words(0, s, placed(f"v_words0{s}", HALF, U32, (84 + 2 * s) * KB))
-        raws.append(halves(load_rows(wp, 0, "wp_raw0", 20 * KB)))
-        raws.append(halves(load_rows(wp, 1, "wp_raw1", 28 * KB)))
+        for s in range(2):
+            gather_words(0, s, placed(f"v_words0{s}", HALF, U32, 86 + 2 * s))
+        wc_raw.append(load_whole(wc, 1, "wc_raw1", 20))
+        wp_raw = [load_whole(wp, 0, "wp_raw0", 28)]
         wg_codes = keep.tile([P, PASSES, 2 * H], U8, name="wg_codes", align_bytes=64)
         nc.vector.tensor_copy(
             out=wg_codes[:].bitcast(U16).rearrange("p a (t n i) -> p a n t i", t=PACK, i=8),
             in_=wg_raw[:].bitcast(U16).rearrange("p a (n i t) -> p a n t i", t=PACK, i=8),
         )
-        windows.append(zeroed_window(3, 56 * KB, nc.vector))
-        for s in range(HALVES):
-            gather_words(1, s, keep.tile([P, HALF], U32, name=f"v_words1{s}", align_bytes=64))
+        windows.append(zeroed_window(3, 56, nc.gpsimd))
+        for s in range(2):
+            gather_words(1, s, kept(f"v_words1{s}", HALF, U32))
+        wp_raw.append([load_half(wp, 1, u, "wp_raw1", 4 * u) for u in range(2)])
 
-        def times_table(acc, lhsT, lhsT_scale, a, entries, start, stop):
+        def interleaved(grouped):
+            return grouped.rearrange("p (n i j) -> p n j i", i=4, j=PACK)
+
+        def mx_tiles(name, width):
+            return kept(name + "_codes", width, U32), kept(name + "_plane", width, U8)
+
+        def quantize(tiles, lo, hi, grouped):
+            nc.vector.quantize_mx(out=tiles[0][:, lo:hi].bitcast(FP8X4), scales=tiles[1][:, lo:hi], in_=grouped)
+
+        w_bf = placed("w_bf", ROWS, BF16, 8)
+
+        def quantize_weight(raw, name):
+            tiles = mx_tiles(name, H)
+            for u in range(2):
+                nc.vector.tensor_copy(out=interleaved(w_bf[:, u * 1024 : (u + 1) * 1024]), in_=raw[u])
+            for u in range(2):
+                quantize(tiles, u * QUARTER, (u + 1) * QUARTER, w_bf[:, u * 1024 : (u + 1) * 1024])
+            return tiles
+
+        def table_moving(acc, lhsT, lhsT_scale, a, entries, start, stop):
             nc.tensor.matmul_mx(
-                out=acc,
-                lhsT=lhsT,
-                lhsT_scale=lhsT_scale,
-                rhs=picked(a, entries),
-                rhs_scale=v_plane[a][:, entries],
-                start=start,
-                stop=stop,
+                out=acc, lhsT=lhsT, lhsT_scale=lhsT_scale, rhs=picked(a, entries), rhs_scale=v_plane[a][:, entries],
+                start=start, stop=stop,
             )
 
-        def bank_tile(name, bank):
-            return psum.tile([P, HALF], F32, name=name, offset=bank * BANK)
+        def table_stationary(acc, tiles, a, b, cols, start, stop):
+            entries = slice(b * P, (b + 1) * P)
+            nc.tensor.matmul_mx(
+                out=acc[:, cols], lhsT=picked(a, entries), lhsT_scale=v_plane[a][:, entries],
+                rhs=tiles[0][:, cols].bitcast(FP8X4), rhs_scale=tiles[1][:, cols], start=start, stop=stop,
+            )
 
-        def product(quantized, b, name, bank):
+        def product(quantized, b, name, bank, pieces=1):
             acc = bank_tile(f"{name}{b}", bank)
-            cols = slice(b * P, (b + 1) * P)
-            for a in range(PASSES):
-                codes, plane = quantized[a]
-                nc.tensor.matmul_mx(
-                    out=acc[:],
-                    lhsT=picked(a, cols),
-                    lhsT_scale=v_plane[a][:, cols],
-                    rhs=codes[:].bitcast(FP8X4),
-                    rhs_scale=plane[:],
-                    start=a == 0,
-                    stop=a == PASSES - 1,
-                )
+            table_stationary(acc, quantized[0], 0, b, slice(0, H), True, False)
+            for u in range(pieces):
+                cols = slice(u * H // pieces, (u + 1) * H // pieces)
+                table_stationary(acc, quantized[1], 1, b, cols, False, u == pieces - 1)
             return acc
 
-        def gate(s, t, bank, g):
-            acc = bank_tile(f"g{s}_{t}", bank)
+        def by_fours(tile_ap, t):
+            return tile_ap.rearrange("p (n t i) -> p n t i", t=PACK, i=4)[:, :, t, :]
+
+        def fours(ap):
+            return ap.rearrange("p (n i) -> p n i", i=4)
+
+        def gate(lo, hi, t, bank, dst):
+            acc = bank_tile(f"g{lo}_{t}", bank)[:, 0 : hi - lo]
             for a in range(PASSES):
-                times_table(
-                    acc[:],
-                    wg_codes[:, a, t * 2 * P : (t + 1) * 2 * P].bitcast(FP4X4),
-                    wg_plane[a][:, t * P : (t + 1) * P],
-                    a, slice(s * HALF, (s + 1) * HALF), a == 0, a == PASSES - 1,
+                table_moving(
+                    acc, wg_codes[:, a, t * 2 * P : (t + 1) * 2 * P].bitcast(FP4X4),
+                    wg_plane[a][:, t * P : (t + 1) * P], a, slice(lo, hi), a == 0, a == PASSES - 1,
                 )
-            nc.scalar.activation(out=g, in_=acc[:], func=ACT.Tanh, scale=0.5)
-            return g
+            nc.scalar.activation(out=dst, in_=fours(acc), func=ACT.Sigmoid)
 
-        def scale_gates(gates, scaled, lo, hi):
-            for t in range(PACK):
-                nc.scalar.activation(
-                    out=scaled[:].rearrange("p (n t i) -> p n t i", t=PACK, i=4)[:, :, t, :],
-                    in_=gates[t][:, lo:hi].rearrange("p (n i) -> p n i", i=4),
-                    func=ACT.Identity,
-                    scale=half_gain[:, t : t + 1],
-                    bias=half_gain[:, t : t + 1],
-                )
-
-        def leave_dealt(dst, acc, func, scale):
-            nc.scalar.activation(
-                out=dst.rearrange("p (t m) -> p t m", t=PACK),
-                in_=acc[:].rearrange("p (m t) -> p t m", t=PACK),
-                func=func,
-                scale=scale,
-            )
-
-        def candidate(b, bank, c):
-            leave_dealt(c, product(wc_q, b, "c", bank), ACT.Tanh, 1.0)
-            return c
-
-        def turn(diff, rows, opens):
-            for t in range(PACK):
-                cols = slice(t * P, (t + 1) * P)
-                nc.tensor.matmul(
-                    out=diff[:, cols], lhsT=rows[:, cols], rhs=ident[:], is_transpose=True,
-                    start=opens and t == 0, stop=not opens and t == PACK - 1,
-                )
-
-        def open_difference(c, b, bank):
-            diff = bank_tile(f"diff{b}", bank)
-            turn(diff, c, True)
-            return diff
-
-        def close_difference(diff, acc, neg, pieces=1):
+        def leave_dealt(dst, acc, func, scale, pieces=1):
             step = PACK // pieces
             for lo in range(0, PACK, step):
                 nc.scalar.activation(
-                    out=neg.rearrange("p (t m) -> p t m", t=PACK)[:, lo : lo + step],
+                    out=dst.rearrange("p (t m) -> p t m", t=PACK)[:, lo : lo + step],
                     in_=acc[:].rearrange("p (m t) -> p t m", t=PACK)[:, lo : lo + step],
-                    func=ACT.Copy,
-                    scale=-1.0,
+                    func=func, scale=scale,
                 )
-            turn(diff, neg, False)
-            return diff
+            return dst
 
-        def gated(diff, scaled, h_bf, k):
-            cols = slice(k * HALF, (k + 1) * HALF)
-            nc.vector.tensor_tensor(
-                out=h_bf[:, cols].rearrange("p (n i t) -> p n t i", i=4, t=PACK),
-                in0=diff[:].rearrange("p (t n i) -> p n t i", t=PACK, i=4),
-                in1=scaled.rearrange("p (n t i) -> p n t i", t=PACK, i=4),
-                op=ALU.mult,
+        def turn(dst, rows, t, start, stop):
+            nc.tensor.matmul(
+                out=dst, lhsT=rows[:, t * P : (t + 1) * P], rhs=ident[:], is_transpose=True, start=start, stop=stop
             )
 
-        early = keep.tile([P, PACK * HALF], F32, name="early", align_bytes=64)
-        gates = [[gate(0, t, t, placed(f"gate{t}", HALF, F32, (88 + 2 * t) * KB)[:]) for t in range(PACK)]]
-        w_bf = placed("w_bf", ROWS, BF16, 8 * KB)
-        wc_q = [quantize_weight(raws[0], "wc0", w_bf)]
-        wo_raw = load_halves(wo, 0, "wo_raw", 132 * KB)
-        wc_q.append(quantize_weight(raws[1], "wc1", w_bf))
-        cands = [placed(f"cand{b}", H, F32, (107 + 2 * b) * KB) for b in range(PACK)]
-        diffs = [open_difference(candidate(b, b, cands[b][:]), b, PACK + b) for b in range(PACK)]
-        scaled0 = placed("scaled0", PACK * HALF, F32, 72 * KB)
-        scale_gates(gates[0], scaled0, 0, HALF)
-        wp_q = [quantize_weight(raws[2], "wp0", w_bf)]
-        wr_codes = placed("wr_codes", PASSES * N, I32, 140 * KB)
+        def gated(engine, h_bf, in0, in1):
+            engine.tensor_tensor(
+                out=h_bf.rearrange("p (n i t) -> p n t i", i=4, t=PACK), in0=in0,
+                in1=in1.rearrange("p (n t i) -> p n t i", t=PACK, i=4), op=ALU.mult,
+            )
+
+        gates0 = [placed(f"gate{t}", HALF, F32, 90 + 2 * t) for t in range(PACK)]
+        for t in range(PACK):
+            gate(0, HALF, t, t, fours(gates0[t][:]))
+        gates1 = [kept(f"gates1{q}", PACK * QUARTER, F32) for q in range(2)]
+        third, fourth = (HALF, HALF + QUARTER), (HALF + QUARTER, S)
+        for t in range(PACK):
+            gate(*third, t, t, by_fours(gates1[0][:], t))
+        wc_q = [quantize_weight(wc_raw[0], "wc0")]
+        wo_raw = [load_half(wo, 0, u, "wo_raw", 132 + 4 * u) for u in range(2)]
+        wc_q.append(quantize_weight(wc_raw[1], "wc1"))
+        cands = [
+            leave_dealt(placed(f"cand{b}", H, F32, 107 + 2 * b)[:], product(wc_q, b, "c", b), ACT.Tanh, 1.0)
+            for b in range(PACK)
+        ]
+        scaled0 = placed("scaled0", PACK * HALF, F32, 20)
+        for t in range(PACK):
+            nc.scalar.activation(
+                out=by_fours(scaled0[:], t), in_=fours(gates0[t][:]), func=ACT.Copy, scale=gains[:, t : t + 1]
+            )
+        wp_q = [quantize_weight(wp_raw[0], "wp0")]
+        wr_codes = placed("wr_codes", PASSES * N, I32, 28)
         nc.sync.dma_start(
             out=wr_codes[:].rearrange("p (a e) -> p a e", a=PASSES),
             in_=wr_words.rearrange("a p e i -> p a (e i)").bitcast(I32),
         )
-        wgo_sb = placed("wgo_sb", S, F32, 144 * KB)
+        wgo_sb = placed("wgo_sb", S, F32, 32)
         nc.sync.dma_start(out=wgo_sb[:], in_=wgo)
-        wp_q.append(quantize_weight(raws[3], "wp1", w_bf))
-        wo_q = quantize_weight(wo_raw, "wo", w_bf)
+        wp_q.append(quantize_weight(wp_raw[1], "wp1"))
+        wo_q = quantize_weight(wo_raw, "wo")
 
-        def new_state(h_q, s, c, bank, y, lo=0, hi=HALF):
-            acc = bank_tile(f"y{s}_{c}_{lo}", bank)[:, lo:hi]
+        def new_state(h_q, c, bank, lo, hi):
+            acc = bank_tile(f"y{c}_{lo}", bank)[:, 0 : hi - lo]
             cols = slice(c * P, (c + 1) * P)
             for a in range(PASSES):
-                times_table(
-                    acc,
-                    wr_codes[:, a * N + c * P : a * N + (c + 1) * P].bitcast(FP8X4),
-                    wr_plane[a][:, cols],
-                    a, slice(s * HALF + lo, s * HALF + hi), a == 0, False,
+                table_moving(
+                    acc, wr_codes[:, a * N + c * P : a * N + (c + 1) * P].bitcast(FP8X4), wr_plane[a][:, cols],
+                    a, slice(lo, hi), a == 0, False,
                 )
             nc.tensor.matmul_mx(
-                out=acc,
-                lhsT=wo_q[0][:, cols].bitcast(FP8X4),
-                lhsT_scale=wo_q[1][:, cols],
-                rhs=h_q[0][:, lo:hi].bitcast(FP8X4),
-                rhs_scale=h_q[1][:, lo:hi],
-                start=False,
-                stop=True,
+                out=acc, lhsT=wo_q[0][:, cols].bitcast(FP8X4), lhsT_scale=wo_q[1][:, cols],
+                rhs=h_q[0][:, lo % HALF : lo % HALF + hi - lo].bitcast(FP8X4),
+                rhs_scale=h_q[1][:, lo % HALF : lo % HALF + hi - lo], start=False, stop=True,
             )
-            nc.scalar.copy(out=y[:, lo:hi], in_=acc)
+            return acc
+
+        def to_sbuf(acc, y):
+            nc.scalar.copy(out=y, in_=acc)
             return y
 
-        def y_tile(s, c):
-            return ring.tile([P, HALF], F32, name=f"y_sb{s}_{c}", tag="y", bufs=4)
+        def y_tile(c, lo, hi):
+            return ring.tile([P, HALF], F32, name=f"y_sb{c}_{lo}", tag="y", bufs=4)[:, 0 : hi - lo]
 
-        def scatter(y, s, c, lo=0, hi=HALF):
-            lo_all, hi_all = s * HALF + lo, s * HALF + hi
+        def weigh(engine, y, c, lo, hi, weighted=None):
+            weighted = kept(f"weighted{c}_{lo}", hi - lo, F32) if weighted is None else weighted
+            engine.tensor_tensor(out=weighted[:], in0=y, in1=wgo_sb[:, lo:hi], op=ALU.mult)
+            return weighted[:]
+
+        def scatter_copy(weighted, c, lo, hi):
+            nc.vector.tensor_copy(out=windows[c][:].indirect(idx2[:, lo // 16 : hi // 16]), in_=weighted)
+
+        def scatter_weigh(y, c, lo, hi):
             nc.vector.tensor_tensor(
-                out=windows[c][:].indirect(idx2[:, lo_all // 16 : hi_all // 16]),
-                in0=y[:, lo:hi],
-                in1=wgo_sb[:, lo_all:hi_all],
-                op=ALU.mult,
+                out=windows[c][:].indirect(idx2[:, lo // 16 : hi // 16]), in0=y, in1=wgo_sb[:, lo:hi], op=ALU.mult
             )
 
-        present = [product(wp_q, b, "p", b) for b in range(PACK)]
-        h_bf0 = placed("h_bf0", PACK * HALF, BF16, 64 * KB)
+        h_bf0 = placed("h_bf0", PACK * HALF, BF16, 64)
         h0 = mx_tiles("h0", HALF)
+        diffs, present = {}, {}
         for b in range(PACK):
-            if b == PACK - 1:
-                neg = placed(f"neg{b}", H, F32, 96 * KB)
-            else:
-                neg = ring.tile([P, H], F32, name=f"neg{b}", tag="neg", bufs=3)
-            gated(close_difference(diffs[b], present[b], neg[:], 2 if b in (0, PACK - 1) else 1), scaled0[:, b * HALF : (b + 1) * HALF], h_bf0, b)
-            if b % 2 == 1:
-                quantize_part(h0, h_bf0[:, (b // 2) * 1024 : (b // 2 + 1) * 1024], b // 2)
-        first = [
-            new_state(h0, 0, 0, 0, placed("y_first", HALF, F32, 96 * KB), 0, 256),
-            new_state(h0, 0, 0, 1, y_tile(0, 0), 256, HALF),
-        ]
-        ys = [new_state(h0, 0, c, (c + 1) % PACK, y_tile(0, c)) for c in range(1, CHUNKS)]
-        for u in range(2):
-            scatter(first[u], 0, 0, u * 256, (u + 1) * 256)
-        for c in range(1, CHUNKS):
-            scatter(ys[c - 1], 0, c)
-        gates.append([gate(1, t, PACK + t, early[:, t * HALF : (t + 1) * HALF]) for t in range(PACK)])
+            if b % 2 == 0:
+                for k in (b, b + 1):
+                    diffs[k] = bank_tile(f"diff{k}", PACK + k)
+                    for t in range(PACK):
+                        turn(diffs[k][:, t * P : (t + 1) * P], cands[k], t, t == 0, False)
+            if b != 1:
+                for k in (0, 1) if b == 0 else (b,):
+                    present[k] = product(wp_q, k, "p", k % 2, 2 - b // 2)
+            neg = leave_dealt(ring.tile([P, H], F32, name=f"neg{b}", tag="neg")[:], present[b], ACT.Copy, -1.0, 2 if b == 0 else 1)
+            for t in range(PACK):
+                turn(diffs[b][:, t * P : (t + 1) * P], neg, t, False, t == PACK - 1)
+            gated(
+                nc.vector, h_bf0[:, b * HALF : (b + 1) * HALF],
+                diffs[b][:].rearrange("p (t n i) -> p n t i", t=PACK, i=4), scaled0[:, b * HALF : (b + 1) * HALF],
+            )
+            if b == 1:
+                quantize(h0, 0, QUARTER, h_bf0[:, 0:1024])
+        first = weigh(nc.vector, new_state(h0, 0, 2, 0, QUARTER), 0, 0, QUARTER)
+        quantize(h0, QUARTER, HALF, h_bf0[:, 1024:2048])
+        scatter_copy(first, 0, 0, QUARTER)
 
-        cands1 = placed("cands1", PACK * H, F32, 40 * KB)
-        diffs = [
-            open_difference(candidate(PACK + k, PACK + k, cands1[:, k * H : (k + 1) * H]), PACK + k, PACK + k)
-            for k in range(PACK)
-        ]
-        scaled1 = placed("scaled1", PACK * HALF, F32, 64 * KB)
-        scale_gates(gates[1], scaled1, 0, HALF)
-        present = [product(wp_q, PACK + k, "p", (k + 1) % PACK) for k in range(PACK)]
-        h_bf1 = keep.tile([P, PACK * HALF], BF16, name="h_bf1", align_bytes=64)
+        def weighed_piece(c, bank, lo, hi, weighted=None):
+            y = to_sbuf(new_state(h0, c, bank, lo, hi), y_tile(c, lo, hi))
+            scatter_copy(weigh(nc.gpsimd, y, c, lo, hi, weighted), c, lo, hi)
+
+        h_bf1 = kept("h_bf1", PACK * QUARTER, BF16)
         h1 = mx_tiles("h1", HALF)
-        for k in range(PACK):
-            neg = placed(f"neg{PACK + k}", H, F32, (48 + 2 * k) * KB)
-            gated(close_difference(diffs[k], present[k], neg[:]), scaled1[:, k * HALF : (k + 1) * HALF], h_bf1, k)
-            if k >= 2:
-                quantize_part(h1, h_bf1[:, (k - 2) * 1024 : (k - 1) * 1024], k - 2)
-        first = [
-            new_state(h1, 1, 0, 1, placed("y_first1", HALF, F32, 54 * KB), 0, 256),
-            new_state(h1, 1, 0, 2, y_tile(1, 0), 256, HALF),
-        ]
-        for u in range(2):
-            scatter(first[u], 1, 0, u * 256, (u + 1) * 256)
-        nc.sync.dma_start(out=out[0:P, :], in_=windows[0][:])
-        for c in range(1, CHUNKS):
-            scatter(new_state(h1, 1, c, (c + 2) % PACK, y_tile(1, c)), 1, c)
+
+        def candidates(q):
+            blocks = (PACK + 2 * q, PACK + 2 * q + 1)
+            return [
+                leave_dealt(placed(f"cand{b}", H, F32, 107 + 2 * (b % PACK))[:], product(wc_q, b, "c", 4 + b % 2), ACT.Tanh, 1.0)
+                for b in blocks
+            ]
+
+        def difference(q, cands, first_bank):
+            banks = [bank_tile(f"diff1{q}_{u}", first_bank + u) for u in range(2)]
+
+            def place(t, k):
+                lo = (t % 2) * QUARTER + k * P
+                return banks[t // 2][:, lo : lo + P]
+
+            for k in range(2):
+                b = PACK + 2 * q + k
+                neg = leave_dealt(
+                    ring.tile([P, H], F32, name=f"neg{b}", tag="neg")[:], product(wp_q, b, "p", k), ACT.Copy, -1.0
+                )
+                for t in range(PACK):
+                    turn(place(t, k), cands[k], t, k == 0 and t % 2 == 0, False)
+                for t in range(PACK):
+                    turn(place(t, k), neg, t, False, k == 1 and t % 2 == 1)
+            return banks
+
+        def gate_difference(q, banks):
+            scaled = placed(f"scaled1{q}", PACK * QUARTER, F32, 36 + 4 * q)
+            for t in range(PACK):
+                nc.scalar.activation(
+                    out=by_fours(scaled[:], t),
+                    in_=fours(banks[t // 2][:, (t % 2) * QUARTER : (t % 2 + 1) * QUARTER]),
+                    func=ACT.Copy, scale=gains[:, t : t + 1],
+                )
+            nc.gpsimd.tensor_tensor(
+                out=h_bf1[:].rearrange("p (n i t) -> p n i t", i=4, t=PACK),
+                in0=scaled[:].rearrange("p (n t i) -> p n i t", t=PACK, i=4),
+                in1=gates1[q][:].rearrange("p (n t i) -> p n i t", t=PACK, i=4),
+                op=ALU.mult,
+            )
+            quantize(h1, q * QUARTER, (q + 1) * QUARTER, h_bf1[:])
+
+        def fused_piece(c, bank, lo, hi, y=None):
+            y = y_tile(c, lo, hi) if y is None else y
+            scatter_weigh(to_sbuf(new_state(h1, c, bank, lo, hi), y), c, lo, hi)
+
+        def store(c):
             nc.sync.dma_start(out=out[c * P : (c + 1) * P, :], in_=windows[c][:])
+
+        cands = candidates(0)
+        weighed_piece(0, 3, QUARTER, HALF)
+        weighed_piece(1, 2, 0, HALF)
+        weighed_piece(2, 3, 0, HALF)
+        y_last = to_sbuf(new_state(h0, 3, 2, 0, HALF), y_tile(3, 0, HALF))
+        scatter_copy(weigh(nc.gpsimd, y_last[:, 0:QUARTER], 3, 0, QUARTER), 3, 0, QUARTER)
+        gate_difference(0, difference(0, cands, 6))
+        held = placed("weighted_last", QUARTER, F32, 36)
+        scatter_copy(weigh(nc.gpsimd, y_last[:, QUARTER:HALF], 3, QUARTER, HALF, held), 3, QUARTER, HALF)
+        for t in range(PACK):
+            gate(*fourth, t, (4, 5, 0, 1)[t], by_fours(gates1[1][:], t))
+        cands = candidates(1)
+        gate_difference(1, difference(1, cands, 6))
+        scatter_copy(weigh(nc.vector, new_state(h1, 0, 3, *third), 0, *third, placed("weighted_third", QUARTER, F32, 36)), 0, *third)
+        fused_piece(1, 2, *third, placed("y_held", QUARTER, F32, 40)[:])
+        for c in range(2):
+            fused_piece(c, 4 + c, *fourth)
+            store(c)
+        for c in range(2, CHUNKS):
+            fused_piece(c, c - 2, HALF, S)
+            store(c)

@@ -108,6 +108,10 @@ def tile_list_gated_node_update_kernel(
         )
         wg_raw = arena.tile([P, PASSES, 2 * H // 4], I32, name="wg_raw", offset=56 * KB, align_bytes=64)
         nc.sync.dma_start(out=wg_raw[:], in_=wg_words.bitcast(I32).rearrange("a p w -> p a w"))
+        idx2 = lists.tile([P, S // 16], U16, name="idx2")
+        nc.sync.dma_start(idx2[:], offs2)
+        gains = kept("gains", PACK, F32)
+        nc.sync.dma_start(out=gains[:], in_=gain.rearrange("(p t) -> p t", t=PACK))
         table.append(load_table(1, 0))
 
         gathered = placed("gathered", PASSES * S, U8, 131)
@@ -125,10 +129,6 @@ def tile_list_gated_node_update_kernel(
         for r in range(4):
             nc.sync.dma_start(out=planes[r:P:32, :], in_=staged[TOP + r : P : 4, :])
         wc_raw = [load_whole(wc, 0, "wc_raw0", 132)]
-        idx2 = lists.tile([P, S // 16], U16, name="idx2")
-        nc.sync.dma_start(idx2[:], offs2)
-        gains = kept("gains", PACK, F32)
-        nc.sync.dma_start(out=gains[:], in_=gain.rearrange("(p t) -> p t", t=PACK))
 
         def plane_of(at, width, a):
             return planes[:, at + a * width : at + (a + 1) * width].bitcast(U8)
@@ -252,11 +252,17 @@ def tile_list_gated_node_update_kernel(
             leave_dealt(placed(f"cand{b}", H, F32, 107 + 2 * b)[:], product(wc_q, b, "c", b), ACT.Tanh, 1.0)
             for b in range(PACK)
         ]
-        scaled0 = placed("scaled0", PACK * HALF, F32, 20)
-        for t in range(PACK):
-            nc.scalar.activation(
-                out=by_fours(scaled0[:], t), in_=fours(gates0[t][:]), func=ACT.Copy, scale=gains[:, t : t + 1]
-            )
+
+        def scale_gates(q, kib):
+            scaled = placed(f"scaled0{q}", PACK * QUARTER, F32, kib)
+            for t in range(PACK):
+                nc.scalar.activation(
+                    out=by_fours(scaled[:], t), in_=fours(gates0[t][:, q * QUARTER : (q + 1) * QUARTER]),
+                    func=ACT.Copy, scale=gains[:, t : t + 1],
+                )
+            return scaled
+
+        scaled0 = [scale_gates(0, 72)]
         wp_q = [quantize_weight(wp_raw[0], "wp0")]
         wr_codes = placed("wr_codes", PASSES * N, I32, 28)
         nc.sync.dma_start(
@@ -305,32 +311,42 @@ def tile_list_gated_node_update_kernel(
 
         h_bf0 = placed("h_bf0", PACK * HALF, BF16, 64)
         h0 = mx_tiles("h0", HALF)
-        diffs, present = {}, {}
-        for b in range(PACK):
-            if b % 2 == 0:
-                for k in (b, b + 1):
-                    diffs[k] = bank_tile(f"diff{k}", PACK + k)
-                    for t in range(PACK):
-                        turn(diffs[k][:, t * P : (t + 1) * P], cands[k], t, t == 0, False)
-            if b != 1:
-                for k in (0, 1) if b == 0 else (b,):
-                    present[k] = product(wp_q, k, "p", k % 2, 2 - b // 2)
-            neg = leave_dealt(ring.tile([P, H], F32, name=f"neg{b}", tag="neg")[:], present[b], ACT.Copy, -1.0, 2 if b == 0 else 1)
+
+        def open_difference(b):
+            diff = bank_tile(f"diff{b}", PACK + b)
             for t in range(PACK):
-                turn(diffs[b][:, t * P : (t + 1) * P], neg, t, False, t == PACK - 1)
+                turn(diff[:, t * P : (t + 1) * P], cands[b], t, t == 0, False)
+            return diff
+
+        def negated(b, present, pieces=1):
+            return leave_dealt(placed(f"neg{b}", H, F32, 44 + 2 * b)[:], present, ACT.Copy, -1.0, pieces)
+
+        def gate_block(b, diff, neg):
+            for t in range(PACK):
+                turn(diff[:, t * P : (t + 1) * P], neg, t, False, t == PACK - 1)
             gated(
                 nc.vector, h_bf0[:, b * HALF : (b + 1) * HALF],
-                diffs[b][:].rearrange("p (t n i) -> p n t i", t=PACK, i=4), scaled0[:, b * HALF : (b + 1) * HALF],
+                diff[:].rearrange("p (t n i) -> p n t i", t=PACK, i=4),
+                scaled0[b // 2][:, b % 2 * HALF : (b % 2 + 1) * HALF],
             )
-            if b == 1:
-                quantize(h0, 0, QUARTER, h_bf0[:, 0:1024])
+
+        diffs = [open_difference(b) for b in range(2)]
+        present = [product(wp_q, b, "p", b, 2) for b in range(2)]
+        for b in range(2):
+            gate_block(b, diffs[b], negated(b, present[b], 2 - b))
+        quantize(h0, 0, QUARTER, h_bf0[:, 0:1024])
+        diffs = [open_difference(b) for b in range(2, PACK)]
+        negs = [negated(b, product(wp_q, b, "p", b - 2)) for b in range(2, PACK)]
+        scaled0.append(scale_gates(1, 41))
+        for b in range(2, PACK):
+            gate_block(b, diffs[b - 2], negs[b - 2])
         first = weigh(nc.vector, new_state(h0, 0, 2, 0, QUARTER), 0, 0, QUARTER)
         quantize(h0, QUARTER, HALF, h_bf0[:, 1024:2048])
         scatter_copy(first, 0, 0, QUARTER)
 
-        def weighed_piece(c, bank, lo, hi, weighted=None):
-            y = to_sbuf(new_state(h0, c, bank, lo, hi), y_tile(c, lo, hi))
-            scatter_copy(weigh(nc.gpsimd, y, c, lo, hi, weighted), c, lo, hi)
+        def weighed_piece(h_q, c, bank, lo, hi):
+            y = to_sbuf(new_state(h_q, c, bank, lo, hi), y_tile(c, lo, hi))
+            scatter_copy(weigh(nc.gpsimd, y, c, lo, hi), c, lo, hi)
 
         h_bf1 = kept("h_bf1", PACK * QUARTER, BF16)
         h1 = mx_tiles("h1", HALF)
@@ -361,7 +377,7 @@ def tile_list_gated_node_update_kernel(
             return banks
 
         def gate_difference(q, banks):
-            scaled = placed(f"scaled1{q}", PACK * QUARTER, F32, 36 + 4 * q)
+            scaled = placed(f"scaled1{q}", PACK * QUARTER, F32, 20 + 4 * q)
             for t in range(PACK):
                 nc.scalar.activation(
                     out=by_fours(scaled[:], t),
@@ -384,23 +400,25 @@ def tile_list_gated_node_update_kernel(
             nc.sync.dma_start(out=out[c * P : (c + 1) * P, :], in_=windows[c][:])
 
         cands = candidates(0)
-        weighed_piece(0, 3, QUARTER, HALF)
-        weighed_piece(1, 2, 0, HALF)
-        weighed_piece(2, 3, 0, HALF)
+        weighed_piece(h0, 0, 3, QUARTER, HALF)
+        weighed_piece(h0, 1, 2, 0, HALF)
+        weighed_piece(h0, 2, 3, 0, HALF)
         y_last = to_sbuf(new_state(h0, 3, 2, 0, HALF), y_tile(3, 0, HALF))
         scatter_copy(weigh(nc.gpsimd, y_last[:, 0:QUARTER], 3, 0, QUARTER), 3, 0, QUARTER)
         gate_difference(0, difference(0, cands, 6))
-        held = placed("weighted_last", QUARTER, F32, 36)
+        held = placed("weighted_last", QUARTER, F32, 20)
         scatter_copy(weigh(nc.gpsimd, y_last[:, QUARTER:HALF], 3, QUARTER, HALF, held), 3, QUARTER, HALF)
         for t in range(PACK):
             gate(*fourth, t, (4, 5, 0, 1)[t], by_fours(gates1[1][:], t))
         cands = candidates(1)
-        gate_difference(1, difference(1, cands, 6))
-        scatter_copy(weigh(nc.vector, new_state(h1, 0, 3, *third), 0, *third, placed("weighted_third", QUARTER, F32, 36)), 0, *third)
-        fused_piece(1, 2, *third, placed("y_held", QUARTER, F32, 40)[:])
-        for c in range(2):
-            fused_piece(c, 4 + c, *fourth)
+        banks = difference(1, cands, 6)
+        weighed_piece(h1, 0, 3, *third)
+        late = new_state(h1, 1, 2, *third)
+        scatter_copy(weigh(nc.vector, late, 1, *third, placed("weighted_third", QUARTER, F32, 20)), 1, *third)
+        gate_difference(1, banks)
+        fused_piece(2, 3, *third, placed("y_held", QUARTER, F32, 24)[:])
+        for c in range(3):
+            fused_piece(c, (4, 5, 0)[c], *fourth)
             store(c)
-        for c in range(2, CHUNKS):
-            fused_piece(c, c - 2, HALF, S)
-            store(c)
+        fused_piece(3, 1, HALF, S)
+        store(3)

@@ -31,8 +31,8 @@ SCALE_ROWS = 16
 TOP = P - SCALE_ROWS
 TAB_W, WG_W, WR_W = S // 4, H // 4, N // 4
 WG_AT = PASSES * TAB_W
-WR_AT = WG_AT + PASSES * WG_W
-PLANE_W = WR_AT + PASSES * WR_W
+PLANE_W = WG_AT + PASSES * WG_W
+QUADRANT = 32
 
 
 def tile_list_gated_node_update_kernel(
@@ -58,9 +58,8 @@ def tile_list_gated_node_update_kernel(
         def side_by_side(scales):
             return scales.bitcast(I32).rearrange("a q w -> q a w")
 
-        tab_rows = [placed(f"tab_rows{a}", T // 4, I32, 80 + 4 * a) for a in range(PASSES)]
-        for rows in tab_rows:
-            nc.gpsimd.memset(rows[0:TOP, :], 0)
+        tab_rows = placed("tab_rows", T // 4, I32, 15.5)
+        nc.gpsimd.memset(tab_rows[0 : TOP - SCALE_ROWS, :], 0)
         wg_rows = placed("wg_rows", PASSES * WG_W, I32, 88)
         nc.gpsimd.memset(wg_rows[0:TOP, :], 0)
         ident = kept("ident", P, F32)
@@ -77,8 +76,7 @@ def tile_list_gated_node_update_kernel(
 
         idx = lists.tile([P, S // 16], U16, name="idx")
         nc.sync.dma_start(idx[:], offs)
-        for a in range(PASSES):
-            nc.sync.dma_start(out=tab_rows[a][TOP:P, :], in_=tab_scales[a].bitcast(I32))
+        nc.sync.dma_start(out=tab_rows[TOP - SCALE_ROWS : P, :], in_=tab_scales.bitcast(I32).rearrange("a q w -> (a q) w"))
 
         def load_table(a, kib):
             words = placed(f"table{a}", T, I32, kib)
@@ -102,30 +100,27 @@ def tile_list_gated_node_update_kernel(
 
         table = [load_table(0, 20)]
         nc.sync.dma_start(out=wg_rows[TOP:P, :].rearrange("q (a w) -> q a w", a=PASSES), in_=side_by_side(wg_scales))
-        staged = kept("staged", PLANE_W, I32)
-        nc.sync.dma_start(
-            out=staged[TOP:P, WR_AT:].rearrange("q (a w) -> q a w", a=PASSES), in_=side_by_side(wr_scales)
-        )
         wg_raw = arena.tile([P, PASSES, 2 * H // 4], I32, name="wg_raw", offset=56 * KB, align_bytes=64)
         nc.sync.dma_start(out=wg_raw[:], in_=wg_words.bitcast(I32).rearrange("a p w -> p a w"))
         idx2 = lists.tile([P, S // 16], U16, name="idx2")
         nc.sync.dma_start(idx2[:], offs2)
         gains = kept("gains", PACK, F32)
         nc.sync.dma_start(out=gains[:], in_=gain.rearrange("(p t) -> p t", t=PACK))
-        table.append(load_table(1, 0))
 
-        gathered = placed("gathered", PASSES * S, U8, 131)
-        for a in range(PASSES):
-            nc.vector.tensor_copy(
-                out=gathered[:, a * S : (a + 1) * S], in_=tab_rows[a][:].bitcast(U8).indirect(idx[:])
-            )
+        gathered = placed("gathered", S, U8, 131.5)
+        nc.vector.tensor_copy(out=gathered[:], in_=tab_rows[:].bitcast(U8).indirect(idx[:]))
+        staged = kept("staged", PLANE_W, I32)
+        nc.sync.dma_start(out=staged[TOP:P, 0:TAB_W], in_=gathered[TOP - SCALE_ROWS : TOP, :].bitcast(I32))
+        table.append(load_table(1, 0))
         nc.vector.tensor_copy(
-            out=staged[:, WG_AT:WR_AT].bitcast(U8).rearrange("p (a t m) -> p a t m", a=PASSES, t=PACK),
+            out=staged[:, WG_AT:PLANE_W].bitcast(U8).rearrange("p (a t m) -> p a t m", a=PASSES, t=PACK),
             in_=wg_rows[:].bitcast(U8).rearrange("p (a m t) -> p a t m", a=PASSES, t=PACK),
         )
-        nc.vector.tensor_copy(out=staged[96:P, 0:WG_AT], in_=gathered[96:P, :].bitcast(I32))
+        nc.vector.tensor_copy(
+            out=staged[TOP - SCALE_ROWS : P, TAB_W:WG_AT], in_=gathered[TOP - SCALE_ROWS : P, :].bitcast(I32)
+        )
         windows.append(zeroed_window(2, 124, nc.gpsimd))
-        planes = placed("planes", PLANE_W, I32, 80)
+        planes = placed("planes", PLANE_W, I32, 16)
         for r in range(4):
             nc.sync.dma_start(out=planes[r:P:32, :], in_=staged[TOP + r : P : 4, :])
         wc_raw = [load_whole(wc, 0, "wc_raw0", 132)]
@@ -135,7 +130,6 @@ def tile_list_gated_node_update_kernel(
 
         v_plane = [plane_of(0, TAB_W, a) for a in range(PASSES)]
         wg_plane = [plane_of(WG_AT, WG_W, a) for a in range(PASSES)]
-        wr_plane = [plane_of(WR_AT, WR_W, a) for a in range(PASSES)]
 
         v_words = {}
 
@@ -263,6 +257,12 @@ def tile_list_gated_node_update_kernel(
             return scaled
 
         scaled0 = [scale_gates(0, 72)]
+        wr_planes = placed("wr_planes", WR_W, I32, 20)
+        for q in range(P // QUADRANT):
+            nc.sync.dma_start(
+                out=wr_planes[QUADRANT * q + 8 : QUADRANT * q + 16, :],
+                in_=wr_scales.bitcast(I32)[:, 4 * q : 4 * q + 4, :],
+            )
         wp_q = [quantize_weight(wp_raw[0], "wp0")]
         wr_codes = placed("wr_codes", PASSES * N, I32, 28)
         nc.sync.dma_start(
@@ -279,7 +279,7 @@ def tile_list_gated_node_update_kernel(
             cols = slice(c * P, (c + 1) * P)
             for a in range(PASSES):
                 table_moving(
-                    acc, wr_codes[:, a * N + c * P : a * N + (c + 1) * P].bitcast(FP8X4), wr_plane[a][:, cols],
+                    acc, wr_codes[:, a * N + c * P : a * N + (c + 1) * P].bitcast(FP8X4), wr_planes[8 + 4 * a : P, :].bitcast(U8)[:, cols],
                     a, slice(lo, hi), a == 0, False,
                 )
             nc.tensor.matmul_mx(
@@ -377,7 +377,7 @@ def tile_list_gated_node_update_kernel(
             return banks
 
         def gate_difference(q, banks):
-            scaled = placed(f"scaled1{q}", PACK * QUARTER, F32, 20 + 4 * q)
+            scaled = placed(f"scaled1{q}", PACK * QUARTER, F32, 36 + 4 * q)
             for t in range(PACK):
                 nc.scalar.activation(
                     out=by_fours(scaled[:], t),
@@ -406,7 +406,7 @@ def tile_list_gated_node_update_kernel(
         y_last = to_sbuf(new_state(h0, 3, 2, 0, HALF), y_tile(3, 0, HALF))
         scatter_copy(weigh(nc.gpsimd, y_last[:, 0:QUARTER], 3, 0, QUARTER), 3, 0, QUARTER)
         gate_difference(0, difference(0, cands, 6))
-        held = placed("weighted_last", QUARTER, F32, 20)
+        held = placed("weighted_last", QUARTER, F32, 36)
         scatter_copy(weigh(nc.gpsimd, y_last[:, QUARTER:HALF], 3, QUARTER, HALF, held), 3, QUARTER, HALF)
         for t in range(PACK):
             gate(*fourth, t, (4, 5, 0, 1)[t], by_fours(gates1[1][:], t))
@@ -414,9 +414,9 @@ def tile_list_gated_node_update_kernel(
         banks = difference(1, cands, 6)
         weighed_piece(h1, 0, 3, *third)
         late = new_state(h1, 1, 2, *third)
-        scatter_copy(weigh(nc.vector, late, 1, *third, placed("weighted_third", QUARTER, F32, 20)), 1, *third)
+        scatter_copy(weigh(nc.vector, late, 1, *third, placed("weighted_third", QUARTER, F32, 36)), 1, *third)
         gate_difference(1, banks)
-        fused_piece(2, 3, *third, placed("y_held", QUARTER, F32, 24)[:])
+        fused_piece(2, 3, *third, placed("y_held", QUARTER, F32, 40)[:])
         for c in range(3):
             fused_piece(c, (4, 5, 0)[c], *fourth)
             store(c)

@@ -60,7 +60,7 @@ def tile_list_gated_node_update_kernel(
 
         tab_rows = placed("tab_rows", T // 4, I32, 15.5)
         nc.gpsimd.memset(tab_rows[0 : TOP - SCALE_ROWS, :], 0)
-        wg_rows = placed("wg_rows", PASSES * WG_W, I32, 88)
+        wg_rows = placed("wg_rows", PASSES * WG_W, I32, 60)
         nc.gpsimd.memset(wg_rows[0:TOP, :], 0)
         ident = kept("ident", P, F32)
         make_identity(nc, ident[:])
@@ -72,7 +72,6 @@ def tile_list_gated_node_update_kernel(
             return window
 
         windows = [zeroed_window(0, 99, nc.vector, (slice(0, T2 - 1), slice(T2 - 1, T2)))]
-        windows.append(zeroed_window(1, 116, nc.gpsimd))
 
         idx = lists.tile([P, S // 16], U16, name="idx")
         nc.sync.dma_start(idx[:], offs)
@@ -98,16 +97,16 @@ def tile_list_gated_node_update_kernel(
             )
             return raw[:].rearrange("p (j n i) -> p n j i", i=4, j=PACK)
 
-        table = [load_table(0, 20)]
         nc.sync.dma_start(out=wg_rows[TOP:P, :].rearrange("q (a w) -> q a w", a=PASSES), in_=side_by_side(wg_scales))
-        wg_raw = arena.tile([P, PASSES, 2 * H // 4], I32, name="wg_raw", offset=56 * KB, align_bytes=64)
+        table = [load_table(0, 27)]
+        wg_raw = arena.tile([P, PASSES, 2 * H // 4], I32, name="wg_raw", offset=58 * KB, align_bytes=64)
         nc.sync.dma_start(out=wg_raw[:], in_=wg_words.bitcast(I32).rearrange("a p w -> p a w"))
         idx2 = lists.tile([P, S // 16], U16, name="idx2")
         nc.sync.dma_start(idx2[:], offs2)
         gains = kept("gains", PACK, F32)
         nc.sync.dma_start(out=gains[:], in_=gain.rearrange("(p t) -> p t", t=PACK))
 
-        gathered = placed("gathered", S, U8, 131.5)
+        gathered = placed("gathered", S, U8, 139.5)
         nc.vector.tensor_copy(out=gathered[:], in_=tab_rows[:].bitcast(U8).indirect(idx[:]))
         staged = kept("staged", PLANE_W, I32)
         nc.sync.dma_start(out=staged[TOP:P, 0:TAB_W], in_=gathered[TOP - SCALE_ROWS : TOP, :].bitcast(I32))
@@ -119,11 +118,12 @@ def tile_list_gated_node_update_kernel(
         nc.vector.tensor_copy(
             out=staged[TOP - SCALE_ROWS : P, TAB_W:WG_AT], in_=gathered[TOP - SCALE_ROWS : P, :].bitcast(I32)
         )
-        windows.append(zeroed_window(2, 124, nc.gpsimd))
+        windows.append(zeroed_window(1, 19, nc.vector))
+        windows.append(zeroed_window(2, 60, nc.vector))
         planes = placed("planes", PLANE_W, I32, 16)
         for r in range(4):
             nc.sync.dma_start(out=planes[r:P:32, :], in_=staged[TOP + r : P : 4, :])
-        wc_raw = [load_whole(wc, 0, "wc_raw0", 132)]
+        wc_raw = [load_whole(wc, a, f"wc_raw{a}", 132 + 8 * a) for a in range(PASSES)]
 
         def plane_of(at, width, a):
             return planes[:, at + a * width : at + (a + 1) * width].bitcast(U8)
@@ -144,17 +144,15 @@ def tile_list_gated_node_update_kernel(
 
         for s in range(2):
             gather_words(0, s, placed(f"v_words0{s}", HALF, U32, 86 + 2 * s))
-        wc_raw.append(load_whole(wc, 1, "wc_raw1", 20))
-        wp_raw = [load_whole(wp, 0, "wp_raw0", 28)]
+        wp_raw = [load_whole(wp, 0, "wp_raw0", 27), [load_half(wp, 1, u, "wp_raw1", 35 + 4 * u) for u in range(2)]]
         wg_codes = keep.tile([P, PASSES, 2 * H], U8, name="wg_codes", align_bytes=64)
         nc.vector.tensor_copy(
             out=wg_codes[:].bitcast(U16).rearrange("p a (t n i) -> p a n t i", t=PACK, i=8),
             in_=wg_raw[:].bitcast(U16).rearrange("p a (n i t) -> p a n t i", t=PACK, i=8),
         )
-        windows.append(zeroed_window(3, 56, nc.gpsimd))
+        windows.append(zeroed_window(3, 52, nc.gpsimd))
         for s in range(2):
             gather_words(1, s, kept(f"v_words1{s}", HALF, U32))
-        wp_raw.append([load_half(wp, 1, u, "wp_raw1", 4 * u) for u in range(2)])
 
         def interleaved(grouped):
             return grouped.rearrange("p (n i j) -> p n j i", i=4, j=PACK)
@@ -257,19 +255,19 @@ def tile_list_gated_node_update_kernel(
             return scaled
 
         scaled0 = [scale_gates(0, 72)]
-        wr_planes = placed("wr_planes", WR_W, I32, 20)
+        wr_planes = placed("wr_planes", WR_W, I32, 140)
         for q in range(P // QUADRANT):
             nc.sync.dma_start(
                 out=wr_planes[QUADRANT * q + 8 : QUADRANT * q + 16, :],
                 in_=wr_scales.bitcast(I32)[:, 4 * q : 4 * q + 4, :],
             )
         wp_q = [quantize_weight(wp_raw[0], "wp0")]
-        wr_codes = placed("wr_codes", PASSES * N, I32, 28)
+        wr_codes = placed("wr_codes", PASSES * N, I32, 27)
         nc.sync.dma_start(
             out=wr_codes[:].rearrange("p (a e) -> p a e", a=PASSES),
             in_=wr_words.rearrange("a p e i -> p a (e i)").bitcast(I32),
         )
-        wgo_sb = placed("wgo_sb", S, F32, 32)
+        wgo_sb = placed("wgo_sb", S, F32, 31)
         nc.sync.dma_start(out=wgo_sb[:], in_=wgo)
         wp_q.append(quantize_weight(wp_raw[1], "wp1"))
         wo_q = quantize_weight(wo_raw, "wo")
@@ -309,7 +307,7 @@ def tile_list_gated_node_update_kernel(
                 out=windows[c][:].indirect(idx2[:, lo // 16 : hi // 16]), in0=y, in1=wgo_sb[:, lo:hi], op=ALU.mult
             )
 
-        h_bf0 = placed("h_bf0", PACK * HALF, BF16, 64)
+        h_bf0 = placed("h_bf0", PACK * HALF, BF16, 68)
         h0 = mx_tiles("h0", HALF)
 
         def open_difference(b):
@@ -331,16 +329,16 @@ def tile_list_gated_node_update_kernel(
             )
 
         diffs = [open_difference(b) for b in range(2)]
-        present = [product(wp_q, b, "p", b, 2) for b in range(2)]
+        present = [product(wp_q, b, "p", b, 2) for b in range(PACK)]
         for b in range(2):
             gate_block(b, diffs[b], negated(b, present[b], 2 - b))
         quantize(h0, 0, QUARTER, h_bf0[:, 0:1024])
         diffs = [open_difference(b) for b in range(2, PACK)]
-        negs = [negated(b, product(wp_q, b, "p", b - 2)) for b in range(2, PACK)]
+        negs = [negated(b, present[b]) for b in range(2, PACK)]
         scaled0.append(scale_gates(1, 41))
         for b in range(2, PACK):
             gate_block(b, diffs[b - 2], negs[b - 2])
-        first = weigh(nc.vector, new_state(h0, 0, 2, 0, QUARTER), 0, 0, QUARTER)
+        first = weigh(nc.vector, new_state(h0, 0, 0, 0, QUARTER), 0, 0, QUARTER)
         quantize(h0, QUARTER, HALF, h_bf0[:, 1024:2048])
         scatter_copy(first, 0, 0, QUARTER)
 
@@ -354,7 +352,7 @@ def tile_list_gated_node_update_kernel(
         def candidates(q):
             blocks = (PACK + 2 * q, PACK + 2 * q + 1)
             return [
-                leave_dealt(placed(f"cand{b}", H, F32, 107 + 2 * (b % PACK))[:], product(wc_q, b, "c", 4 + b % 2), ACT.Tanh, 1.0)
+                leave_dealt(placed(f"cand{b}", H, F32, 107 + 2 * (b % PACK))[:], product(wc_q, b, "c", 6 - 2 * q + b % 2), ACT.Tanh, 1.0)
                 for b in blocks
             ]
 
@@ -368,7 +366,7 @@ def tile_list_gated_node_update_kernel(
             for k in range(2):
                 b = PACK + 2 * q + k
                 neg = leave_dealt(
-                    ring.tile([P, H], F32, name=f"neg{b}", tag="neg")[:], product(wp_q, b, "p", k), ACT.Copy, -1.0
+                    ring.tile([P, H], F32, name=f"neg{b}", tag="neg")[:], product(wp_q, b, "p", 2 + k), ACT.Copy, -1.0
                 )
                 for t in range(PACK):
                     turn(place(t, k), cands[k], t, k == 0 and t % 2 == 0, False)
@@ -399,26 +397,26 @@ def tile_list_gated_node_update_kernel(
         def store(c):
             nc.sync.dma_start(out=out[c * P : (c + 1) * P, :], in_=windows[c][:])
 
+        weighed_piece(h0, 0, 1, QUARTER, HALF)
+        weighed_piece(h0, 1, 0, 0, HALF)
         cands = candidates(0)
-        weighed_piece(h0, 0, 3, QUARTER, HALF)
-        weighed_piece(h0, 1, 2, 0, HALF)
-        weighed_piece(h0, 2, 3, 0, HALF)
-        y_last = to_sbuf(new_state(h0, 3, 2, 0, HALF), y_tile(3, 0, HALF))
+        weighed_piece(h0, 2, 1, 0, HALF)
+        y_last = to_sbuf(new_state(h0, 3, 0, 0, HALF), y_tile(3, 0, HALF))
         scatter_copy(weigh(nc.gpsimd, y_last[:, 0:QUARTER], 3, 0, QUARTER), 3, 0, QUARTER)
-        gate_difference(0, difference(0, cands, 6))
+        gate_difference(0, difference(0, cands, 4))
         held = placed("weighted_last", QUARTER, F32, 36)
         scatter_copy(weigh(nc.gpsimd, y_last[:, QUARTER:HALF], 3, QUARTER, HALF, held), 3, QUARTER, HALF)
         for t in range(PACK):
-            gate(*fourth, t, (4, 5, 0, 1)[t], by_fours(gates1[1][:], t))
+            gate(*fourth, t, (6, 7, 2, 3)[t], by_fours(gates1[1][:], t))
         cands = candidates(1)
         banks = difference(1, cands, 6)
-        weighed_piece(h1, 0, 3, *third)
-        late = new_state(h1, 1, 2, *third)
+        weighed_piece(h1, 0, 1, *third)
+        late = new_state(h1, 1, 0, *third)
         scatter_copy(weigh(nc.vector, late, 1, *third, placed("weighted_third", QUARTER, F32, 36)), 1, *third)
         gate_difference(1, banks)
-        fused_piece(2, 3, *third, placed("y_held", QUARTER, F32, 40)[:])
+        fused_piece(2, 1, *third, placed("y_held", QUARTER, F32, 40)[:])
         for c in range(3):
-            fused_piece(c, (4, 5, 0)[c], *fourth)
+            fused_piece(c, (4, 5, 2)[c], *fourth)
             store(c)
-        fused_piece(3, 1, HALF, S)
+        fused_piece(3, 3, HALF, S)
         store(3)

@@ -144,7 +144,7 @@ def tile_list_gated_node_update_kernel(
 
         for s in range(2):
             gather_words(0, s, placed(f"v_words0{s}", HALF, U32, 86 + 2 * s))
-        wp_raw = [load_whole(wp, 0, "wp_raw0", 27), [load_half(wp, 1, u, "wp_raw1", 35 + 4 * u) for u in range(2)]]
+        wp_raw = [load_whole(wp, a, f"wp_raw{a}", 27 + 8 * a) for a in range(PASSES)]
         wg_codes = keep.tile([P, PASSES, 2 * H], U8, name="wg_codes", align_bytes=64)
         nc.vector.tensor_copy(
             out=wg_codes[:].bitcast(U16).rearrange("p a (t n i) -> p a n t i", t=PACK, i=8),

@@ -233,10 +233,10 @@ def tile_list_gated_node_update_kernel(
         gates0 = [placed(f"gate{t}", HALF, F32, 90 + 2 * t) for t in range(PACK)]
         for t in range(PACK):
             gate(0, HALF, t, t, fours(gates0[t][:]))
-        gates1 = [kept(f"gates1{q}", PACK * QUARTER, F32) for q in range(2)]
+        gates1 = kept("gates1", PACK * HALF, F32)
         third, fourth = (HALF, HALF + QUARTER), (HALF + QUARTER, S)
         for t in range(PACK):
-            gate(*third, t, t, by_fours(gates1[0][:], t))
+            gate(HALF, S, t, t, by_fours(gates1[:], t))
         wc_q = [quantize_weight(wc_raw[0], "wc0")]
         wo_raw = [load_half(wo, 0, u, "wo_raw", 132 + 4 * u) for u in range(2)]
         wc_q.append(quantize_weight(wc_raw[1], "wc1"))
@@ -254,7 +254,7 @@ def tile_list_gated_node_update_kernel(
                 )
             return scaled
 
-        scaled0 = [scale_gates(0, 72)]
+        scaled0 = [scale_gates(0, 144)]
         wr_planes = placed("wr_planes", WR_W, I32, 140)
         for q in range(P // QUADRANT):
             nc.sync.dma_start(
@@ -329,7 +329,7 @@ def tile_list_gated_node_update_kernel(
             )
 
         diffs = [open_difference(b) for b in range(2)]
-        present = [product(wp_q, b, "p", b, 2) for b in range(PACK)]
+        present = [product(wp_q, b, "p", b) for b in range(PACK)]
         for b in range(2):
             gate_block(b, diffs[b], negated(b, present[b], 2 - b))
         quantize(h0, 0, QUARTER, h_bf0[:, 0:1024])
@@ -352,7 +352,7 @@ def tile_list_gated_node_update_kernel(
         def candidates(q):
             blocks = (PACK + 2 * q, PACK + 2 * q + 1)
             return [
-                leave_dealt(placed(f"cand{b}", H, F32, 107 + 2 * (b % PACK))[:], product(wc_q, b, "c", 6 - 2 * q + b % 2), ACT.Tanh, 1.0)
+                leave_dealt(placed(f"cand{b}", H, F32, 107 + 2 * (b % PACK))[:], product(wc_q, b, "c", 6 + b % 2), ACT.Tanh, 1.0)
                 for b in blocks
             ]
 
@@ -385,7 +385,7 @@ def tile_list_gated_node_update_kernel(
             nc.gpsimd.tensor_tensor(
                 out=h_bf1[:].rearrange("p (n i t) -> p n i t", i=4, t=PACK),
                 in0=scaled[:].rearrange("p (n t i) -> p n i t", t=PACK, i=4),
-                in1=gates1[q][:].rearrange("p (n t i) -> p n i t", t=PACK, i=4),
+                in1=gates1[:, q * PACK * QUARTER : (q + 1) * PACK * QUARTER].rearrange("p (n t i) -> p n i t", t=PACK, i=4),
                 op=ALU.mult,
             )
             quantize(h1, q * QUARTER, (q + 1) * QUARTER, h_bf1[:])
@@ -401,22 +401,17 @@ def tile_list_gated_node_update_kernel(
         weighed_piece(h0, 1, 0, 0, HALF)
         cands = candidates(0)
         weighed_piece(h0, 2, 1, 0, HALF)
+        banks = difference(0, cands, 4)
         y_last = to_sbuf(new_state(h0, 3, 0, 0, HALF), y_tile(3, 0, HALF))
-        scatter_copy(weigh(nc.gpsimd, y_last[:, 0:QUARTER], 3, 0, QUARTER), 3, 0, QUARTER)
-        gate_difference(0, difference(0, cands, 4))
-        held = placed("weighted_last", QUARTER, F32, 36)
-        scatter_copy(weigh(nc.gpsimd, y_last[:, QUARTER:HALF], 3, QUARTER, HALF, held), 3, QUARTER, HALF)
-        for t in range(PACK):
-            gate(*fourth, t, (6, 7, 2, 3)[t], by_fours(gates1[1][:], t))
-        cands = candidates(1)
-        banks = difference(1, cands, 6)
+        gate_difference(0, banks)
+        scatter_copy(weigh(nc.gpsimd, y_last, 3, 0, HALF, placed("weighted_last", HALF, F32, 36)), 3, 0, HALF)
+        banks = difference(1, candidates(1), 6)
         weighed_piece(h1, 0, 1, *third)
-        late = new_state(h1, 1, 0, *third)
-        scatter_copy(weigh(nc.vector, late, 1, *third, placed("weighted_third", QUARTER, F32, 36)), 1, *third)
         gate_difference(1, banks)
-        fused_piece(2, 1, *third, placed("y_held", QUARTER, F32, 40)[:])
-        for c in range(3):
-            fused_piece(c, (4, 5, 2)[c], *fourth)
+        fused_piece(1, 0, *third, placed("y_held", QUARTER, F32, 40)[:])
+        for c in range(2):
+            fused_piece(c, 4 + c, *fourth)
             store(c)
-        fused_piece(3, 3, HALF, S)
-        store(3)
+        for c in range(2, CHUNKS):
+            fused_piece(c, c, HALF, S)
+            store(c)

@@ -28,11 +28,9 @@ BANK = 2048
 KB = 1024
 ROWS = PACK * H
 SCALE_ROWS = 16
-TOP = P - SCALE_ROWS
+TOP = P - PASSES * SCALE_ROWS
 TAB_W, WG_W, WR_W = S // 4, H // 4, N // 4
-WG_AT = PASSES * TAB_W
-PLANE_W = WG_AT + PASSES * WG_W
-QUADRANT = 32
+PLANE_W = TAB_W + WG_W + WR_W
 
 
 def tile_list_gated_node_update_kernel(
@@ -55,12 +53,12 @@ def tile_list_gated_node_update_kernel(
         def bank_tile(name, bank):
             return psum.tile([P, HALF], F32, name=name, offset=bank * BANK)
 
-        def side_by_side(scales):
-            return scales.bitcast(I32).rearrange("a q w -> q a w")
+        def scale_rows(scales):
+            return scales.bitcast(I32).rearrange("a q w -> (a q) w")
 
-        tab_rows = placed("tab_rows", T // 4, I32, 15.5)
-        nc.gpsimd.memset(tab_rows[0 : TOP - SCALE_ROWS, :], 0)
-        wg_rows = placed("wg_rows", PASSES * WG_W, I32, 60)
+        tab_rows = placed("tab_rows", T // 4, I32, 80)
+        nc.gpsimd.memset(tab_rows[0:TOP, :], 0)
+        wg_rows = placed("wg_rows", WG_W, I32, 84)
         nc.gpsimd.memset(wg_rows[0:TOP, :], 0)
         ident = kept("ident", P, F32)
         make_identity(nc, ident[:])
@@ -72,10 +70,11 @@ def tile_list_gated_node_update_kernel(
             return window
 
         windows = [zeroed_window(0, 99, nc.vector, (slice(0, T2 - 1), slice(T2 - 1, T2)))]
+        windows.extend(zeroed_window(c, 108 + 8 * c, nc.gpsimd) for c in (1, 2))
 
         idx = lists.tile([P, S // 16], U16, name="idx")
         nc.sync.dma_start(idx[:], offs)
-        nc.sync.dma_start(out=tab_rows[TOP - SCALE_ROWS : P, :], in_=tab_scales.bitcast(I32).rearrange("a q w -> (a q) w"))
+        nc.sync.dma_start(out=tab_rows[TOP:P, :], in_=scale_rows(tab_scales))
 
         def load_table(a, kib):
             words = placed(f"table{a}", T, I32, kib)
@@ -97,10 +96,13 @@ def tile_list_gated_node_update_kernel(
             )
             return raw[:].rearrange("p (j n i) -> p n j i", i=4, j=PACK)
 
-        nc.sync.dma_start(out=wg_rows[TOP:P, :].rearrange("q (a w) -> q a w", a=PASSES), in_=side_by_side(wg_scales))
-        table = [load_table(0, 27)]
-        wg_raw = arena.tile([P, PASSES, 2 * H // 4], I32, name="wg_raw", offset=58 * KB, align_bytes=64)
+        table = [load_table(0, 20)]
+        nc.sync.dma_start(out=wg_rows[TOP:P, :], in_=scale_rows(wg_scales))
+        staged = kept("staged", PLANE_W, I32)
+        nc.sync.dma_start(out=staged[TOP:P, TAB_W + WG_W :], in_=scale_rows(wr_scales))
+        wg_raw = arena.tile([P, PASSES, 2 * H // 4], I32, name="wg_raw", offset=56 * KB, align_bytes=64)
         nc.sync.dma_start(out=wg_raw[:], in_=wg_words.bitcast(I32).rearrange("a p w -> p a w"))
+        table.append(load_table(1, 0))
         idx2 = lists.tile([P, S // 16], U16, name="idx2")
         nc.sync.dma_start(idx2[:], offs2)
         gains = kept("gains", PACK, F32)
@@ -108,28 +110,25 @@ def tile_list_gated_node_update_kernel(
 
         gathered = placed("gathered", S, U8, 139.5)
         nc.vector.tensor_copy(out=gathered[:], in_=tab_rows[:].bitcast(U8).indirect(idx[:]))
-        staged = kept("staged", PLANE_W, I32)
-        nc.sync.dma_start(out=staged[TOP:P, 0:TAB_W], in_=gathered[TOP - SCALE_ROWS : TOP, :].bitcast(I32))
-        table.append(load_table(1, 0))
         nc.vector.tensor_copy(
-            out=staged[:, WG_AT:PLANE_W].bitcast(U8).rearrange("p (a t m) -> p a t m", a=PASSES, t=PACK),
-            in_=wg_rows[:].bitcast(U8).rearrange("p (a m t) -> p a t m", a=PASSES, t=PACK),
+            out=staged[:, TAB_W : TAB_W + WG_W].bitcast(U8).rearrange("p (t m) -> p t m", t=PACK),
+            in_=wg_rows[:].bitcast(U8).rearrange("p (m t) -> p t m", t=PACK),
         )
-        nc.vector.tensor_copy(
-            out=staged[TOP - SCALE_ROWS : P, TAB_W:WG_AT], in_=gathered[TOP - SCALE_ROWS : P, :].bitcast(I32)
-        )
-        windows.append(zeroed_window(1, 19, nc.vector))
-        windows.append(zeroed_window(2, 60, nc.vector))
-        planes = placed("planes", PLANE_W, I32, 16)
-        for r in range(4):
-            nc.sync.dma_start(out=planes[r:P:32, :], in_=staged[TOP + r : P : 4, :])
-        wc_raw = [load_whole(wc, a, f"wc_raw{a}", 132 + 8 * a) for a in range(PASSES)]
+        nc.vector.tensor_copy(out=staged[TOP:P, 0:TAB_W], in_=gathered[TOP:P, :].bitcast(I32))
+        planes, wc_raw = [], []
+        for a in range(PASSES):
+            planes.append(placed(f"planes{a}", PLANE_W, I32, 80 + 2 * a))
+            first = TOP + SCALE_ROWS * a
+            for r in range(4):
+                nc.sync.dma_start(out=planes[a][r:P:32, :], in_=staged[first + r : first + SCALE_ROWS : 4, :])
+            wc_raw.append(load_whole(wc, a, f"wc_raw{a}", 132 + 8 * a))
 
-        def plane_of(at, width, a):
-            return planes[:, at + a * width : at + (a + 1) * width].bitcast(U8)
+        def plane_of(a, lo, hi):
+            return planes[a][:, lo:hi].bitcast(U8)
 
-        v_plane = [plane_of(0, TAB_W, a) for a in range(PASSES)]
-        wg_plane = [plane_of(WG_AT, WG_W, a) for a in range(PASSES)]
+        v_plane = [plane_of(a, 0, TAB_W) for a in range(PASSES)]
+        wg_plane = [plane_of(a, TAB_W, TAB_W + WG_W) for a in range(PASSES)]
+        wr_plane = [plane_of(a, TAB_W + WG_W, PLANE_W) for a in range(PASSES)]
 
         v_words = {}
 
@@ -143,14 +142,14 @@ def tile_list_gated_node_update_kernel(
             return v_words[a, s][:, entries.start - s * HALF : entries.stop - s * HALF].bitcast(FP8X4)
 
         for s in range(2):
-            gather_words(0, s, placed(f"v_words0{s}", HALF, U32, 86 + 2 * s))
-        wp_raw = [load_whole(wp, a, f"wp_raw{a}", 27 + 8 * a) for a in range(PASSES)]
+            gather_words(0, s, placed(f"v_words0{s}", HALF, U32, 84 + 2 * s))
+        wp_raw = [load_whole(wp, a, f"wp_raw{a}", 20 + 8 * a) for a in range(PASSES)]
         wg_codes = keep.tile([P, PASSES, 2 * H], U8, name="wg_codes", align_bytes=64)
         nc.vector.tensor_copy(
             out=wg_codes[:].bitcast(U16).rearrange("p a (t n i) -> p a n t i", t=PACK, i=8),
             in_=wg_raw[:].bitcast(U16).rearrange("p a (n i t) -> p a n t i", t=PACK, i=8),
         )
-        windows.append(zeroed_window(3, 52, nc.gpsimd))
+        windows.append(zeroed_window(3, 56, nc.vector))
         for s in range(2):
             gather_words(1, s, kept(f"v_words1{s}", HALF, U32))
 
@@ -230,13 +229,13 @@ def tile_list_gated_node_update_kernel(
                 in1=in1.rearrange("p (n t i) -> p n t i", t=PACK, i=4), op=ALU.mult,
             )
 
-        gates0 = [placed(f"gate{t}", HALF, F32, 90 + 2 * t) for t in range(PACK)]
+        gates0 = [placed(f"gate{t}", HALF, F32, 88 + 2 * t) for t in range(PACK)]
         for t in range(PACK):
             gate(0, HALF, t, t, fours(gates0[t][:]))
-        gates1 = kept("gates1", PACK * HALF, F32)
+        gates1 = [kept(f"gates1{q}", PACK * QUARTER, F32) for q in range(2)]
         third, fourth = (HALF, HALF + QUARTER), (HALF + QUARTER, S)
         for t in range(PACK):
-            gate(HALF, S, t, t, by_fours(gates1[:], t))
+            gate(*third, t, t, by_fours(gates1[0][:], t))
         wc_q = [quantize_weight(wc_raw[0], "wc0")]
         wo_raw = [load_half(wo, 0, u, "wo_raw", 132 + 4 * u) for u in range(2)]
         wc_q.append(quantize_weight(wc_raw[1], "wc1"))
@@ -254,20 +253,14 @@ def tile_list_gated_node_update_kernel(
                 )
             return scaled
 
-        scaled0 = [scale_gates(0, 144)]
-        wr_planes = placed("wr_planes", WR_W, I32, 140)
-        for q in range(P // QUADRANT):
-            nc.sync.dma_start(
-                out=wr_planes[QUADRANT * q + 8 : QUADRANT * q + 16, :],
-                in_=wr_scales.bitcast(I32)[:, 4 * q : 4 * q + 4, :],
-            )
+        scaled0 = [scale_gates(0, 20)]
         wp_q = [quantize_weight(wp_raw[0], "wp0")]
-        wr_codes = placed("wr_codes", PASSES * N, I32, 27)
+        wr_codes = placed("wr_codes", PASSES * N, I32, 140)
         nc.sync.dma_start(
             out=wr_codes[:].rearrange("p (a e) -> p a e", a=PASSES),
             in_=wr_words.rearrange("a p e i -> p a (e i)").bitcast(I32),
         )
-        wgo_sb = placed("wgo_sb", S, F32, 31)
+        wgo_sb = placed("wgo_sb", S, F32, 144)
         nc.sync.dma_start(out=wgo_sb[:], in_=wgo)
         wp_q.append(quantize_weight(wp_raw[1], "wp1"))
         wo_q = quantize_weight(wo_raw, "wo")
@@ -277,7 +270,7 @@ def tile_list_gated_node_update_kernel(
             cols = slice(c * P, (c + 1) * P)
             for a in range(PASSES):
                 table_moving(
-                    acc, wr_codes[:, a * N + c * P : a * N + (c + 1) * P].bitcast(FP8X4), wr_planes[8 + 4 * a : P, :].bitcast(U8)[:, cols],
+                    acc, wr_codes[:, a * N + c * P : a * N + (c + 1) * P].bitcast(FP8X4), wr_plane[a][:, cols],
                     a, slice(lo, hi), a == 0, False,
                 )
             nc.tensor.matmul_mx(
@@ -292,7 +285,7 @@ def tile_list_gated_node_update_kernel(
             return y
 
         def y_tile(c, lo, hi):
-            return ring.tile([P, HALF], F32, name=f"y_sb{c}_{lo}", tag="y", bufs=4)[:, 0 : hi - lo]
+            return ring.tile([P, HALF], F32, name=f"y_sb{c}_{lo}", tag="y", bufs=5)[:, 0 : hi - lo]
 
         def weigh(engine, y, c, lo, hi, weighted=None):
             weighted = kept(f"weighted{c}_{lo}", hi - lo, F32) if weighted is None else weighted
@@ -339,6 +332,7 @@ def tile_list_gated_node_update_kernel(
         for b in range(2, PACK):
             gate_block(b, diffs[b - 2], negs[b - 2])
         first = weigh(nc.vector, new_state(h0, 0, 0, 0, QUARTER), 0, 0, QUARTER)
+        second = to_sbuf(new_state(h0, 1, 1, 0, QUARTER), y_tile(1, 0, QUARTER))
         quantize(h0, QUARTER, HALF, h_bf0[:, 1024:2048])
         scatter_copy(first, 0, 0, QUARTER)
 
@@ -352,7 +346,7 @@ def tile_list_gated_node_update_kernel(
         def candidates(q):
             blocks = (PACK + 2 * q, PACK + 2 * q + 1)
             return [
-                leave_dealt(placed(f"cand{b}", H, F32, 107 + 2 * (b % PACK))[:], product(wc_q, b, "c", 6 + b % 2), ACT.Tanh, 1.0)
+                leave_dealt(placed(f"cand{b}", H, F32, 107 + 2 * (b % PACK))[:], product(wc_q, b, "c", 4 + b % 2), ACT.Tanh, 1.0)
                 for b in blocks
             ]
 
@@ -385,7 +379,7 @@ def tile_list_gated_node_update_kernel(
             nc.gpsimd.tensor_tensor(
                 out=h_bf1[:].rearrange("p (n i t) -> p n i t", i=4, t=PACK),
                 in0=scaled[:].rearrange("p (n t i) -> p n i t", t=PACK, i=4),
-                in1=gates1[:, q * PACK * QUARTER : (q + 1) * PACK * QUARTER].rearrange("p (n t i) -> p n i t", t=PACK, i=4),
+                in1=gates1[q][:].rearrange("p (n t i) -> p n i t", t=PACK, i=4),
                 op=ALU.mult,
             )
             quantize(h1, q * QUARTER, (q + 1) * QUARTER, h_bf1[:])
@@ -397,18 +391,23 @@ def tile_list_gated_node_update_kernel(
         def store(c):
             nc.sync.dma_start(out=out[c * P : (c + 1) * P, :], in_=windows[c][:])
 
-        weighed_piece(h0, 0, 1, QUARTER, HALF)
-        weighed_piece(h0, 1, 0, 0, HALF)
+        scatter_copy(weigh(nc.gpsimd, second, 1, 0, QUARTER, placed("weighted_second", QUARTER, F32, 68)), 1, 0, QUARTER)
         cands = candidates(0)
-        weighed_piece(h0, 2, 1, 0, HALF)
-        banks = difference(0, cands, 4)
-        y_last = to_sbuf(new_state(h0, 3, 0, 0, HALF), y_tile(3, 0, HALF))
-        gate_difference(0, banks)
-        scatter_copy(weigh(nc.gpsimd, y_last, 3, 0, HALF, placed("weighted_last", HALF, F32, 36)), 3, 0, HALF)
+        for c in range(2):
+            weighed_piece(h0, c, c, QUARTER, HALF)
+        weighed_piece(h0, 2, 0, 0, HALF)
+        y_last = to_sbuf(new_state(h0, 3, 1, 0, HALF), y_tile(3, 0, HALF))
+        scatter_copy(weigh(nc.gpsimd, y_last[:, 0:QUARTER], 3, 0, QUARTER), 3, 0, QUARTER)
+        gate_difference(0, difference(0, cands, 6))
+        held = placed("weighted_last", QUARTER, F32, 36)
+        scatter_copy(weigh(nc.gpsimd, y_last[:, QUARTER:HALF], 3, QUARTER, HALF, held), 3, QUARTER, HALF)
+        for t in range(PACK):
+            gate(*fourth, t, (4, 5, 2, 3)[t], by_fours(gates1[1][:], t))
         banks = difference(1, candidates(1), 6)
-        weighed_piece(h1, 0, 1, *third)
+        late = new_state(h1, 0, 0, *third)
+        scatter_copy(weigh(nc.vector, late, 0, *third, placed("weighted_third", QUARTER, F32, 36)), 0, *third)
         gate_difference(1, banks)
-        fused_piece(1, 0, *third, placed("y_held", QUARTER, F32, 40)[:])
+        fused_piece(1, 1, *third, placed("y_held", QUARTER, F32, 40)[:])
         for c in range(2):
             fused_piece(c, 4 + c, *fourth)
             store(c)

@@ -232,10 +232,10 @@ def tile_list_gated_node_update_kernel(
         gates0 = [placed(f"gate{t}", HALF, F32, 88 + 2 * t) for t in range(PACK)]
         for t in range(PACK):
             gate(0, HALF, t, t, fours(gates0[t][:]))
-        gates1 = [kept(f"gates1{q}", PACK * QUARTER, F32) for q in range(2)]
+        gates1 = kept("gates1", PACK * HALF, F32)
         third, fourth = (HALF, HALF + QUARTER), (HALF + QUARTER, S)
         for t in range(PACK):
-            gate(*third, t, t, by_fours(gates1[0][:], t))
+            gate(HALF, S, t, t, by_fours(gates1[:], t))
         wc_q = [quantize_weight(wc_raw[0], "wc0")]
         wo_raw = [load_half(wo, 0, u, "wo_raw", 132 + 4 * u) for u in range(2)]
         wc_q.append(quantize_weight(wc_raw[1], "wc1"))
@@ -379,7 +379,7 @@ def tile_list_gated_node_update_kernel(
             nc.gpsimd.tensor_tensor(
                 out=h_bf1[:].rearrange("p (n i t) -> p n i t", i=4, t=PACK),
                 in0=scaled[:].rearrange("p (n t i) -> p n i t", t=PACK, i=4),
-                in1=gates1[q][:].rearrange("p (n t i) -> p n i t", t=PACK, i=4),
+                in1=gates1[:, q * PACK * QUARTER : (q + 1) * PACK * QUARTER].rearrange("p (n t i) -> p n i t", t=PACK, i=4),
                 op=ALU.mult,
             )
             quantize(h1, q * QUARTER, (q + 1) * QUARTER, h_bf1[:])
@@ -396,13 +396,11 @@ def tile_list_gated_node_update_kernel(
         for c in range(2):
             weighed_piece(h0, c, c, QUARTER, HALF)
         weighed_piece(h0, 2, 0, 0, HALF)
-        y_last = to_sbuf(new_state(h0, 3, 1, 0, HALF), y_tile(3, 0, HALF))
-        scatter_copy(weigh(nc.gpsimd, y_last[:, 0:QUARTER], 3, 0, QUARTER), 3, 0, QUARTER)
+        weighed_piece(h0, 3, 1, 0, QUARTER)
         gate_difference(0, difference(0, cands, 6))
+        y_last = to_sbuf(new_state(h0, 3, 0, QUARTER, HALF), y_tile(3, QUARTER, HALF))
         held = placed("weighted_last", QUARTER, F32, 36)
-        scatter_copy(weigh(nc.gpsimd, y_last[:, QUARTER:HALF], 3, QUARTER, HALF, held), 3, QUARTER, HALF)
-        for t in range(PACK):
-            gate(*fourth, t, (4, 5, 2, 3)[t], by_fours(gates1[1][:], t))
+        scatter_copy(weigh(nc.gpsimd, y_last, 3, QUARTER, HALF, held), 3, QUARTER, HALF)
         banks = difference(1, candidates(1), 6)
         late = new_state(h1, 0, 0, *third)
         scatter_copy(weigh(nc.vector, late, 0, *third, placed("weighted_third", QUARTER, F32, 36)), 0, *third)

from contextlib import ExitStack

import concourse.mybir as mybir
from concourse.masks import make_identity

K, T, S, H, N, T2 = 1024, 4096, 1024, 512, 512, 2048
FLOPS = 2 * S * (3 * K * H + K * N + H * N)

F32 = mybir.dt.float32
BF16 = mybir.dt.bfloat16
I32 = mybir.dt.int32
U32 = mybir.dt.uint32
U16 = mybir.dt.uint16
U8 = mybir.dt.uint8
FP8X4 = mybir.dt.float8_e4m3fn_x4
FP4X4 = mybir.dt.float4_e2m1fn_x4
ACT = mybir.ActivationFunctionType
ALU = mybir.AluOpType

P = 128
PACK = 4
K_PASS = P * PACK
PASSES = K // K_PASS
HALF = 512
QUARTER = 256
CHUNKS = N // P
BANK = 2048
KB = 1024
ROWS = PACK * H
SCALE_ROWS = 16
TOP = P - PASSES * SCALE_ROWS
TAB_W, WG_W, WR_W = S // 4, H // 4, N // 4
PLANE_W = TAB_W + WG_W + WR_W


def tile_list_gated_node_update_kernel(
    tc, tab_words, tab_scales, offs, offs2, wg_words, wg_scales, wr_words, wr_scales, wc, wp, gain, wo, wgo, out
):
    nc = tc.nc
    with ExitStack() as ctx:
        lists = ctx.enter_context(tc.tile_pool(name="lists", bufs=1))
        keep = ctx.enter_context(tc.tile_pool(name="keep", bufs=1))
        ring = ctx.enter_context(tc.tile_pool(name="ring", bufs=3))
        arena = ctx.enter_context(tc.tile_pool(name="arena", bufs=1))
        psum = ctx.enter_context(tc.psum_pool(name="psum", bufs=1))

        def kept(name, width, dtype):
            return keep.tile([P, width], dtype, name=name, align_bytes=64)

        def placed(name, width, dtype, kib):
            return arena.tile([P, width], dtype, name=name, offset=int(kib * KB), align_bytes=64)

        def bank_tile(name, bank):
            return psum.tile([P, HALF], F32, name=name, offset=bank * BANK)

        def scale_rows(scales):
            return scales.bitcast(I32).rearrange("a q w -> (a q) w")

        tab_rows = placed("tab_rows", T // 4, I32, 80)
        nc.gpsimd.memset(tab_rows[0:TOP, :], 0)
        wg_rows = placed("wg_rows", WG_W, I32, 84)
        nc.gpsimd.memset(wg_rows[0:TOP, :], 0)
        ident = kept("ident", P, F32)
        make_identity(nc, ident[:])

        def zeroed_window(c, kib, engine, parts=(slice(0, T2),)):
            window = placed(f"window{c}", T2, F32, kib)
            for cols in parts:
                engine.memset(window[:, cols].bitcast(I32), 0)
            return window

        windows = [zeroed_window(0, 99, nc.vector, (slice(0, T2 - 1), slice(T2 - 1, T2)))]
        windows.extend(zeroed_window(c, 108 + 8 * c, nc.gpsimd) for c in (1, 2))

        idx = lists.tile([P, S // 16], U16, name="idx")
        nc.sync.dma_start(idx[:], offs)
        nc.sync.dma_start(out=tab_rows[TOP:P, :], in_=scale_rows(tab_scales))

        def load_table(a, kib):
            words = placed(f"table{a}", T, I32, kib)
            nc.sync.dma_start(out=words[:], in_=tab_words[a].rearrange("p t i -> p (t i)").bitcast(I32))
            return words

        def load_whole(w, a, name, kib):
            raw = placed(name, ROWS, F32, kib)
            rows = w[a * K_PASS : (a + 1) * K_PASS, :].rearrange("(p j) c -> p (j c)", j=PACK)
            nc.sync.dma_start(out=raw[:], in_=rows)
            view = raw[:].rearrange("p (j n i) -> p n j i", i=4, j=PACK)
            return [view[:, u * 64 : (u + 1) * 64] for u in range(2)]

        def load_half(w, a, u, name, kib):
            rows = w[a * K_PASS : (a + 1) * K_PASS, :].rearrange("(p j) c -> p j c", j=PACK)
            raw = placed(f"{name}_{u}", ROWS // 2, F32, kib)
            nc.sync.dma_start(
                out=raw[:].rearrange("p (j c) -> p j c", j=PACK), in_=rows[:, :, u * QUARTER : (u + 1) * QUARTER]
            )
            return raw[:].rearrange("p (j n i) -> p n j i", i=4, j=PACK)

        table = [load_table(0, 20)]
        nc.sync.dma_start(out=wg_rows[TOP:P, :], in_=scale_rows(wg_scales))
        staged = kept("staged", PLANE_W, I32)
        nc.sync.dma_start(out=staged[TOP:P, TAB_W + WG_W :], in_=scale_rows(wr_scales))
        wg_raw = arena.tile([P, PASSES, 2 * H // 4], I32, name="wg_raw", offset=56 * KB, align_bytes=64)
        nc.sync.dma_start(out=wg_raw[:], in_=wg_words.bitcast(I32).rearrange("a p w -> p a w"))
        table.append(load_table(1, 0))
        idx2 = lists.tile([P, S // 16], U16, name="idx2")
        nc.sync.dma_start(idx2[:], offs2)
        gains = kept("gains", PACK, F32)
        nc.sync.dma_start(out=gains[:], in_=gain.rearrange("(p t) -> p t", t=PACK))

        gathered = placed("gathered", S, U8, 139.5)
        nc.vector.tensor_copy(out=gathered[:], in_=tab_rows[:].bitcast(U8).indirect(idx[:]))
        nc.vector.tensor_copy(
            out=staged[:, TAB_W : TAB_W + WG_W].bitcast(U8).rearrange("p (t m) -> p t m", t=PACK),
            in_=wg_rows[:].bitcast(U8).rearrange("p (m t) -> p t m", t=PACK),
        )
        nc.vector.tensor_copy(out=staged[TOP:P, 0:TAB_W], in_=gathered[TOP:P, :].bitcast(I32))
        planes, wc_raw = [], []
        for a in range(PASSES):
            planes.append(placed(f"planes{a}", PLANE_W, I32, 80 + 2 * a))
            first = TOP + SCALE_ROWS * a
            for r in range(4):
                nc.sync.dma_start(out=planes[a][r:P:32, :], in_=staged[first + r : first + SCALE_ROWS : 4, :])
            wc_raw.append(load_whole(wc, a, f"wc_raw{a}", 132 + 8 * a))

        def plane_of(a, lo, hi):
            return planes[a][:, lo:hi].bitcast(U8)

        v_plane = [plane_of(a, 0, TAB_W) for a in range(PASSES)]
        wg_plane = [plane_of(a, TAB_W, TAB_W + WG_W) for a in range(PASSES)]
        wr_plane = [plane_of(a, TAB_W + WG_W, PLANE_W) for a in range(PASSES)]

        v_words = {}

        def gather_words(a, s, words):
            offsets = idx[:, s * HALF // 16 : (s + 1) * HALF // 16]
            nc.vector.tensor_copy(out=words[:], in_=table[a][:].bitcast(U32).indirect(offsets))
            v_words[a, s] = words

        def picked(a, entries):
            s = entries.start // HALF
            return v_words[a, s][:, entries.start - s * HALF : entries.stop - s * HALF].bitcast(FP8X4)

        for s in range(2):
            gather_words(0, s, placed(f"v_words0{s}", HALF, U32, 84 + 2 * s))
        wp_raw = [load_whole(wp, a, f"wp_raw{a}", 20 + 8 * a) for a in range(PASSES)]
        wg_codes = keep.tile([P, PASSES, 2 * H], U8, name="wg_codes", align_bytes=64)
        nc.vector.tensor_copy(
            out=wg_codes[:].bitcast(U16).rearrange("p a (t n i) -> p a n t i", t=PACK, i=8),
            in_=wg_raw[:].bitcast(U16).rearrange("p a (n i t) -> p a n t i", t=PACK, i=8),
        )
        windows.append(zeroed_window(3, 56, nc.vector))
        for s in range(2):
            gather_words(1, s, kept(f"v_words1{s}", HALF, U32))

        def interleaved(grouped):
            return grouped.rearrange("p (n i j) -> p n j i", i=4, j=PACK)

        def mx_tiles(name, width):
            return kept(name + "_codes", width, U32), kept(name + "_plane", width, U8)

        def quantize(tiles, lo, hi, grouped):
            nc.vector.quantize_mx(out=tiles[0][:, lo:hi].bitcast(FP8X4), scales=tiles[1][:, lo:hi], in_=grouped)

        w_bf = placed("w_bf", ROWS, BF16, 8)

        def quantize_weight(raw, name):
            tiles = mx_tiles(name, H)
            for u in range(2):
                nc.vector.tensor_copy(out=interleaved(w_bf[:, u * 1024 : (u + 1) * 1024]), in_=raw[u])
            for u in range(2):
                quantize(tiles, u * QUARTER, (u + 1) * QUARTER, w_bf[:, u * 1024 : (u + 1) * 1024])
            return tiles

        def table_moving(acc, lhsT, lhsT_scale, a, entries, start, stop):
            nc.tensor.matmul_mx(
                out=acc, lhsT=lhsT, lhsT_scale=lhsT_scale, rhs=picked(a, entries), rhs_scale=v_plane[a][:, entries],
                start=start, stop=stop,
            )

        def table_stationary(acc, tiles, a, b, cols, start, stop):
            entries = slice(b * P, (b + 1) * P)
            nc.tensor.matmul_mx(
                out=acc[:, cols], lhsT=picked(a, entries), lhsT_scale=v_plane[a][:, entries],
                rhs=tiles[0][:, cols].bitcast(FP8X4), rhs_scale=tiles[1][:, cols], start=start, stop=stop,
            )

        def product(quantized, b, name, bank, pieces=1):
            acc = bank_tile(f"{name}{b}", bank)
            table_stationary(acc, quantized[0], 0, b, slice(0, H), True, False)
            for u in range(pieces):
                cols = slice(u * H // pieces, (u + 1) * H // pieces)
                table_stationary(acc, quantized[1], 1, b, cols, False, u == pieces - 1)
            return acc

        def by_fours(tile_ap, t):
            return tile_ap.rearrange("p (n t i) -> p n t i", t=PACK, i=4)[:, :, t, :]

        def fours(ap):
            return ap.rearrange("p (n i) -> p n i", i=4)

        def gate(lo, hi, t, bank, dst):
            acc = bank_tile(f"g{lo}_{t}", bank)[:, 0 : hi - lo]
            for a in range(PASSES):
                table_moving(
                    acc, wg_codes[:, a, t * 2 * P : (t + 1) * 2 * P].bitcast(FP4X4),
                    wg_plane[a][:, t * P : (t + 1) * P], a, slice(lo, hi), a == 0, a == PASSES - 1,
                )
            nc.scalar.activation(out=dst, in_=fours(acc), func=ACT.Sigmoid)

        def leave_dealt(dst, acc, func, scale, pieces=1):
            step = PACK // pieces
            for lo in range(0, PACK, step):
                nc.scalar.activation(
                    out=dst.rearrange("p (t m) -> p t m", t=PACK)[:, lo : lo + step],
                    in_=acc[:].rearrange("p (m t) -> p t m", t=PACK)[:, lo : lo + step],
                    func=func, scale=scale,
                )
            return dst

        def turn(dst, rows, t, start, stop):
            nc.tensor.matmul(
                out=dst, lhsT=rows[:, t * P : (t + 1) * P], rhs=ident[:], is_transpose=True, start=start, stop=stop
            )

        def gated(engine, h_bf, in0, in1):
            engine.tensor_tensor(
                out=h_bf.rearrange("p (n i t) -> p n t i", i=4, t=PACK), in0=in0,
                in1=in1.rearrange("p (n t i) -> p n t i", t=PACK, i=4), op=ALU.mult,
            )

        gates0 = [placed(f"gate{t}", HALF, F32, 88 + 2 * t) for t in range(PACK)]
        for t in range(PACK):
            gate(0, HALF, t, t, fours(gates0[t][:]))
        gates1 = kept("gates1", PACK * HALF, F32)
        third, fourth = (HALF, HALF + QUARTER), (HALF + QUARTER, S)
        for t in range(PACK):
            gate(HALF, S, t, t, by_fours(gates1[:], t))
        wc_q = [quantize_weight(wc_raw[0], "wc0")]
        wo_raw = [load_half(wo, 0, u, "wo_raw", 132 + 4 * u) for u in range(2)]
        wc_q.append(quantize_weight(wc_raw[1], "wc1"))
        cands = [
            leave_dealt(placed(f"cand{b}", H, F32, 107 + 2 * b)[:], product(wc_q, b, "c", b), ACT.Tanh, 1.0)
            for b in range(PACK)
        ]

        def scale_gates(q, kib):
            scaled = placed(f"scaled0{q}", PACK * QUARTER, F32, kib)
            for t in range(PACK):
                nc.scalar.activation(
                    out=by_fours(scaled[:], t), in_=fours(gates0[t][:, q * QUARTER : (q + 1) * QUARTER]),
                    func=ACT.Copy, scale=gains[:, t : t + 1],
                )
            return scaled

        scaled0 = [scale_gates(0, 20)]
        wp_q = [quantize_weight(wp_raw[0], "wp0")]
        wr_codes = placed("wr_codes", PASSES * N, I32, 140)
        nc.sync.dma_start(
            out=wr_codes[:].rearrange("p (a e) -> p a e", a=PASSES),
            in_=wr_words.rearrange("a p e i -> p a (e i)").bitcast(I32),
        )
        wgo_sb = placed("wgo_sb", S, F32, 144)
        nc.sync.dma_start(out=wgo_sb[:], in_=wgo)
        wp_q.append(quantize_weight(wp_raw[1], "wp1"))
        wo_q = quantize_weight(wo_raw, "wo")

        def new_state(h_q, c, bank, lo, hi):
            acc = bank_tile(f"y{c}_{lo}", bank)[:, 0 : hi - lo]
            cols = slice(c * P, (c + 1) * P)
            for a in range(PASSES):
                table_moving(
                    acc, wr_codes[:, a * N + c * P : a * N + (c + 1) * P].bitcast(FP8X4), wr_plane[a][:, cols],
                    a, slice(lo, hi), a == 0, False,
                )
            nc.tensor.matmul_mx(
                out=acc, lhsT=wo_q[0][:, cols].bitcast(FP8X4), lhsT_scale=wo_q[1][:, cols],
                rhs=h_q[0][:, lo % HALF : lo % HALF + hi - lo].bitcast(FP8X4),
                rhs_scale=h_q[1][:, lo % HALF : lo % HALF + hi - lo], start=False, stop=True,
            )
            return acc

        def to_sbuf(acc, y):
            nc.scalar.copy(out=y, in_=acc)
            return y

        def y_tile(c, lo, hi):
            return ring.tile([P, HALF], F32, name=f"y_sb{c}_{lo}", tag="y", bufs=5)[:, 0 : hi - lo]

        def weigh(engine, y, c, lo, hi, weighted=None):
            weighted = kept(f"weighted{c}_{lo}", hi - lo, F32) if weighted is None else weighted
            engine.tensor_tensor(out=weighted[:], in0=y, in1=wgo_sb[:, lo:hi], op=ALU.mult)
            return weighted[:]

        def scatter_copy(weighted, c, lo, hi):
            nc.vector.tensor_copy(out=windows[c][:].indirect(idx2[:, lo // 16 : hi // 16]), in_=weighted)

        def scatter_weigh(y, c, lo, hi):
            nc.vector.tensor_tensor(
                out=windows[c][:].indirect(idx2[:, lo // 16 : hi // 16]), in0=y, in1=wgo_sb[:, lo:hi], op=ALU.mult
            )

        h_bf0 = placed("h_bf0", PACK * HALF, BF16, 68)
        h0 = mx_tiles("h0", HALF)

        def open_difference(b):
            diff = bank_tile(f"diff{b}", PACK + b)
            for t in range(PACK):
                turn(diff[:, t * P : (t + 1) * P], cands[b], t, t == 0, False)
            return diff

        def negated(b, present, pieces=1):
            return leave_dealt(placed(f"neg{b}", H, F32, 44 + 2 * b)[:], present, ACT.Copy, -1.0, pieces)

        def gate_block(b, diff, neg):
            for t in range(PACK):
                turn(diff[:, t * P : (t + 1) * P], neg, t, False, t == PACK - 1)
            gated(
                nc.vector, h_bf0[:, b * HALF : (b + 1) * HALF],
                diff[:].rearrange("p (t n i) -> p n t i", t=PACK, i=4),
                scaled0[b // 2][:, b % 2 * HALF : (b % 2 + 1) * HALF],
            )

        diffs = [open_difference(b) for b in range(2)]
        present = [product(wp_q, b, "p", b) for b in range(PACK)]
        for b in range(2):
            gate_block(b, diffs[b], negated(b, present[b], 2 - b))
        quantize(h0, 0, QUARTER, h_bf0[:, 0:1024])
        diffs = [open_difference(b) for b in range(2, PACK)]
        negs = [negated(b, present[b]) for b in range(2, PACK)]
        scaled0.append(scale_gates(1, 41))
        for b in range(2, PACK):
            gate_block(b, diffs[b - 2], negs[b - 2])
        first = weigh(nc.vector, new_state(h0, 0, 0, 0, QUARTER), 0, 0, QUARTER)
        second = to_sbuf(new_state(h0, 1, 1, 0, QUARTER), y_tile(1, 0, QUARTER))
        quantize(h0, QUARTER, HALF, h_bf0[:, 1024:2048])
        scatter_copy(first, 0, 0, QUARTER)

        def weighed_piece(h_q, c, bank, lo, hi):
            y = to_sbuf(new_state(h_q, c, bank, lo, hi), y_tile(c, lo, hi))
            scatter_copy(weigh(nc.gpsimd, y, c, lo, hi), c, lo, hi)

        h_bf1 = kept("h_bf1", PACK * QUARTER, BF16)
        h1 = mx_tiles("h1", HALF)

        def candidates(q):
            blocks = (PACK + 2 * q, PACK + 2 * q + 1)
            return [
                leave_dealt(placed(f"cand{b}", H, F32, 107 + 2 * (b % PACK))[:], product(wc_q, b, "c", 4 + b % 2), ACT.Tanh, 1.0)
                for b in blocks
            ]

        def difference(q, cands, first_bank):
            banks = [bank_tile(f"diff1{q}_{u}", first_bank + u) for u in range(2)]

            def place(t, k):
                lo = (t % 2) * QUARTER + k * P
                return banks[t // 2][:, lo : lo + P]

            for k in range(2):
                b = PACK + 2 * q + k
                neg = leave_dealt(
                    ring.tile([P, H], F32, name=f"neg{b}", tag="neg")[:], product(wp_q, b, "p", 2 + k), ACT.Copy, -1.0
                )
                for t in range(PACK):
                    turn(place(t, k), cands[k], t, k == 0 and t % 2 == 0, False)
                for t in range(PACK):
                    turn(place(t, k), neg, t, False, k == 1 and t % 2 == 1)
            return banks

        def gate_difference(q, banks):
            scaled = placed(f"scaled1{q}", PACK * QUARTER, F32, 36 + 4 * q)
            for t in range(PACK):
                nc.scalar.activation(
                    out=by_fours(scaled[:], t),
                    in_=fours(banks[t // 2][:, (t % 2) * QUARTER : (t % 2 + 1) * QUARTER]),
                    func=ACT.Copy, scale=gains[:, t : t + 1],
                )
            nc.gpsimd.tensor_tensor(
                out=h_bf1[:].rearrange("p (n i t) -> p n i t", i=4, t=PACK),
                in0=scaled[:].rearrange("p (n t i) -> p n i t", t=PACK, i=4),
                in1=gates1[:, q * PACK * QUARTER : (q + 1) * PACK * QUARTER].rearrange("p (n t i) -> p n i t", t=PACK, i=4),
                op=ALU.mult,
            )
            quantize(h1, q * QUARTER, (q + 1) * QUARTER, h_bf1[:])

        def fused_piece(c, bank, lo, hi, y=None):
            y = y_tile(c, lo, hi) if y is None else y
            scatter_weigh(to_sbuf(new_state(h1, c, bank, lo, hi), y), c, lo, hi)

        def store(c):
            nc.sync.dma_start(out=out[c * P : (c + 1) * P, :], in_=windows[c][:])

        scatter_copy(weigh(nc.gpsimd, second, 1, 0, QUARTER, placed("weighted_second", QUARTER, F32, 68)), 1, 0, QUARTER)
        cands = candidates(0)
        for c in range(2):
            weighed_piece(h0, c, c, QUARTER, HALF)
        weighed_piece(h0, 2, 0, 0, HALF)
        weighed_piece(h0, 3, 1, 0, QUARTER)
        gate_difference(0, difference(0, cands, 6))
        y_last = to_sbuf(new_state(h0, 3, 0, QUARTER, HALF), y_tile(3, QUARTER, HALF))
        held = placed("weighted_last", QUARTER, F32, 36)
        scatter_copy(weigh(nc.gpsimd, y_last, 3, QUARTER, HALF, held), 3, QUARTER, HALF)
        banks = difference(1, candidates(1), 6)
        late = new_state(h1, 0, 0, *third)
        scatter_copy(weigh(nc.vector, late, 0, *third, placed("weighted_third", QUARTER, F32, 36)), 0, *third)
        gate_difference(1, banks)
        fused_piece(1, 1, *third, placed("y_held", QUARTER, F32, 40)[:])
        for c in range(2):
            fused_piece(c, 4 + c, *fourth)
            store(c)
        for c in range(2, CHUNKS):
            fused_piece(c, c, HALF, S)
            store(c)
